import numpy as np, ml_dtypes
CORES = [3,11,19,27,35,43,51,59]
N = 8
BF = ml_dtypes.bfloat16
W, C, B, VI, S = 4096, 4096, 192, 4, 3
def parts(rng):
    rt = rng.integers(0, 16, (N, 8, 16, W)); pf = rng.integers(0, W, (N, 8, 16, C))
    jc = np.argsort(rng.random((N, 8, C)), axis=-1)[..., :16 * B].reshape(N, 8, 16, B)
    return rt, pf, jc, rng.integers(0, 16, (N, 8, 16, B)), rng.integers(0, 16, (N, 8, B))
def pack(rt, pf, jc, fx, sr):
    return {"rt": np.ascontiguousarray(rt.reshape(N, 128, W)).astype(np.float32).astype(BF),
            "pk": np.ascontiguousarray((pf[..., :C // 2] + 4096 * pf[..., C // 2:]).reshape(N, 128, C // 2)).astype(np.int32),
            "jc": np.ascontiguousarray(jc.reshape(N, 128, B)).astype(np.int32),
            "fx": np.ascontiguousarray(fx.reshape(N, 128, B)).astype(np.float32).astype(BF), "sr": np.ascontiguousarray(sr).astype(np.int32)}
def setup_inputs(rng):
    return pack(*parts(rng))
def setup_inputs_ties(rng):
    rt, pf, jc, fx, sr = parts(rng)
    pool = rng.integers(0, 16, (N, 8, 16, 8)); pool[:, 1::2] = rng.integers(0, 2, (N, 4, 16, 8))
    rt = np.take_along_axis(pool, rng.integers(0, 8, (N, 8, 1, W)), 3)
    fx = np.where(rng.random((N, 8, 1, B)) < 0.5, np.take_along_axis(pool, rng.integers(0, 8, (N, 8, 1, B)), 3), fx)
    q = rng.permutation(C)[:C // 8]; pf[..., q] = pf[:, :, :1, q]
    return pack(rt, pf, jc, fx, sr)
def setup_inputs_rounds(rng):
    rt, pf, jc, fx, sr = parts(rng); h = W // 2
    o = np.argsort(rng.random((N, 8, W)), axis=-1); light = np.zeros((N, 8, W), bool); np.put_along_axis(light, o[..., :h], True, 2)
    rt = np.where(light[:, :, None, :], rng.integers(0, 2, (N, 8, 16, W)), rng.integers(8, 16, (N, 8, 16, W)))
    ln = rng.integers(1, S + 2, (8, B)); back = (rng.random((8, B)) * ln).astype(np.int64)
    ln[0] = S; back[0] = 0; ln[1] = S + 1; ln[2] = 1; back[2] = 0
    if np.count_nonzero(ln <= S) % 2 == 0:
        ln[3, 0] = S + 1 if ln[3, 0] <= S else S; back[3, 0] = 0
    s0 = rng.integers(0, 16, (8, B)); a = (np.arange(16)[None, :, None] - s0[:, None, :]) % 16
    nxt = (np.where(a == ln[:, None, :] - 1, back[:, None, :], a + 1) + s0[:, None, :]) % 16
    pc = np.argsort(rng.random((8, C)), axis=-1)[:, :16 * B]
    kap = rng.integers(0, 16, (8, C)); np.put_along_axis(kap, pc, nxt.reshape(8, 16 * B), 1)
    one = kap[None, :, None, :] == np.arange(16)[None, None, :, None]
    pf = np.take_along_axis(o[:, :, None, :], rng.integers(0, h, (N, 8, 16, C)) + np.where(one, 0, h), 3)
    e = np.argsort(rng.random((N, 8, B)), axis=-1)
    jc = np.take_along_axis(np.broadcast_to(pc.reshape(1, 8, 16, B), (N, 8, 16, B)), np.broadcast_to(e[:, :, None, :], (N, 8, 16, B)), 3)
    sr = np.take_along_axis(np.broadcast_to(s0[None], (N, 8, B)), e, 2)
    return pack(rt, pf, jc, rng.integers(0, 2, (N, 8, 16, B)), sr)
def setup_inputs_full(rng):
    h = W // 2; u = h // 2; rows = np.arange(16)
    side = (np.arange(N)[:, None] + np.arange(8)[None, :]) % 2 * h
    o = np.argsort(rng.random((N, 8, h)), axis=-1) + side[:, :, None]; light = np.zeros((N, 8, W), bool); np.put_along_axis(light, o[..., :u], True, 2)
    rt = np.where(light[:, :, None, :], rng.integers(0, 2, (N, 8, 16, W)), rng.integers(8, 16, (N, 8, 16, W)))
    s0 = 2 * rng.permutation(8) + rng.integers(0, 2, 8); a = (rows[None, :] - s0[:, None]) % 16
    nxt = (np.where(a == S - 1, 0, a + 1) + s0[:, None]) % 16
    lower = np.argsort(rng.random((8, C // 2)), axis=-1)[:, :8 * B]; upper = np.argsort(rng.random((8, C // 2)), axis=-1)[:, :8 * B] + C // 2
    pc = np.concatenate([lower, upper], axis=1).reshape(8, 16, B)
    kap = rng.integers(0, 16, (N, 8, C))
    np.put_along_axis(kap, np.broadcast_to(pc.reshape(1, 8, 16 * B), (N, 8, 16 * B)), np.broadcast_to(np.repeat(nxt, B, axis=1)[None], (N, 8, 16 * B)), 2)
    whole = int(rng.integers(0, 8))
    for g in range(8):
        if g != whole: kap[1::2, g, int(pc[g, (s0[g] + S - 1) % 16, 0])] = (s0[g] + S) % 16
    one = kap[:, :, None, :] == rows[None, None, :, None]
    pf = np.take_along_axis(o[:, :, None, :], rng.integers(0, u, (N, 8, 16, C)) + np.where(one, 0, u), 3)
    e = np.argsort(rng.random((N, 8, 16, B)), axis=-1)
    jc = np.take_along_axis(np.broadcast_to(pc[None], (N, 8, 16, B)), e, 3)
    return pack(rt, pf, jc, rng.integers(0, 2, (N, 8, 16, B)), np.broadcast_to(s0[None, :, None], (N, 8, B)))
def setup_inputs_ends(rng):
    rt, pf, jc, fx, sr = parts(rng)
    pf[:, ::2] = rng.choice(np.array([0, 1, W // 2, W - 1]), (N, 4, 16, C)); pf[:, 1::2, :, C // 2 - 1] = W - 1; pf[:, 1::2, :, C - 1] = W - 1
    jc[:, ::2] = np.concatenate([np.arange(8 * B), np.arange(C - 8 * B, C)]).reshape(16, B)
    rt[:, 1::2] = 15 * rng.integers(0, 2, (N, 4, 16, W)); fx = 15 * rng.integers(0, 2, (N, 8, 16, B)); sr = 15 * rng.integers(0, 2, (N, 8, B))
    o = rng.permutation(W); n = B // 2; hi = o[:W // 4]; mid = o[W // 4:W // 2]; lo = o[W // 2:3 * W // 4]
    rt[:, 1][:, :, hi] = 15; rt[:, 1][:, :, mid] = 14; rt[:, 1][:, :, lo] = 0
    for q in range(N):
        x = rng.permutation(B)[:n]; p = np.argsort(rng.random((16, n)), axis=0)[:3]; c = jc[q, 1, p, x]
        for i, k, a, b in ((0, p[1], mid, hi), (1, p[2], hi, lo), (2, p[1], lo, hi)):
            pf[q, 1][:, c[i]] = rng.choice(b, (16, n)); pf[q, 1][k, c[i]] = rng.choice(a, n)
        fx[q, 1][:, x] = 0; sr[q, 1][x] = p[0]
    return pack(rt, pf, jc, fx, sr)
def setup_inputs_spread(rng):
    rt, pf, jc, fx, sr = parts(rng)
    rt = np.minimum((16 * rng.random((N, 8, 16, W)) ** np.exp2(rng.integers(-2, 4, (N, 8, 1, W)))).astype(np.int64), 15)
    pf = np.minimum((W * rng.random((N, 8, 16, C)) ** np.exp2(rng.integers(-2, 4, (N, 8, 1, C)))).astype(np.int64), W - 1)
    fx = np.minimum((16 * rng.random((N, 8, 16, B)) ** np.exp2(rng.integers(-2, 4, (N, 8, 1, B)))).astype(np.int64), 15)
    sr = np.minimum((16 * rng.random((N, 8, B)) ** np.exp2(rng.integers(-1, 3, (N, 8, 1)))).astype(np.int64), 15)
    return pack(rt, pf, jc, fx, sr)
def check_inputs(d):
    bad = []
    for k in ("rt", "fx"):
        a = np.asarray(d[k]).astype(np.float32)
        if not np.all((a >= 0) & (a <= 15) & (a == np.floor(a))): bad.append("whole numbers of " + k)
    a = np.asarray(d["pk"]).astype(np.int64)
    if np.min(a) < 0 or np.max(a & 4095) >= W or np.max(a >> 12) >= W: bad.append("range of pk")
    for k, hi in (("jc", C - 1), ("sr", 15)):
        if np.min(d[k]) < 0 or np.max(d[k]) > hi: bad.append("range of " + k)
    s = np.sort(np.asarray(d["jc"]).reshape(N, 8, 16 * B), axis=-1)
    if np.any(s[..., 1:] == s[..., :-1]): bad.append("courts of a group differ")
    return bad
def reference(rt, pk, jc, fx, sr):
    R = rt.astype(np.float32).astype(np.int32).reshape(N, 8, 16, W); f = fx.astype(np.float32).astype(np.int32).reshape(N, 8, 16, B)
    two = pk.astype(np.int32).reshape(N, 8, 16, C // 2); pf = np.concatenate([two & 4095, two >> 12], axis=3)
    J = jc.astype(np.int32).reshape(N, 8, 16, B); start = sr.astype(np.int32); Z = np.zeros(N, np.int32); rows = np.arange(16, dtype=np.int32)
    for t in range(VI):
        if t > 0:
            f = np.roll(f, 1, axis=0); J = np.roll(J, 1, axis=0); start = np.roll(start, 1, axis=0)
        m = np.zeros((N, 8, 16, B), np.int32); v = np.zeros((N, 8, 16, B), np.int32); num = np.zeros((N, 8, 16, B), np.int32)
        p = start; go = np.ones((N, 8, B), bool); first = np.zeros((N, 8, B), np.int32); new = np.zeros((N, 8, B), np.int32)
        for s in range(1, S + 1):
            c = np.take_along_axis(J, p[:, :, None, :], 2)
            n = np.take_along_axis(pf, np.broadcast_to(c, (N, 8, 16, B)), 3)
            x = np.take_along_axis(R, np.broadcast_to(n.reshape(N, 8, 1, 16 * B), (N, 8, 16, 16 * B)), 3).reshape(N, 8, 16, 16, B)
            dist = np.add.reduce(np.abs(x - f[:, :, :, None, :]), axis=2)
            k = np.argmin(dist, axis=2).astype(np.int32)
            kk = k[:, :, None, :]; nk = np.take_along_axis(n, kk, 2)
            rule = np.take_along_axis(R, np.broadcast_to(nk, (N, 8, 16, B)), 3)
            here = (rows[None, None, :, None] == p[:, :, None, :]) & go[:, :, None, :]
            v = np.where(here, kk, v); num = np.where(here, nk, num); m = np.where(here, np.int32(s), m)
            f = np.where(go[:, :, None, :], np.abs(f - rule), f)
            mk = np.take_along_axis(m, kk, 2)[:, :, 0]; nr = np.take_along_axis(num, kk, 2)
            shut = go & (mk > 0)
            tot = np.add.reduce(np.take_along_axis(R, np.broadcast_to(nr, (N, 8, 16, B)), 3), axis=2)
            odd = ((tot + Z[:, None, None]) & 1) == 1
            new = np.where(shut, np.where(odd, nk[:, :, 0], nr[:, :, 0]), new); first = np.where(shut, mk, first)
            go = go & ~shut; p = np.where(go, k, p)
        closed = first > 0
        loop = closed[:, :, None, :] & (m >= first[:, :, None, :])
        at = np.broadcast_to(J.reshape(N, 8, 1, 16 * B), (N, 8, 16, 16 * B))
        old = np.take_along_axis(pf, at, 3).reshape(N, 8, 16, 16, B)
        hit = loop[:, :, None] & (v[:, :, None] == rows[None, None, :, None, None])
        np.put_along_axis(pf, at, np.where(hit, new[:, :, None, None, :], old).reshape(N, 8, 16, 16 * B), 3)
        Z = Z + np.add.reduce(closed.astype(np.int32), axis=(1, 2))
    return {"yp": (pf[..., :C // 2] + 4096 * pf[..., C // 2:]).reshape(N, 128, C // 2).astype(np.float32), "yf": f.reshape(N, 128, B).astype(np.float32).astype(BF)}

@@ -1,0 +1,492 @@
+from concourse.mybir import dt, AluOpType, AxisListType, ActivationFunctionType
+
+N = 8
+VI = 4
+NV = 8
+KS = 3
+F32, BF, I32T, U16 = "float32", "bfloat16", "int32", "uint16"
+SIZES = {
+    F32: "pkg0 204 pkg1 204 pkg2 204 pkg3 204 ones32 128 I32 128 BD32 128 W32 2048 pm 16 cols 8 M1 192 Me 192 Mo 192 KU 224 TA 192 "
+         "TB 208 TC 208 t1 192 t2 192 t3 192 OH 192 Q0 192 Qs 192 rst 192 run 192 fw 1400 P24 24 P 80 Bv 576 yps 2048",
+    BF: "rtb 4096 fin0 192 fin1 192 fin2 192 fin3 192 fo0 192 fo1 192 fo2 192 fo3 192 fa 192 fb 192 onesb 128 Ib 128 nI 128 zt 512 "
+        "BDb 128 W65 2048 Vi 2048 DIAG 192 FX %d dall 9216 GC %d o3b 12 kb 12 kA 12 R 192 EQ 576" % (256 * NV, 256 * (12 - NV)),
+    I32T: "pks 2048 pf 4480 jcs 192 pidx 4 CPi 192 i16 192 J256 12 D24 24 x12 12 r96 96 iw 640 kk2 12 kk3 12 K 80 sk 36 newv 384",
+    U16: "exo 12 rk 6 rp 6 N16 192 c16_0 12 c16_1 12 c16n 12 L16 12 cl16 36",
+}
+SCRATCH = {
+    "sr8": ("sbuf", [8, 192], I32T), "srb": ("sbuf", [8, 192], BF), "Sel": ("sbuf", [8, 128], BF), "D3": ("sbuf", [128, NV, 256], BF),
+    "key": ("psum", [128, 512], F32), "psC": ("psum", [128, 4, 256], F32), "U": ("psum", [128, 1024], F32),
+    "Wp": ("psum", [128, 512], F32), "mis": ("psum", [128, 512], F32),
+}
+for _ty in SIZES:
+    _l = SIZES[_ty].split()
+    for _i in range(0, len(_l), 2):
+        SCRATCH[_l[_i]] = ("sbuf", [128, int(_l[_i + 1])], _ty)
+SEMAPHORES = "cv cs ct cg ls pk1 pk2 pk3 fa1 fa2 fa3 dj ds df dp0 dp1 dr dyf dy0 dy1 dy2 dy3".split()
+
+
+def rank_program(g, core, T, topo):
+    rank = T.rank_of(core)
+    if rank is None:
+        return
+    A, AF, X = AluOpType, ActivationFunctionType, AxisListType.X
+    add, sub, mul, eq = A.add, A.subtract, A.mult, A.is_equal
+    queues = {"v": g.vector, "s": g.scalar, "t": g.tensor, "g": g, "y": g.sync}
+    csem = {"v": "cv", "s": "cs", "t": "ct", "g": "cg"}
+    know = {q: {} for q in queues}
+    total, clock, hist = {}, {}, {}
+
+    def ap(name, a=None, b=None, P=None, third=None):
+        shape = SCRATCH[name][1]
+        p = slice(0, shape[0]) if P is None else slice(0, P)
+        if len(shape) == 2:
+            lo, hi, st = (0, shape[1], 1) if a is None else (a if isinstance(a, tuple) else (a, b, 1))
+            return (T[name][p, slice(lo, hi) if st == 1 else slice(lo, hi, st)], [(name, lo, hi, st)])
+        w = shape[2]
+        k0, k1 = third if third else (0, w)
+        if b is None:
+            return (T[name][p, a, k0:k1], [(name, a * w + k0, a * w + k1, 1)])
+        return (T[name][p, a:b, k0:k1], [(name, a * w + k0, (b - 1) * w + k1, 1)])
+
+    def ind(win, off):
+        return (win[0].indirect(off[0]), win[1] + off[1])
+
+    def order(q, rw):
+        want = {}
+        for (name, lo, hi, st), isw in rw:
+            ps = SCRATCH[name][0] == "psum"
+            for (l2, h2, s2, w2, q2, sem, val) in hist.get(name, []):
+                same = q2 == q
+                if ps and not same:
+                    if not (lo // 512 <= (h2 - 1) // 512 and l2 // 512 <= (hi - 1) // 512):
+                        continue
+                else:
+                    if lo >= h2 or l2 >= hi or (st > 1 and st == s2 and (lo - l2) % st):
+                        continue
+                    if not (isw or w2) or (same and q == "t"):
+                        continue
+                if want.get(sem, 0) < val:
+                    want[sem] = val
+        k = know[q]
+        for sem in sorted(want, key=lambda s: -len(clock[(s, want[s])])):
+            if k.get(sem, 0) < want[sem]:
+                queues[q].wait_ge(T.sem[sem], want[sem])
+                for s2, v2 in clock[(sem, want[sem])].items():
+                    if k.get(s2, 0) < v2:
+                        k[s2] = v2
+
+    def note(owner, sem, val, rw, c):
+        total[sem] = val
+        c[sem] = val
+        clock[(sem, val)] = c
+        for (name, lo, hi, st), isw in rw:
+            keep = []
+            for e in hist.get(name, []):
+                inside = lo <= e[0] and e[1] <= hi and (st == 1 or (st == e[2] and (lo - e[0]) % st == 0))
+                if not (inside and (isw or (not e[3] and e[4] == owner))):
+                    keep.append(e)
+            keep.append((lo, hi, st, isw, owner, sem, val))
+            hist[name] = keep
+
+    def both(reads, writes):
+        return [(x, False) for r in reads for x in r[1]] + [(x, True) for r in writes for x in r[1]]
+
+    def emit(q, reads, writes, call):
+        rw = both(reads, writes)
+        order(q, rw)
+        sem = csem[q]
+        call().then_inc(T.sem[sem], 1)
+        note(q, sem, total.get(sem, 0) + 1, rw, dict(know[q]))
+
+    def dma(q, sem, out, in_, reads, writes):
+        rw = both(reads, writes)
+        order(q, rw)
+        queues[q].dma_start(out, in_).then_inc(T.sem[sem], 16)
+        note("d" + sem, sem, 16, rw, dict(know[q]))
+
+    def load(q, sem, buf, x):
+        dma(q, sem, buf[0], x, [], [buf])
+
+    def send(dst, dst_ap, src, rsem):
+        order("g", both([src], []))
+        rid, pid, _ = topo.addr(dst)
+        g.remote_dma(dst_ap, src[0], T.sem[rsem], T.sem["ls"], pid, rid, topo.mask(core, dst))
+        total["ls"] = total.get("ls", 0) + len(topo.engines(core, dst))
+
+    def landing(name, sem, src):
+        note("r" + sem, sem, len(topo.engines(src, core)), both([], [ap(name)]), {})
+
+    def tt(out, a, b, op):
+        emit("v", [a, b], [out], lambda: g.vector.tensor_tensor(out[0], a[0], b[0], op))
+
+    def ts(out, a, s1, op0, s2=None, op1=None):
+        rd = [a] + [s for s in (s1, s2) if isinstance(s, tuple)]
+        x1, x2 = [s[0] if isinstance(s, tuple) else s for s in (s1, s2)]
+        more = [] if op1 is None else [op1]
+        emit("v", rd, [out], lambda: g.vector.tensor_scalar(out[0], a[0], x1, x2, op0, *more))
+
+    def cp(out, a):
+        emit("v", [a], [out], lambda: g.vector.tensor_copy(out[0], a[0]))
+
+    def fill(out, c):
+        emit("v", [], [out], lambda: g.vector.memset(out[0], c))
+
+    def act(out, a, func, scale=1.0):
+        sc = scale[0] if isinstance(scale, tuple) else scale
+        emit("s", [a] + ([scale] if isinstance(scale, tuple) else []), [out], lambda: g.scalar.activation(out[0], a[0], func, scale=sc))
+
+    def mm(out, l, r, start, stop):
+        emit("t", [l, r], [out], lambda: g.tensor.matmul(out[0], l[0], r[0], start, stop))
+
+    def iota(out, pattern, base, cm):
+        emit("g", [], [out], lambda: g.iota(out[0], pattern, base, cm))
+
+    def asel(out, a, pattern, op, base, cm):
+        emit("g", [a], [out], lambda: g.affine_select(out[0], a[0], pattern, op, 0.0, base, cm))
+
+    cols = {"fw": {}, "iw": {}}
+
+    def work(buf, name, n, a, b):
+        c = cols[buf]
+        if name not in c:
+            c[name] = (sum(w for _, w in c.values()), n)
+        o, w = c[name]
+        return ap(buf, o + a, o + (w if b is None else b))
+
+    def fw(name, n=12, a=0, b=None):
+        return work("fw", name, n, a, b)
+
+    def iw(name, n=12, a=0, b=None):
+        return work("iw", name, n, a, b)
+
+    def blk(name, i):
+        return ap(name, 128 * i, 128 * i + 128)
+
+    load("y", "dj", ap("jcs"), T.jc[:])
+    load("s", "ds", ap("sr8"), T.sr[:])
+    load("s", "df", ap("fin0"), T.fx[:])
+    load("y", "dp0", ap("pks", 0, 1024), T.pk[:, 0:1024])
+    load("y", "dp1", ap("pks", 1024, 2048), T.pk[:, 1024:2048])
+    load("y", "dr", ap("rtb"), T.rt[:])
+    for t in range(1, VI):
+        landing("pkg%d" % t, "pk%d" % t, T.cores[(rank - t) % N])
+        landing("fin%d" % t, "fa%d" % t, T.cores[(rank - 1) % N])
+
+    kp, kp4096, kp16, par, Zc, Zn = [ap("cols", c, c + 1) for c in range(6)]
+    fill(ap("onesb"), 1.0)
+    fill(ap("ones32"), 1.0)
+    iota(ap("pidx", 0, 1), [[0, 1]], 0, 1)
+    sel = ap("Sel")
+    asel(sel, ap("onesb", P=8), [[1, 128]], A.is_ge, 0, -16)
+    asel(sel, sel, [[-1, 128]], A.is_ge, 15, 16)
+    iota(ap("CPi"), [[0, 6], [1, 2], [0, 16]], 0, 0)
+    mm(ap("mis", 0, 128), sel, sel, True, True)
+    ts(ap("pidx", 1, 2), ap("pidx", 0, 1), 15, A.bitwise_and)
+    ts(ap("pidx", 2, 3), ap("pidx", 0, 1), 4, A.arith_shift_right, 1, A.bitwise_and)
+    cp(kp, ap("pidx", 1, 2))
+    ts(kp4096, ap("pidx", 1, 2), 4096.0, mul)
+    ts(kp16, ap("pidx", 1, 2), 16.0, mul)
+    cp(par, ap("pidx", 2, 3))
+    ts(ap("W65", 0, 128), ap("mis", 0, 128), 65536.0, mul)
+    w = 128
+    while w < 2048:
+        cp(ap("W65", w, 2 * w), ap("W65", 0, w))
+        w *= 2
+    for h in range(2):
+        o = ap("W65", 1024 * h, 1024 * h + 1024)
+        asel(o, o, [[-1, 8], [0, 8], [1, 16]], eq, -8 * h, 0)
+        act(ap("W32", 1024 * h, 1024 * h + 1024), o, AF.Copy, 2.0 ** -16)
+    asel(ap("I32"), ap("ones32"), [[-1, 128]], eq, 0, 1)
+    cp(ap("BDb"), ap("mis", 0, 128))
+    cp(ap("BD32"), ap("mis", 0, 128))
+
+    for n, a, b in (("KU", 0, 16), ("KU", 208, 224), ("TB", 0, 16), ("TC", 192, 208)):
+        fill(ap(n, a, b), 0.0)
+    ts(ap("KU", 16, 208), ap("jcs"), kp4096, add)
+    cp(ap("srb"), ap("sr8"))
+    mm(ap("Wp", 0, 192), sel, ap("srb"), True, True)
+    ts(ap("OH"), ap("Wp", 0, 192), kp, eq)
+    tt(ap("Q0"), ap("OH"), ap("KU", 16, 208), mul)
+    for i in range(16):
+        mm(ap("mis", 128, 140), blk("W32", i), ap("Q0", (i, 192, 16)), i == 0, i == 15)
+
+    def tr(out, a):
+        emit("v", [a], [out], lambda: g.vector.transpose(out[0], a[0]))
+    tr(ap("TA"), ap("KU", 16, 208))
+    tr(ap("TB", 16, 208), ap("KU", 32, 224))
+    tr(ap("TC", 0, 192), ap("KU", 0, 192))
+    ts(ap("M1"), ap("CPi"), par, eq)
+    ts(ap("Me"), ap("CPi"), par, A.is_gt)
+    ts(ap("Mo"), ap("CPi"), par, A.is_lt)
+    tt(ap("t1"), ap("TA"), ap("M1"), mul)
+    tt(ap("t2"), ap("TB", 0, 192), ap("Me"), mul)
+    tt(ap("t3"), ap("TC", 16, 208), ap("Mo"), mul)
+    tt(ap("t1"), ap("t1"), ap("t2"), add)
+    tt(ap("pkg0", 0, 192), ap("t1"), ap("t3"), add)
+    cp(ap("pkg0", 192, 204), ap("mis", 128, 140))
+
+    def prep(t):
+        cp(iw("m0"), ap("pkg%d" % t, 192, 204))
+        ts(iw("c1n"), iw("m0"), 4095, A.bitwise_and)
+        ts(iw("p1n"), iw("m0"), 12, A.arith_shift_right)
+        cp(ap("c16n"), iw("c1n"))
+    prep(0)
+    for h in (0, 1024):
+        ts(ap("pf", h, h + 1024), ap("pks", h, h + 1024), 4095, A.bitwise_and)
+        ts(ap("pf", 2048 + h, 3072 + h), ap("pks", h, h + 1024), 12, A.arith_shift_right)
+    cp(ap("Ib"), ap("I32"))
+    ts(ap("nI"), ap("I32"), -1.0, mul)
+    fill(ap("rst"), 0.0)
+    fill(ap("rst", (0, 192, 16)), 33554432.0)
+    fill(ap("pf", 4096, 4480), 0)
+    fill(Zc, 0.0)
+    fill(ap("zt"), 0.0)
+
+    def late():
+        for t in range(1, VI):
+            send(T.cores[(rank + t) % N], T["pkg%d" % t][:], ap("pkg0"), "pk%d" % t)
+        iota(ap("J256"), [[256, 12]], 0, 0)
+        iota(ap("D24"), [[16, 24]], 4096, 0)
+        iota(ap("x12"), [[1, 12]], 0, 0)
+        iota(ap("i16"), [[0, 12], [1, 16]], 0, 0)
+        iota(ap("r96"), [[16, 6], [1, 16]], 0, 0)
+        for s in range(3):
+            ts(fw("POS%d" % s, 12, 0, NV), ap("J256", 0, NV), kp16, add, 3072.0 * s, add)
+            ts(fw("POS%d" % s, 12, NV, 12), ap("J256", NV, 12), kp, add, 3072.0 * s, add)
+        fill(fw("D36", 36, 0, 12), 0.0)
+        ts(fw("D36", 36, 12, 36), ap("D24"), kp, add)
+        fill(fw("G", 72), 0.0)
+        cp(ap("exo"), ap("x12"))
+        ts(ap("DIAG"), ap("i16"), kp, eq)
+        ts(ap("pm"), ap("i16", 0, 16), kp, eq)
+        for i in range(16):
+            act(blk("Vi", i), ap("BDb"), AF.Copy, ap("pm", i, i + 1))
+        rn, ra, rs = fw("rn", 6), fw("ra", 6), fw("rs", 6)
+        ts(rn, ap("r96", (0, 96, 16)), kp, add)
+        cp(rs, rn)
+        for b in range(1, 6):
+            ts(ra, rn, 12.0 * b, A.is_ge, -12.0, mul)
+            tt(rs, rs, ra, add)
+        ts(rs, rs, 11.0, A.min)
+        cp(ap("rk"), rs)
+        ts(ra, rn, 36.0, A.is_ge, 12.0, mul)
+        tt(rs, rs, ra, add)
+        cp(ap("rp"), rs)
+
+    nb = 16 * NV
+    cb = [(j, j + 2) for j in range(NV, 12, 2)]
+    vb = [(j, j + 2) for j in range(0, NV, 2)]
+    Y1, odd1, ev1 = iw("Y1", 24), iw("Y1", 24, 0, 12), iw("Y1", 24, 12, 24)
+    Y2, odd2, ev2 = iw("Y2", 24), iw("Y2", 24, 0, 12), iw("Y2", 24, 12, 24)
+    CC, c2, c3 = iw("CC", 24), iw("ci0"), iw("CC", 24, 0, 12)
+    p1, c1, kk1, kk2 = iw("p1"), iw("c1"), iw("kk1"), ap("kk2")
+    o1, o2, T21, V1, V2 = fw("o1"), fw("o2"), fw("T21"), fw("V1"), fw("V2")
+    SA, SAa, SAb = fw("SA", 24), fw("SA", 24, 0, 12), fw("SA", 24, 12, 24)
+
+    def C(a, b):
+        return fw("C", 72, a, b)
+    for t in range(VI):
+        fname = "fin%d" % t
+        K1 = "pkg%d" % t
+        dA, dB = fw("D36", 36, 12, 24), fw("D36", 36, 24, 36)
+        cp(p1, iw("p1n"))
+        cp(c1, iw("c1n"))
+        for s in range(3):
+            base = 3072 * s
+            cp(ap("N16"), ind(ap("pf"), ap("c16n" if s == 0 else "c16_%d" % (s - 1))))
+            if s == 2:
+                ts(kk2, iw("mi1"), 12, A.arith_shift_right, 15, A.bitwise_and)
+                cp(ap("kb"), kk2)
+            for k in range(16):
+                o, f = ap("FX", (k, 16 * nb, 16)), ap(fname, 0, nb)
+                if k < KS:
+                    act(o, f, AF.Copy)
+                else:
+                    cp(o, f)
+            for (j0, j1) in cb:
+                act(ap("GC", 256 * (j0 - NV), 256 * (j1 - NV)), ind(ap("rtb"), ap("N16", 16 * j0, 16 * j1)), AF.Copy)
+
+            def pc(j0, j1, k):
+                return ap("psC", j0 - NV, j1 - NV, third=(16 * k, 16 * k + 16))
+            for (j0, j1) in cb:
+                mm(ap("psC", j0 - NV, j1 - NV), ap("Ib"), ap("zt"), True, False)
+                for k in range(16):
+                    mm(pc(j0, j1, k), ap("nI"), ap(fname, 16 * j0, 16 * j1), False, False)
+            for (j0, j1) in cb:
+                for k in range(16):
+                    mm(pc(j0, j1, k), ap("Ib"), ap("GC", (256 * (j0 - NV) + k, 256 * (j1 - NV), 16)), False, k == 15)
+            for (j0, j1) in vb:
+                tt(ap("dall", base + 256 * j0, base + 256 * j1), ind(ap("rtb"), ap("N16", 16 * j0, 16 * j1)), ap("FX", 256 * j0, 256 * j1), sub)
+
+            def absv(b):
+                for j in range(*vb[b]):
+                    act(ap("D3", j), ap("dall", base + 256 * j, base + 256 * j + 256), AF.Abs)
+
+            def absc(b):
+                for j in range(*cb[b]):
+                    act(ap("dall", base + 256 * j, base + 256 * j + 256), ap("psC", j - NV), AF.Abs)
+
+            def key(j0, j1):
+                o = ap("key", 16 * j0, 16 * j1)
+                mm(o, ap("I32"), ap(K1, 16 * j0, 16 * j1), True, False)
+                for i in range(16):
+                    if j0 < NV:
+                        r = ap("D3", j0, j1, third=(16 * i, 16 * i + 16))
+                    else:
+                        r = ap("dall", (base + 256 * j0 + i, base + 256 * j1, 16))
+                    mm(o, blk("W65", i), r, False, i == 15)
+            if s == 2:
+                for i in range(16):
+                    mm(ap("Wp", (i, 192, 16)), blk("Vi", i), ap("kb"), True, True)
+            absv(0)
+            absc(0)
+            absv(1)
+            absc(1)
+            absv(2)
+            absv(3)
+            key(0, 4)
+            key(NV, 12)
+            key(4, NV)
+
+            if s == 0:
+                if t == 0:
+                    late()
+                else:
+                    tt(fw("x"), kk2, ap("kk3"), eq)
+                    tt(fw("xa"), fw("x"), o2, mul)
+                    tt(fw("xb"), o2, fw("xa"), sub)
+                    tt(fw("xc"), fw("xb"), fw("T", 72, 0, 12), sub)
+                    tt(ap("o3b"), fw("xc"), fw("T", 72, 36, 48), sub)
+                    mm(ap("mis", 0, 12), ap("onesb"), ap("o3b"), True, True)
+                    emit("v", [ap("mis", 0, 12)], [Zn], lambda: g.vector.tensor_reduce(Zn[0], ap("mis", 0, 12)[0], X, add))
+                    tt(Zc, Zc, Zn, add)
+                for i in range(16):
+                    mm(ap("mis", 128, 140), blk("W65", i), ap(fname, (i, 192, 16)), i == 0, i == 15)
+                ts(iw("d0z"), ap("mis", 128, 140), 2.0 ** -16, mul, Zc, add)
+            if s == 1:
+                ts(kk1, iw("mi0"), 12, A.arith_shift_right, 15, A.bitwise_and)
+                ts(iw("d1"), iw("mi0"), 16, A.arith_shift_right)
+                tt(fw("Ly"), fw("POS1"), fw("L0"), sub)
+                tt(o1, kk1, p1, A.not_equal)
+                tt(iw("x1"), iw("d1"), iw("d0z"), add)
+                ts(fw("V1a"), kk1, 8192.0, mul)
+                ts(iw("d1z"), iw("d1"), Zc, add)
+                tt(fw("Lya"), fw("Ly"), o1, mul)
+                ts(odd1, iw("x1"), 1, A.bitwise_and)
+                tt(V1, fw("V1a"), c1, add)
+                ts(fw("q"), o1, -16.0, mul, 16.0, add)
+                tt(fw("Lb1"), fw("Lya"), fw("L0"), add)
+                ts(ev1, odd1, -1.0, mul, 1.0, add)
+                tt(fw("VA1"), V1, dA, sub)
+                tt(fw("p1x"), fw("q"), p1, add)
+                tt(fw("k1x"), fw("q"), kk1, add)
+                ts(fw("G", 72, 0, 24), Y1, 8192.0, mul)
+                tt(SAa, V1, ev1, mul)
+                tt(SAb, fw("VA1"), odd1, mul)
+                if t + 1 < VI:
+                    prep(t + 1)
+            if s == 2:
+                ts(iw("d2"), iw("mi1"), 16, A.arith_shift_right)
+                tt(T21, kk2, fw("p1x"), eq)
+                tt(fw("e22"), kk2, fw("k1x"), eq)
+                ts(fw("V2a"), kk2, 8192.0, mul)
+                tt(iw("x2"), iw("d2"), iw("d1z"), add)
+                tt(fw("o2a"), o1, T21, sub)
+                tt(V2, fw("V2a"), c2, add)
+                ts(odd2, iw("x2"), 1, A.bitwise_and)
+                tt(o2, fw("o2a"), fw("e22"), sub)
+                tt(fw("Lu"), fw("POS2"), fw("L1"), sub)
+                ts(ap("EQ", 384, 576), ap("Wp", 0, 192), kp, eq, 8192.0, mul)
+                ts(ev2, odd2, -1.0, mul, 1.0, add)
+                ts(fw("qb"), o2, -16.0, mul, 16.0, add)
+                tt(C(24, 36), V2, dB, sub)
+                tt(fw("Lv"), fw("Lu"), o2, mul)
+                tt(ap("P24", 0, 12), fw("qb"), p1, add)
+                tt(ap("P24", 12, 24), fw("qb"), kk1, add)
+                tt(ap("Bv", 384, 576), ind(ap("pf"), ap("c16_0")), ap("EQ", 384, 576), sub)
+                cp(ap("P"), ind(ap("P24"), ap("rp", 0, 5)))
+                tt(fw("Lb"), fw("Lv"), fw("L1"), add)
+                tt(iw("CC", 24, 12, 24), c3, dA, sub)
+                tt(fw("eV"), V2, ev2, mul)
+                tt(fw("x3"), V2, odd1, mul)
+                tt(fw("x4"), C(24, 36), ev1, mul)
+                tt(fw("CA", 24), Y1, CC, mul)
+                tt(fw("CB", 24), Y2, CC, mul)
+                tt(C(60, 72), C(24, 36), odd2, mul)
+                ts(fw("G", 72, 36, 60), Y2, 8192.0, mul)
+                tt(fw("x5"), fw("x3"), SAa, add)
+                tt(fw("X36", 36, 12, 24), SAb, T21, mul)
+                tt(fw("X36", 36, 24, 36), fw("x4"), T21, mul)
+                tt(C(0, 24), fw("CA", 24), SA, add)
+                tt(C(36, 48), fw("CB", 24, 0, 12), fw("eV"), add)
+                tt(fw("X36", 36, 0, 12), fw("x5"), T21, mul)
+                cp(C(48, 60), fw("CB", 24, 12, 24))
+                tt(fw("BX", 36), fw("X36", 36), fw("D36", 36), add)
+
+            kr = ap("key", 0, 192)
+            emit("v", [ap("rst"), kr], [ap("run")], lambda: g.vector.tensor_tensor_scan(ap("run")[0], ap("rst")[0], kr[0], 0.0, A.max, A.min))
+            mn, kn = "mi%d" % s, "kL%d" % s
+            mi, kL = iw(mn), iw(kn)
+            cp(mi, ap("run", (15, 192, 16)))
+            if s < 2:
+                ts(c2 if s == 0 else c3, mi, 4095, A.bitwise_and)
+            ts(iw(kn, 12, 0, NV), iw(mn, 12, 0, NV), 12, A.arith_shift_right, 15, A.bitwise_and)
+            ts(iw(kn, 12, NV, 12), iw(mn, 12, NV, 12), 8, A.arith_shift_right, 240, A.bitwise_and)
+            if s < 2:
+                cp(ap("c16_%d" % s), c2 if s == 0 else c3)
+                if s == 1:
+                    tt(iw("kLo"), kL, o1, mul)
+                    kL = iw("kLo")
+                tt(fw("L%d" % s), kL, fw("POS0" if s == 0 else "Lb1"), add)
+                cp(ap("L16"), fw("L%d" % s))
+                fname = "fa" if s == 0 else "fb"
+                act(ap(fname), ind(ap("dall", 0, base + 3072), ap("L16")), AF.Abs)
+            else:
+                tt(fw("Lz"), kL, o2, mul)
+                ts(ap("kk3"), mi, 12, A.arith_shift_right, 15, A.bitwise_and)
+                tt(fw("Lw"), fw("Lz"), fw("Lb"), add)
+                cp(ap("K"), ind(ap("kk3"), ap("rk", 0, 5)))
+                cp(ap("L16"), fw("Lw"))
+                fo = ap("fo%d" % t)
+                act(fo, ind(ap("dall"), ap("L16")), AF.Abs)
+        if t + 1 < VI:
+            send(T.cores[(rank + 1) % N], T["fin%d" % (t + 1)][:], fo, "fa%d" % (t + 1))
+        else:
+            dma("y", "dyf", T.yf[:], fo[0], [fo], [])
+
+        tt(fw("T", 72), ap("K", 0, 72), ap("P", 0, 72), eq)
+        tt(fw("H", 72), ap("K", 0, 72), fw("G", 72), mul)
+        tt(fw("Ha", 72), fw("H", 72), fw("C", 72), add)
+        tt(fw("Hb", 72), fw("Ha", 72), fw("T", 72), mul)
+        tt(fw("Hc", 36), fw("Hb", 72, 0, 36), fw("Hb", 72, 36, 72), add)
+        tt(iw("sel", 36), fw("Hc", 36), fw("BX", 36), add)
+        ts(ap("sk"), iw("sel", 36), 13, A.arith_shift_right)
+        ts(iw("sc", 36), iw("sel", 36), 8191, A.bitwise_and)
+        tt(ap("R"), ind(ap("sk"), ap("exo")), ap("DIAG"), mul)
+        mm(ap("U", 512, 704), ap("BDb"), ap("R"), True, True)
+        cp(ap("cl16"), iw("sc", 36))
+        cp(ap("kA"), ap("sk", 12, 24))
+        for i in range(16):
+            mm(ap("U", (i, 192, 16)), blk("Vi", i), ap("kA"), True, True)
+        ts(ap("EQ", 0, 192), ap("U", 512, 704), kp, eq, 8192.0, mul)
+        tt(ap("Bv", 0, 192), ind(ap("pf"), ap("cl16", 0, 12)), ap("EQ", 0, 192), sub)
+        ts(ap("Qs"), ap("Bv", 0, 192), 0.0, A.min)
+        mm(ap("Wp", 0, 192), ap("BD32"), ap("Qs"), True, False)
+        mm(ap("Wp", 0, 192), ap("Ib"), ap("EQ", 384, 576), False, True)
+        ts(ap("EQ", 192, 384), ap("U", 0, 192), kp, eq, 8192.0, mul)
+        mm(ap("U", 192, 384), ap("BD32"), ap("Qs"), True, False)
+        mm(ap("U", 192, 384), ap("Ib"), ap("EQ", 192, 384), False, True)
+        tt(ap("Bv", 192, 384), ind(ap("pf"), ap("cl16", 12, 24)), ap("EQ", 192, 384), sub)
+        tt(ap("newv", 192, 384), ap("Bv", 384, 576), ap("Wp", 0, 192), A.max)
+        tt(ap("newv", 0, 192), ap("Bv", 192, 384), ap("U", 192, 384), A.max)
+        pfo = ind(ap("pf"), ap("cl16", 12, 36))
+        emit("v", [ap("newv"), ap("cl16", 12, 36)], [ap("pf")], lambda: g.vector.tensor_copy(pfo[0], ap("newv")[0]))
+
+    for q in range(4):
+        o, u = 512 * q, 512 * (q % 2)
+        ts(ap("U", u, u + 512), ap("pf", 2048 + o, 2560 + o), 4096.0, mul)
+        tt(ap("yps", o, o + 512), ap("pf", o, o + 512), ap("U", u, u + 512), add)
+        dma("y", "dy%d" % q, T.yp[:, o:o + 512], ap("yps", o, o + 512)[0], [ap("yps", o, o + 512)], [])
+    for sem in SEMAPHORES:
+        if total.get(sem, 0) > know["g"].get(sem, 0):
+            g.wait_ge(T.sem[sem], total[sem])

@@ -2,27 +2,87 @@ from concourse.mybir import dt, AluOpType, AxisListType, ActivationFunctionType
 
 N = 8
 VI = 4
-NV = 8
-KS = 3
+NJ, NC = 6, 96
+SG = [[32, 16], [32, 32], [32, 48]]
+VC = 32
+M = 8192.0
+CY, PE, GA, SC, WAKE, DL, RL, BW = 0.92, 0.46, 1.56, 3.8, 100, 2000, 3000, 250
 F32, BF, I32T, U16 = "float32", "bfloat16", "int32", "uint16"
 SIZES = {
-    F32: "pkg0 204 pkg1 204 pkg2 204 pkg3 204 ones32 128 I32 128 BD32 128 W32 2048 pm 16 cols 8 M1 192 Me 192 Mo 192 KU 224 TA 192 "
-         "TB 208 TC 208 t1 192 t2 192 t3 192 OH 192 Q0 192 Qs 192 rst 192 run 192 fw 1400 P24 24 P 80 Bv 576 yps 2048",
-    BF: "rtb 4096 fin0 192 fin1 192 fin2 192 fin3 192 fo0 192 fo1 192 fo2 192 fo3 192 fa 192 fb 192 onesb 128 Ib 128 nI 128 zt 512 "
-        "BDb 128 W65 2048 Vi 2048 DIAG 192 FX %d dall 9216 GC %d o3b 12 kb 12 kA 12 R 192 EQ 576" % (256 * NV, 256 * (12 - NV)),
-    I32T: "pks 2048 pf 4480 jcs 192 pidx 4 CPi 192 i16 192 J256 12 D24 24 x12 12 r96 96 iw 640 kk2 12 kk3 12 K 80 sk 36 newv 384",
-    U16: "exo 12 rk 6 rp 6 N16 192 c16_0 12 c16_1 12 c16n 12 L16 12 cl16 36",
+    F32: "pkg0 216 pkg1 216 pkg2 216 pkg3 216 ones32 128 I32 128 BD32 128 Wz32 144 cols 8 KU 224 TA 416 "
+         "OH 192 Q0 192 rst 96 run0 96 run1 96 tab 32 Q 192 Bv 384 yps 2048 H 128 S1 64 S2 64",
+    BF: "rtb 4096 fxs 192 fin 768 fo 768 fw 768 yfs 192 onesb 144 Ib 128 nI 128 Wz 144 En 1536 nM 192 "
+        "GC00 1552 GC01 1552 GC10 1552 GC11 1552 RS 384 R3 192 EQD 192 EQ 384 E 32 E3 12 O2 12",
+    I32T: "pks 2048 pf 4096 jcs 192 pidx 4 tl 36 i32 32 mi 12 m0 12 r4 12 yi 24 newv 384",
+    U16: "rep 4 TL 12 N16 192 CL0 12 CL1 24 CL2 24 L3 12 SL 64",
 }
+SEG = "c1 c2 c3 p1 k1 k2 k3 L1 L2 L3".split()
+WSEG = "POS POSb POSc PO2 PO3 P1 P2 P3 o1 oa ne T Tb da db ea eb fa fb ga gb ha hb ma mb qa qb".split()
+YSEG = "y1 y1b y2 y2b".split()
 SCRATCH = {
-    "sr8": ("sbuf", [8, 192], I32T), "srb": ("sbuf", [8, 192], BF), "Sel": ("sbuf", [8, 128], BF), "D3": ("sbuf", [128, NV, 256], BF),
-    "key": ("psum", [128, 512], F32), "psC": ("psum", [128, 4, 256], F32), "U": ("psum", [128, 1024], F32),
-    "Wp": ("psum", [128, 512], F32), "mis": ("psum", [128, 512], F32),
+    "sr8": ("sbuf", [8, 192], I32T), "srb": ("sbuf", [8, 192], BF), "Sel": ("sbuf", [8, 128], BF),
+    "D0": ("sbuf", [128, NJ, 256], BF), "D1": ("sbuf", [128, NJ, 256], BF),
+    "KC0": ("sbuf", [128, 2, len(SEG), NJ], I32T), "KC1": ("sbuf", [128, 2, len(SEG), NJ], I32T),
+    "W4": ("sbuf", [128, 2, len(WSEG), NJ], F32), "Y4": ("sbuf", [128, 2, len(YSEG), NJ], I32T),
+    "AB": ("sbuf", [128, 2, 64], F32), "BS": ("sbuf", [128, 2, 32], F32),
+    "sub": ("psum", [128, 3072], F32), "pb0": ("psum", [128, 512], F32), "pb1": ("psum", [128, 512], F32),
 }
 for _ty in SIZES:
     _l = SIZES[_ty].split()
     for _i in range(0, len(_l), 2):
         SCRATCH[_l[_i]] = ("sbuf", [128, int(_l[_i + 1])], _ty)
-SEMAPHORES = "cv cs ct cg ls pk1 pk2 pk3 fa1 fa2 fa3 dj ds df dp0 dp1 dr dyf dy0 dy1 dy2 dy3".split()
+SEMAPHORES = "cv cs ct cg ls pk1 pk2 pk3 fa0 fa1 fa2 fa3 fa4 fa5 dj ds df dp0 dp1 dp2 dp3 dr dyf dy0 dy1 dy2 dy3".split()
+WIDTH = {F32: 4, BF: 2, I32T: 4, U16: 2}
+
+
+def place(ops, before, rank):
+    busy, start = {}, {}
+    for n in sorted(range(len(ops)), key=lambda n: rank[n]):
+        o = ops[n]
+        t = max([start[p] + gap for p, gap in before[n]] + [0.0])
+        slots = busy.setdefault(o["q"], [])
+        i = len(slots)
+        while i and slots[i - 1][1] > t:
+            i -= 1
+        while i < len(slots) and o["q"] and slots[i][0] < t + o["cost"]:
+            t = max(t, slots[i][1])
+            i += 1
+        slots.insert(i, (t, t + o["cost"]))
+        start[n] = t
+    return start
+
+
+def issue(g, T, ops):
+    fore, back = [[] for _ in ops], [[] for _ in ops]
+    for n, o in enumerate(ops):
+        for p in o["dep"] + o["soft"]:
+            gap = ops[p]["lat"] + (0 if p in o["soft"] else WAKE)
+            fore[n].append((p, ops[p]["cost"] + gap))
+            back[p].append((n, o["cost"] + gap))
+    start = place(ops, fore, [(n, n) for n in range(len(ops))])
+    late = place(ops, back, [(-start[n] - o["cost"], -n) for n, o in enumerate(ops)])
+    start = place(ops, fore, [(-late[n] - o["cost"], n) for n, o in enumerate(ops)])
+    seq = sorted(range(len(ops)), key=lambda n: (start[n], n))
+    queues = {"v": g.vector, "s": g.scalar, "t": g.tensor, "g": g, "y": g.sync}
+    know = {q: {} for q in queues}
+    total, mark = {}, {}
+    for n in seq:
+        o = ops[n]
+        k = know.get(o["q"], {})
+        for sem, val, clock in sorted([mark[p] for p in o["dep"]], key=lambda e: (-len(e[2]), -e[1])):
+            if k.get(sem, 0) < val:
+                queues[o["q"]].wait_ge(T.sem[sem], val)
+                for s2, v2 in clock.items():
+                    k[s2] = max(k.get(s2, 0), v2)
+        total[o["sem"]] = total.get(o["sem"], 0) + o["inc"]
+        if o["call"]:
+            r = o["call"]()
+            if o["sem"] != "ls":
+                r.then_inc(T.sem[o["sem"]], o["inc"])
+        mark[n] = (o["sem"], total[o["sem"]], dict(k, **{o["sem"]: total[o["sem"]]}))
+    for sem in SEMAPHORES:
+        if total.get(sem, 0) > know["g"].get(sem, 0):
+            g.wait_ge(T.sem[sem], total[sem])
 
 
 def rank_program(g, core, T, topo):
@@ -31,462 +91,370 @@ def rank_program(g, core, T, topo):
         return
     A, AF, X = AluOpType, ActivationFunctionType, AxisListType.X
     add, sub, mul, eq = A.add, A.subtract, A.mult, A.is_equal
-    queues = {"v": g.vector, "s": g.scalar, "t": g.tensor, "g": g, "y": g.sync}
-    csem = {"v": "cv", "s": "cs", "t": "ct", "g": "cg"}
-    know = {q: {} for q in queues}
-    total, clock, hist = {}, {}, {}
+    ops, wrote, read, sent, loaded = [], {}, {}, {}, [0, None]
 
-    def ap(name, a=None, b=None, P=None, third=None):
+    def ap(name, a=None, b=None, P=None):
         shape = SCRATCH[name][1]
-        p = slice(0, shape[0]) if P is None else slice(0, P)
-        if len(shape) == 2:
-            lo, hi, st = (0, shape[1], 1) if a is None else (a if isinstance(a, tuple) else (a, b, 1))
-            return (T[name][p, slice(lo, hi) if st == 1 else slice(lo, hi, st)], [(name, lo, hi, st)])
-        w = shape[2]
-        k0, k1 = third if third else (0, w)
-        if b is None:
-            return (T[name][p, a, k0:k1], [(name, a * w + k0, a * w + k1, 1)])
-        return (T[name][p, a:b, k0:k1], [(name, a * w + k0, (b - 1) * w + k1, 1)])
+        p = slice(0, shape[0] if P is None else P)
+        lo, hi, st = (0, shape[1], 1) if a is None else (a if isinstance(a, tuple) else (a, b, 1))
+        return (T[name][p, slice(lo, hi) if st == 1 else slice(lo, hi, st)], [(name, lo, hi, st)])
+
+    def nd(name, *ix):
+        shape = SCRATCH[name][1]
+        runs = [0]
+        for d, (lo, hi, st) in enumerate(ix[:-1]):
+            runs = [(r + i) * shape[d + 2] for r in runs for i in range(lo, hi, st)]
+        lo, hi, _ = ix[-1]
+        view = T[name][(slice(0, 128),) + tuple(l if h == l + 1 else slice(l, h, s) for l, h, s in ix)]
+        return (view, [(name, r + lo, r + hi, 1) for r in runs])
 
     def ind(win, off):
-        return (win[0].indirect(off[0]), win[1] + off[1])
+        return (win[0].indirect(off[0]), win[1] + off[1], True)
 
-    def order(q, rw):
-        want = {}
+    def cols(a):
+        return sum(len(range(lo, hi, st)) for _, lo, hi, st in a[1])
+
+    def record(q, reads, writes, call, cost, sem=None, inc=1, lat=0, soft=()):
+        me, dep = len(ops), set()
+        rw = [(x, False) for r in reads for x in r[1]] + [(x, True) for r in writes for x in r[1]]
         for (name, lo, hi, st), isw in rw:
-            ps = SCRATCH[name][0] == "psum"
-            for (l2, h2, s2, w2, q2, sem, val) in hist.get(name, []):
-                same = q2 == q
-                if ps and not same:
-                    if not (lo // 512 <= (h2 - 1) // 512 and l2 // 512 <= (hi - 1) // 512):
-                        continue
-                else:
-                    if lo >= h2 or l2 >= hi or (st > 1 and st == s2 and (lo - l2) % st):
-                        continue
-                    if not (isw or w2) or (same and q == "t"):
-                        continue
-                if want.get(sem, 0) < val:
-                    want[sem] = val
-        k = know[q]
-        for sem in sorted(want, key=lambda s: -len(clock[(s, want[s])])):
-            if k.get(sem, 0) < want[sem]:
-                queues[q].wait_ge(T.sem[sem], want[sem])
-                for s2, v2 in clock[(sem, want[sem])].items():
-                    if k.get(s2, 0) < v2:
-                        k[s2] = v2
-
-    def note(owner, sem, val, rw, c):
-        total[sem] = val
-        c[sem] = val
-        clock[(sem, val)] = c
-        for (name, lo, hi, st), isw in rw:
-            keep = []
-            for e in hist.get(name, []):
-                inside = lo <= e[0] and e[1] <= hi and (st == 1 or (st == e[2] and (lo - e[0]) % st == 0))
-                if not (inside and (isw or (not e[3] and e[4] == owner))):
-                    keep.append(e)
-            keep.append((lo, hi, st, isw, owner, sem, val))
-            hist[name] = keep
-
-    def both(reads, writes):
-        return [(x, False) for r in reads for x in r[1]] + [(x, True) for r in writes for x in r[1]]
-
-    def emit(q, reads, writes, call):
-        rw = both(reads, writes)
-        order(q, rw)
-        sem = csem[q]
-        call().then_inc(T.sem[sem], 1)
-        note(q, sem, total.get(sem, 0) + 1, rw, dict(know[q]))
+            if SCRATCH[name][0] == "psum":
+                lo, hi, st, isw = lo // 512 * 512, (hi + 511) // 512 * 512, 1, True
+            for log in (wrote, read) if isw else (wrote,):
+                keep = []
+                for e in log.get(name, []):
+                    meets = lo < e[1] and e[0] < hi and not (st > 1 and st == e[2] and (lo - e[0]) % st)
+                    if meets and e[3] != me:
+                        dep.add(e[3])
+                    if not (isw and lo <= e[0] and e[1] <= hi and (st == 1 or (st == e[2] and (lo - e[0]) % st == 0))):
+                        keep.append(e)
+                log[name] = keep
+            (wrote if isw else read).setdefault(name, []).append((lo, hi, st, me))
+        inorder = [p for p in dep if q == "t" and ops[p]["q"] == "t"]
+        ops.append({"q": q, "call": call, "cost": cost, "lat": lat, "sem": sem or "c" + q, "inc": inc,
+                    "dep": [p for p in dep if p not in inorder], "soft": inorder + list(soft)})
+        return me
 
     def dma(q, sem, out, in_, reads, writes):
-        rw = both(reads, writes)
-        order(q, rw)
-        queues[q].dma_start(out, in_).then_inc(T.sem[sem], 16)
-        note("d" + sem, sem, 16, rw, dict(know[q]))
+        buf = (reads + writes)[0]
+        queue = g.sync if q == "y" else g.scalar
+        size = 128 * cols(buf) * WIDTH[SCRATCH[buf[1][0][0]][2]]
+        loaded[0] = size + (loaded[0] if writes else 0)
+        me = record(q, reads, writes, lambda: queue.dma_start(out, in_), 60, sem, 16, DL + loaded[0] / BW,
+                    [loaded[1]] if q == "y" and loaded[1] is not None else [])
+        if q == "y":
+            loaded[1] = me
 
     def load(q, sem, buf, x):
         dma(q, sem, buf[0], x, [], [buf])
 
-    def send(dst, dst_ap, src, rsem):
-        order("g", both([src], []))
+    def send(dst, src_core, dst_ap, src, rsem):
         rid, pid, _ = topo.addr(dst)
-        g.remote_dma(dst_ap, src[0], T.sem[rsem], T.sem["ls"], pid, rid, topo.mask(core, dst))
-        total["ls"] = total.get("ls", 0) + len(topo.engines(core, dst))
+        me = record("g", [src], [], lambda: g.remote_dma(dst_ap[0], src[0], T.sem[rsem], T.sem["ls"], pid, rid, topo.mask(core, dst)),
+                    300, "ls", len(topo.engines(core, dst)))
+        record(None, [], [dst_ap], None, 0, rsem, len(topo.engines(src_core, core)), RL, [me])
 
-    def landing(name, sem, src):
-        note("r" + sem, sem, len(topo.engines(src, core)), both([], [ap(name)]), {})
+    def vector(out, ins, per, call, more=()):
+        if len(ins) and len(ins[0]) == 3:
+            cost = 50 + CY * GA * cols(out)
+        else:
+            if all(WIDTH[SCRATCH[a[1][0][0]][2]] == 2 for a in [out] + ins) and per == 1:
+                per = 0.5
+            cost = CY * max(64, per * cols(out))
+        record("v", ins + list(more), [out], call, cost)
 
     def tt(out, a, b, op):
-        emit("v", [a, b], [out], lambda: g.vector.tensor_tensor(out[0], a[0], b[0], op))
+        per = 1.01 if "psum" in (SCRATCH[a[1][0][0]][0], SCRATCH[b[1][0][0]][0]) else 2
+        vector(out, [a, b], per, lambda: g.vector.tensor_tensor(out[0], a[0], b[0], op))
 
     def ts(out, a, s1, op0, s2=None, op1=None):
-        rd = [a] + [s for s in (s1, s2) if isinstance(s, tuple)]
         x1, x2 = [s[0] if isinstance(s, tuple) else s for s in (s1, s2)]
         more = [] if op1 is None else [op1]
-        emit("v", rd, [out], lambda: g.vector.tensor_scalar(out[0], a[0], x1, x2, op0, *more))
+        vector(out, [a], 1, lambda: g.vector.tensor_scalar(out[0], a[0], x1, x2, op0, *more), [s for s in (s1, s2) if isinstance(s, tuple)])
 
     def cp(out, a):
-        emit("v", [a], [out], lambda: g.vector.tensor_copy(out[0], a[0]))
+        vector(out, [a], 1, lambda: g.vector.tensor_copy(out[0], a[0]))
+
+    def scatter(win, off, a):
+        o = ind(win, off)
+        record("v", [a, off], [win], lambda: g.vector.tensor_copy(o[0], a[0]), 50 + CY * SC * cols(a))
 
     def fill(out, c):
-        emit("v", [], [out], lambda: g.vector.memset(out[0], c))
+        vector(out, [], 1, lambda: g.vector.memset(out[0], c))
 
     def act(out, a, func, scale=1.0):
-        sc = scale[0] if isinstance(scale, tuple) else scale
-        emit("s", [a] + ([scale] if isinstance(scale, tuple) else []), [out], lambda: g.scalar.activation(out[0], a[0], func, scale=sc))
+        record("s", [a], [out], lambda: g.scalar.activation(out[0], a[0], func, scale=scale), 65 + CY * cols(out) * (GA if len(a) == 3 else 1))
 
     def mm(out, l, r, start, stop):
-        emit("t", [l, r], [out], lambda: g.tensor.matmul(out[0], l[0], r[0], start, stop))
+        wide = 4 if SCRATCH[l[1][0][0]][2] == F32 else 1
+        record("t", [l, r], [out], lambda: g.tensor.matmul(out[0], l[0], r[0], start, stop), PE * wide * max(min(64, cols(l)), cols(r)))
 
     def iota(out, pattern, base, cm):
-        emit("g", [], [out], lambda: g.iota(out[0], pattern, base, cm))
+        record("g", [], [out], lambda: g.iota(out[0], pattern, base, cm, allow_small_or_imprecise_dtypes=True), 130 + 2 * CY * cols(out))
 
     def asel(out, a, pattern, op, base, cm):
-        emit("g", [a], [out], lambda: g.affine_select(out[0], a[0], pattern, op, 0.0, base, cm))
+        record("g", [a], [out], lambda: g.affine_select(out[0], a[0], pattern, op, 0.0, base, cm), 170 + 2 * CY * cols(out))
 
-    cols = {"fw": {}, "iw": {}}
+    def seg(buf, names, a, c, b):
+        i = names.index(a)
+        j = i if c is None else names.index(c)
+        return nd(buf, (0, 2, 1) if b is None else (b, b + 1, 1), (i, j + 1, max(j - i, 1)), (0, NJ, 1))
 
-    def work(buf, name, n, a, b):
-        c = cols[buf]
-        if name not in c:
-            c[name] = (sum(w for _, w in c.values()), n)
-        o, w = c[name]
-        return ap(buf, o + a, o + (w if b is None else b))
-
-    def fw(name, n=12, a=0, b=None):
-        return work("fw", name, n, a, b)
-
-    def iw(name, n=12, a=0, b=None):
-        return work("iw", name, n, a, b)
+    def w(a, c=None, b=None):
+        return seg("Y4", YSEG, a, c, b) if a in YSEG else seg("W4", WSEG, a, c, b)
 
     def blk(name, i):
-        return ap(name, 128 * i, 128 * i + 128)
+        return ap(name, 15 - i, 143 - i)
+
+    def pb(b, lo, hi, P=None):
+        return ap("pb%d" % b, lo, hi, P)
+
+    def ft(name, n):
+        return ap(name, 128 * n, 128 * n + 128, NC)
+
+    def ab(lo, hi):
+        return nd("AB", (0, 2, 1), (lo, hi, 1))
+
+    def bs(lo, hi):
+        return nd("BS", (0, 2, 1), (lo, hi, 1))
+
+    def ring(d):
+        return T.cores[(rank + d) % N]
 
     load("y", "dj", ap("jcs"), T.jc[:])
     load("s", "ds", ap("sr8"), T.sr[:])
-    load("s", "df", ap("fin0"), T.fx[:])
-    load("y", "dp0", ap("pks", 0, 1024), T.pk[:, 0:1024])
-    load("y", "dp1", ap("pks", 1024, 2048), T.pk[:, 1024:2048])
+    load("s", "df", ap("fxs"), T.fx[:])
+    for h in range(4):
+        load("y", "dp%d" % h, ap("pks", 512 * h, 512 * h + 512), T.pk[:, 512 * h:512 * h + 512])
     load("y", "dr", ap("rtb"), T.rt[:])
-    for t in range(1, VI):
-        landing("pkg%d" % t, "pk%d" % t, T.cores[(rank - t) % N])
-        landing("fin%d" % t, "fa%d" % t, T.cores[(rank - 1) % N])
 
     kp, kp4096, kp16, par, Zc, Zn = [ap("cols", c, c + 1) for c in range(6)]
+    pos = nd("W4", (0, 2, 1), (0, 3, 1), (0, NJ, 1))
+    sel = ap("Sel")
     fill(ap("onesb"), 1.0)
     fill(ap("ones32"), 1.0)
     iota(ap("pidx", 0, 1), [[0, 1]], 0, 1)
-    sel = ap("Sel")
-    asel(sel, ap("onesb", P=8), [[1, 128]], A.is_ge, 0, -16)
+    asel(sel, ap("onesb", 0, 128, P=8), [[1, 128]], A.is_ge, 0, -16)
     asel(sel, sel, [[-1, 128]], A.is_ge, 15, 16)
-    iota(ap("CPi"), [[0, 6], [1, 2], [0, 16]], 0, 0)
-    mm(ap("mis", 0, 128), sel, sel, True, True)
+    iota(ap("i32"), [[1, 32]], 0, 0)
+    iota(ap("tl", 0, 12), [[0, 6], [1, 2]], 0, 0)
+    asel(ap("I32"), ap("ones32"), [[-1, 128]], eq, 0, 1)
+    iota(pos, [[0, 6], [256, NJ]], 0, 0)
+    mm(pb(0, 0, 128), sel, sel, True, True)
+    fill(ap("En"), -1.0)
+    asel(ap("En"), ap("En"), [[1, NC], [0, 16]], eq, 0, -1)
     ts(ap("pidx", 1, 2), ap("pidx", 0, 1), 15, A.bitwise_and)
     ts(ap("pidx", 2, 3), ap("pidx", 0, 1), 4, A.arith_shift_right, 1, A.bitwise_and)
     cp(kp, ap("pidx", 1, 2))
     ts(kp4096, ap("pidx", 1, 2), 4096.0, mul)
-    ts(kp16, ap("pidx", 1, 2), 16.0, mul)
+    ts(kp16, ap("pidx", 1, 2), 16.0, mul, 16.0, add)
     cp(par, ap("pidx", 2, 3))
-    ts(ap("W65", 0, 128), ap("mis", 0, 128), 65536.0, mul)
-    w = 128
-    while w < 2048:
-        cp(ap("W65", w, 2 * w), ap("W65", 0, w))
-        w *= 2
-    for h in range(2):
-        o = ap("W65", 1024 * h, 1024 * h + 1024)
-        asel(o, o, [[-1, 8], [0, 8], [1, 16]], eq, -8 * h, 0)
-        act(ap("W32", 1024 * h, 1024 * h + 1024), o, AF.Copy, 2.0 ** -16)
-    asel(ap("I32"), ap("ones32"), [[-1, 128]], eq, 0, 1)
-    cp(ap("BDb"), ap("mis", 0, 128))
-    cp(ap("BD32"), ap("mis", 0, 128))
+    fill(ap("Wz32"), 0.0)
+    cp(ap("Wz32", (15, 143, 16)), pb(0, (0, 128, 16), None))
+    act(ap("BD32"), pb(0, 0, 128), AF.Copy)
+    act(ap("Wz"), ap("Wz32"), AF.Copy, 65536.0)
+    act(ap("Ib"), ap("I32"), AF.Copy)
+    act(ap("nI"), ap("I32"), AF.Copy, -1.0)
+    for b in range(2):
+        for h in range(2):
+            fill(ap("GC%d%d" % (b, h), 0, 16), 0.0)
+    fill(ap("rst"), 0.0)
+    fill(ap("rst", (0, NC, 16)), 33554432.0)
+    ts(pos, pos, kp16, add)
+    fill(Zc, 0.0)
+    ts(ap("tab"), ap("i32"), kp, eq)
+    fill(ap("nM"), -M)
+    fill(ap("fo"), 0.0)
+    fill(ab(0, 64), -16.0)
+    n, q, u = ap("r4", 0, 4), ap("r4", 4, 8), ap("r4", 8, 12)
+    ts(n, ap("i32", (0, 16, 4)), 4.0, mul, kp, add)
+    ts(q, n, -2.5, add, 1.0 / 6, mul)
+    ts(u, n, 30.0, A.is_ge)
+    tt(q, q, u, sub)
+    ts(q, q, -6.0, mul)
+    tt(n, n, q, add)
+    cp(ap("rep"), n)
 
-    for n, a, b in (("KU", 0, 16), ("KU", 208, 224), ("TB", 0, 16), ("TC", 192, 208)):
-        fill(ap(n, a, b), 0.0)
-    ts(ap("KU", 16, 208), ap("jcs"), kp4096, add)
+    fill(ap("KU", 0, 16), 0.0)
+    fill(ap("KU", 208, 224), 0.0)
     cp(ap("srb"), ap("sr8"))
-    mm(ap("Wp", 0, 192), sel, ap("srb"), True, True)
-    ts(ap("OH"), ap("Wp", 0, 192), kp, eq)
+    ts(ap("KU", 16, 208), ap("jcs"), kp4096, add)
+    mm(pb(1, 0, 192), sel, ap("srb"), True, True)
+    ts(ap("OH"), pb(1, 0, 192), kp, eq)
     tt(ap("Q0"), ap("OH"), ap("KU", 16, 208), mul)
     for i in range(16):
-        mm(ap("mis", 128, 140), blk("W32", i), ap("Q0", (i, 192, 16)), i == 0, i == 15)
+        mm(pb(1, 192, 204), blk("Wz32", i), ap("Q0", (i, 192, 16)), i == 0, i == 15)
+    cp(ap("m0"), pb(1, 192, 204))
+    ts(seg("KC0", SEG, "c1", None, None), ap("m0"), 4095, A.bitwise_and)
+    ts(seg("KC0", SEG, "p1", None, None), ap("m0"), 12, A.arith_shift_right)
+    cp(ap("CL0"), seg("KC0", SEG, "c1", None, None))
+    for b in range(2):
+        mm(pb(0, 128, 256, NC), ap("fxs", NC * b, NC * b + NC), ap("Ib"), True, True)
+        act(ft("fw", 4 + b), pb(0, 128, 256, NC), AF.Copy)
+    for o, a in ((ap("TA", 0, 192), ap("KU", 16, 208)), (ap("TA", 192, 416), ap("KU"))):
+        vector(o, [a], 1, lambda o=o, a=a: g.vector.transpose(o[0], a[0]))
+    ts(ap("tl", 12, 24), ap("tl", 0, 12), par, A.not_equal, 208.0, mul)
+    ts(ap("tl", 24, 36), ap("i32", 0, 12), 16.0, mul, kp, add)
+    tt(ap("tl", 24, 36), ap("tl", 24, 36), ap("tl", 12, 24), add)
+    cp(ap("TL"), ap("tl", 24, 36))
+    act(ap("pkg0", 0, 192), ind(ap("TA"), ap("TL")), AF.Copy)
+    cp(ap("pkg0", 192, 216), seg("KC0", SEG, "c1", "p1", None))
+    for t in range(1, VI):
+        send(ring(t), ring(-t), ap("pkg%d" % t), ap("pkg0"), "pk%d" % t)
+    for h in range(0, 2048, 512):
+        ts(ap("pf", h, h + 512), ap("pks", h, h + 512), 4095, A.bitwise_and)
+        ts(ap("pf", 2048 + h, 2560 + h), ap("pks", h, h + 512), 12, A.arith_shift_right)
 
-    def tr(out, a):
-        emit("v", [a], [out], lambda: g.vector.transpose(out[0], a[0]))
-    tr(ap("TA"), ap("KU", 16, 208))
-    tr(ap("TB", 16, 208), ap("KU", 32, 224))
-    tr(ap("TC", 0, 192), ap("KU", 0, 192))
-    ts(ap("M1"), ap("CPi"), par, eq)
-    ts(ap("Me"), ap("CPi"), par, A.is_gt)
-    ts(ap("Mo"), ap("CPi"), par, A.is_lt)
-    tt(ap("t1"), ap("TA"), ap("M1"), mul)
-    tt(ap("t2"), ap("TB", 0, 192), ap("Me"), mul)
-    tt(ap("t3"), ap("TC", 16, 208), ap("Mo"), mul)
-    tt(ap("t1"), ap("t1"), ap("t2"), add)
-    tt(ap("pkg0", 0, 192), ap("t1"), ap("t3"), add)
-    cp(ap("pkg0", 192, 204), ap("mis", 128, 140))
+    def visit(t):
+        KC, KN, last = "KC%d" % (t % 2), "KC%d" % ((t + 1) % 2), t + 1 == VI
+        facts = [ft("fw", 4 + b) if t == 0 else ft("fin", 2 * (t - 1) + b) for b in range(2)]
 
-    def prep(t):
-        cp(iw("m0"), ap("pkg%d" % t, 192, 204))
-        ts(iw("c1n"), iw("m0"), 4095, A.bitwise_and)
-        ts(iw("p1n"), iw("m0"), 12, A.arith_shift_right)
-        cp(ap("c16n"), iw("c1n"))
-    prep(0)
-    for h in (0, 1024):
-        ts(ap("pf", h, h + 1024), ap("pks", h, h + 1024), 4095, A.bitwise_and)
-        ts(ap("pf", 2048 + h, 3072 + h), ap("pks", h, h + 1024), 12, A.arith_shift_right)
-    cp(ap("Ib"), ap("I32"))
-    ts(ap("nI"), ap("I32"), -1.0, mul)
-    fill(ap("rst"), 0.0)
-    fill(ap("rst", (0, 192, 16)), 33554432.0)
-    fill(ap("pf", 4096, 4480), 0)
-    fill(Zc, 0.0)
-    fill(ap("zt"), 0.0)
+        def k(a, c=None, b=None):
+            return seg(KC, SEG, a, c, b)
 
-    def late():
-        for t in range(1, VI):
-            send(T.cores[(rank + t) % N], T["pkg%d" % t][:], ap("pkg0"), "pk%d" % t)
-        iota(ap("J256"), [[256, 12]], 0, 0)
-        iota(ap("D24"), [[16, 24]], 4096, 0)
-        iota(ap("x12"), [[1, 12]], 0, 0)
-        iota(ap("i16"), [[0, 12], [1, 16]], 0, 0)
-        iota(ap("r96"), [[16, 6], [1, 16]], 0, 0)
-        for s in range(3):
-            ts(fw("POS%d" % s, 12, 0, NV), ap("J256", 0, NV), kp16, add, 3072.0 * s, add)
-            ts(fw("POS%d" % s, 12, NV, 12), ap("J256", NV, 12), kp, add, 3072.0 * s, add)
-        fill(fw("D36", 36, 0, 12), 0.0)
-        ts(fw("D36", 36, 12, 36), ap("D24"), kp, add)
-        fill(fw("G", 72), 0.0)
-        cp(ap("exo"), ap("x12"))
-        ts(ap("DIAG"), ap("i16"), kp, eq)
-        ts(ap("pm"), ap("i16", 0, 16), kp, eq)
-        for i in range(16):
-            act(blk("Vi", i), ap("BDb"), AF.Copy, ap("pm", i, i + 1))
-        rn, ra, rs = fw("rn", 6), fw("ra", 6), fw("rs", 6)
-        ts(rn, ap("r96", (0, 96, 16)), kp, add)
-        cp(rs, rn)
-        for b in range(1, 6):
-            ts(ra, rn, 12.0 * b, A.is_ge, -12.0, mul)
-            tt(rs, rs, ra, add)
-        ts(rs, rs, 11.0, A.min)
-        cp(ap("rk"), rs)
-        ts(ra, rn, 36.0, A.is_ge, 12.0, mul)
-        tt(rs, rs, ra, add)
-        cp(ap("rp"), rs)
+        def court(s, b):
+            return ap("CL0", NJ * b, NJ * b + NJ) if s == 0 else ap("CL%d" % s, 12 * b, 12 * b + NJ)
 
-    nb = 16 * NV
-    cb = [(j, j + 2) for j in range(NV, 12, 2)]
-    vb = [(j, j + 2) for j in range(0, NV, 2)]
-    Y1, odd1, ev1 = iw("Y1", 24), iw("Y1", 24, 0, 12), iw("Y1", 24, 12, 24)
-    Y2, odd2, ev2 = iw("Y2", 24), iw("Y2", 24, 0, 12), iw("Y2", 24, 12, 24)
-    CC, c2, c3 = iw("CC", 24), iw("ci0"), iw("CC", 24, 0, 12)
-    p1, c1, kk1, kk2 = iw("p1"), iw("c1"), iw("kk1"), ap("kk2")
-    o1, o2, T21, V1, V2 = fw("o1"), fw("o2"), fw("T21"), fw("V1"), fw("V2")
-    SA, SAa, SAb = fw("SA", 24), fw("SA", 24, 0, 12), fw("SA", 24, 12, 24)
+        def keys(s, b):
+            gc, D = "GC%d%d" % (b, (t + s) % 2), "D%d" % b
+            cp(ap("N16", NC * b, NC * b + NC), ind(ap("pf"), court(s, b)))
+            nv = NC - SG[s][b]
+            cut = list(range(0, nv, VC)) + [nv] + [x for x in (32, 64) if x > nv] + [NC]
+            for x0, x1 in zip(cut, cut[1:]):
+                o, a = ap(gc, 16 + 16 * x0, 16 + 16 * x1), ind(ap("rtb"), ap("N16", NC * b + x0, NC * b + x1))
+                if x0 < nv:
+                    cp(o, a)
+                elif x0 < x1:
+                    act(o, a, AF.Copy)
+            for c in range(3):
+                bank = ap("sub", 1536 * b + 512 * c, 1536 * b + 512 * c + 512)
+                mm(bank, facts[b], ap("En", 512 * c, 512 * c + 512, NC), True, False)
+                mm(bank, ap("Ib"), ap(gc, 16 + 512 * c, 528 + 512 * c), False, True)
+                act(nd(D, (2 * c, 2 * c + 2, 1), (0, 256, 1)), bank, AF.Abs)
+            mm(pb(b, 0, NC), ap("I32"), ap("pkg%d" % t, NC * b, NC * b + NC), True, False)
+            for i in range(16):
+                mm(pb(b, 0, NC), blk("Wz", i), nd(D, (0, NJ, 1), (16 * i, 16 * i + 16, 1)), False, i == 15)
 
-    def C(a, b):
-        return fw("C", 72, a, b)
-    for t in range(VI):
-        fname = "fin%d" % t
-        K1 = "pkg%d" % t
-        dA, dB = fw("D36", 36, 12, 24), fw("D36", 36, 24, 36)
-        cp(p1, iw("p1n"))
-        cp(c1, iw("c1n"))
-        for s in range(3):
-            base = 3072 * s
-            cp(ap("N16"), ind(ap("pf"), ap("c16n" if s == 0 else "c16_%d" % (s - 1))))
-            if s == 2:
-                ts(kk2, iw("mi1"), 12, A.arith_shift_right, 15, A.bitwise_and)
-                cp(ap("kb"), kk2)
-            for k in range(16):
-                o, f = ap("FX", (k, 16 * nb, 16)), ap(fname, 0, nb)
-                if k < KS:
-                    act(o, f, AF.Copy)
-                else:
-                    cp(o, f)
-            for (j0, j1) in cb:
-                act(ap("GC", 256 * (j0 - NV), 256 * (j1 - NV)), ind(ap("rtb"), ap("N16", 16 * j0, 16 * j1)), AF.Copy)
-
-            def pc(j0, j1, k):
-                return ap("psC", j0 - NV, j1 - NV, third=(16 * k, 16 * k + 16))
-            for (j0, j1) in cb:
-                mm(ap("psC", j0 - NV, j1 - NV), ap("Ib"), ap("zt"), True, False)
-                for k in range(16):
-                    mm(pc(j0, j1, k), ap("nI"), ap(fname, 16 * j0, 16 * j1), False, False)
-            for (j0, j1) in cb:
-                for k in range(16):
-                    mm(pc(j0, j1, k), ap("Ib"), ap("GC", (256 * (j0 - NV) + k, 256 * (j1 - NV), 16)), False, k == 15)
-            for (j0, j1) in vb:
-                tt(ap("dall", base + 256 * j0, base + 256 * j1), ind(ap("rtb"), ap("N16", 16 * j0, 16 * j1)), ap("FX", 256 * j0, 256 * j1), sub)
-
-            def absv(b):
-                for j in range(*vb[b]):
-                    act(ap("D3", j), ap("dall", base + 256 * j, base + 256 * j + 256), AF.Abs)
-
-            def absc(b):
-                for j in range(*cb[b]):
-                    act(ap("dall", base + 256 * j, base + 256 * j + 256), ap("psC", j - NV), AF.Abs)
-
-            def key(j0, j1):
-                o = ap("key", 16 * j0, 16 * j1)
-                mm(o, ap("I32"), ap(K1, 16 * j0, 16 * j1), True, False)
-                for i in range(16):
-                    if j0 < NV:
-                        r = ap("D3", j0, j1, third=(16 * i, 16 * i + 16))
-                    else:
-                        r = ap("dall", (base + 256 * j0 + i, base + 256 * j1, 16))
-                    mm(o, blk("W65", i), r, False, i == 15)
-            if s == 2:
-                for i in range(16):
-                    mm(ap("Wp", (i, 192, 16)), blk("Vi", i), ap("kb"), True, True)
-            absv(0)
-            absc(0)
-            absv(1)
-            absc(1)
-            absv(2)
-            absv(3)
-            key(0, 4)
-            key(NV, 12)
-            key(4, NV)
-
-            if s == 0:
-                if t == 0:
-                    late()
-                else:
-                    tt(fw("x"), kk2, ap("kk3"), eq)
-                    tt(fw("xa"), fw("x"), o2, mul)
-                    tt(fw("xb"), o2, fw("xa"), sub)
-                    tt(fw("xc"), fw("xb"), fw("T", 72, 0, 12), sub)
-                    tt(ap("o3b"), fw("xc"), fw("T", 72, 36, 48), sub)
-                    mm(ap("mis", 0, 12), ap("onesb"), ap("o3b"), True, True)
-                    emit("v", [ap("mis", 0, 12)], [Zn], lambda: g.vector.tensor_reduce(Zn[0], ap("mis", 0, 12)[0], X, add))
-                    tt(Zc, Zc, Zn, add)
-                for i in range(16):
-                    mm(ap("mis", 128, 140), blk("W65", i), ap(fname, (i, 192, 16)), i == 0, i == 15)
-                ts(iw("d0z"), ap("mis", 128, 140), 2.0 ** -16, mul, Zc, add)
-            if s == 1:
-                ts(kk1, iw("mi0"), 12, A.arith_shift_right, 15, A.bitwise_and)
-                ts(iw("d1"), iw("mi0"), 16, A.arith_shift_right)
-                tt(fw("Ly"), fw("POS1"), fw("L0"), sub)
-                tt(o1, kk1, p1, A.not_equal)
-                tt(iw("x1"), iw("d1"), iw("d0z"), add)
-                ts(fw("V1a"), kk1, 8192.0, mul)
-                ts(iw("d1z"), iw("d1"), Zc, add)
-                tt(fw("Lya"), fw("Ly"), o1, mul)
-                ts(odd1, iw("x1"), 1, A.bitwise_and)
-                tt(V1, fw("V1a"), c1, add)
-                ts(fw("q"), o1, -16.0, mul, 16.0, add)
-                tt(fw("Lb1"), fw("Lya"), fw("L0"), add)
-                ts(ev1, odd1, -1.0, mul, 1.0, add)
-                tt(fw("VA1"), V1, dA, sub)
-                tt(fw("p1x"), fw("q"), p1, add)
-                tt(fw("k1x"), fw("q"), kk1, add)
-                ts(fw("G", 72, 0, 24), Y1, 8192.0, mul)
-                tt(SAa, V1, ev1, mul)
-                tt(SAb, fw("VA1"), odd1, mul)
-                if t + 1 < VI:
-                    prep(t + 1)
-            if s == 2:
-                ts(iw("d2"), iw("mi1"), 16, A.arith_shift_right)
-                tt(T21, kk2, fw("p1x"), eq)
-                tt(fw("e22"), kk2, fw("k1x"), eq)
-                ts(fw("V2a"), kk2, 8192.0, mul)
-                tt(iw("x2"), iw("d2"), iw("d1z"), add)
-                tt(fw("o2a"), o1, T21, sub)
-                tt(V2, fw("V2a"), c2, add)
-                ts(odd2, iw("x2"), 1, A.bitwise_and)
-                tt(o2, fw("o2a"), fw("e22"), sub)
-                tt(fw("Lu"), fw("POS2"), fw("L1"), sub)
-                ts(ap("EQ", 384, 576), ap("Wp", 0, 192), kp, eq, 8192.0, mul)
-                ts(ev2, odd2, -1.0, mul, 1.0, add)
-                ts(fw("qb"), o2, -16.0, mul, 16.0, add)
-                tt(C(24, 36), V2, dB, sub)
-                tt(fw("Lv"), fw("Lu"), o2, mul)
-                tt(ap("P24", 0, 12), fw("qb"), p1, add)
-                tt(ap("P24", 12, 24), fw("qb"), kk1, add)
-                tt(ap("Bv", 384, 576), ind(ap("pf"), ap("c16_0")), ap("EQ", 384, 576), sub)
-                cp(ap("P"), ind(ap("P24"), ap("rp", 0, 5)))
-                tt(fw("Lb"), fw("Lv"), fw("L1"), add)
-                tt(iw("CC", 24, 12, 24), c3, dA, sub)
-                tt(fw("eV"), V2, ev2, mul)
-                tt(fw("x3"), V2, odd1, mul)
-                tt(fw("x4"), C(24, 36), ev1, mul)
-                tt(fw("CA", 24), Y1, CC, mul)
-                tt(fw("CB", 24), Y2, CC, mul)
-                tt(C(60, 72), C(24, 36), odd2, mul)
-                ts(fw("G", 72, 36, 60), Y2, 8192.0, mul)
-                tt(fw("x5"), fw("x3"), SAa, add)
-                tt(fw("X36", 36, 12, 24), SAb, T21, mul)
-                tt(fw("X36", 36, 24, 36), fw("x4"), T21, mul)
-                tt(C(0, 24), fw("CA", 24), SA, add)
-                tt(C(36, 48), fw("CB", 24, 0, 12), fw("eV"), add)
-                tt(fw("X36", 36, 0, 12), fw("x5"), T21, mul)
-                cp(C(48, 60), fw("CB", 24, 12, 24))
-                tt(fw("BX", 36), fw("X36", 36), fw("D36", 36), add)
-
-            kr = ap("key", 0, 192)
-            emit("v", [ap("rst"), kr], [ap("run")], lambda: g.vector.tensor_tensor_scan(ap("run")[0], ap("rst")[0], kr[0], 0.0, A.max, A.min))
-            mn, kn = "mi%d" % s, "kL%d" % s
-            mi, kL = iw(mn), iw(kn)
-            cp(mi, ap("run", (15, 192, 16)))
+        def least(s, b):
+            kr, run, mi = pb(b, 0, NC), ap("run%d" % b), ap("mi", NJ * b, NJ * b + NJ)
+            vector(run, [kr, ap("rst")], 1, lambda: g.vector.tensor_tensor_scan(run[0], ap("rst")[0], kr[0], 0.0, A.max, A.min))
+            cp(mi, ap("run%d" % b, (15, NC, 16)))
+            kn, Ln = "k%d" % (s + 1), "L%d" % (s + 1)
+            ts(k(kn, None, b), mi, 12, A.arith_shift_right, 15, A.bitwise_and)
             if s < 2:
-                ts(c2 if s == 0 else c3, mi, 4095, A.bitwise_and)
-            ts(iw(kn, 12, 0, NV), iw(mn, 12, 0, NV), 12, A.arith_shift_right, 15, A.bitwise_and)
-            ts(iw(kn, 12, NV, 12), iw(mn, 12, NV, 12), 8, A.arith_shift_right, 240, A.bitwise_and)
+                ts(k("c%d" % (s + 2), None, b), mi, 4095, A.bitwise_and)
+            tt(k(Ln, None, b), k(kn, None, b), w(("POS", "PO2", "PO3")[s], None, b), add)
             if s < 2:
-                cp(ap("c16_%d" % s), c2 if s == 0 else c3)
-                if s == 1:
-                    tt(iw("kLo"), kL, o1, mul)
-                    kL = iw("kLo")
-                tt(fw("L%d" % s), kL, fw("POS0" if s == 0 else "Lb1"), add)
-                cp(ap("L16"), fw("L%d" % s))
-                fname = "fa" if s == 0 else "fb"
-                act(ap(fname), ind(ap("dall", 0, base + 3072), ap("L16")), AF.Abs)
+                cp(ap("CL%d" % (s + 1), 12 * b, 12 * b + 12), k("c%d" % (s + 2), Ln, b))
+                L, r = ap("CL%d" % (s + 1), 12 * b + NJ, 12 * b + 12), ap("RS", 192 * b + NC * s, 192 * b + NC * s + NC)
             else:
-                tt(fw("Lz"), kL, o2, mul)
-                ts(ap("kk3"), mi, 12, A.arith_shift_right, 15, A.bitwise_and)
-                tt(fw("Lw"), fw("Lz"), fw("Lb"), add)
-                cp(ap("K"), ind(ap("kk3"), ap("rk", 0, 5)))
-                cp(ap("L16"), fw("Lw"))
-                fo = ap("fo%d" % t)
-                act(fo, ind(ap("dall"), ap("L16")), AF.Abs)
-        if t + 1 < VI:
-            send(T.cores[(rank + 1) % N], T["fin%d" % (t + 1)][:], fo, "fa%d" % (t + 1))
-        else:
-            dma("y", "dyf", T.yf[:], fo[0], [fo], [])
+                L, r = ap("L3", NJ * b, NJ * b + NJ), ap("R3", NC * b, NC * b + NC)
+                cp(L, k(Ln, None, b))
+            act(r, ind(ap("GC%d%d" % (b, (t + s) % 2)), L), AF.Copy)
+            if s == 2 and last:
+                mm(pb(b, 128, 128 + NC), facts[b], ap("nI", 0, NC, NC), True, False)
+                mm(pb(b, 128, 128 + NC), ap("Ib"), r, False, True)
+                act(ap("yfs", NC * b, NC * b + NC), pb(b, 128, 128 + NC), AF.Abs)
+                return
+            mm(pb(b, 128, 256, NC), ap("nI", 0, NC, NC), facts[b], True, False)
+            mm(pb(b, 128, 256, NC), r, ap("Ib"), False, True)
+            facts[b] = ft("fw", 2 * s + b) if s < 2 else ft("fo", 2 * t + b)
+            act(facts[b], pb(b, 128, 256, NC), AF.Abs)
+            if s == 2:
+                n = 2 * t + b
+                send(ring(1), ring(-1), ap("fin", 128 * n, 128 * n + 128), ap("fo", 128 * n, 128 * n + 128), "fa%d" % n)
 
-        tt(fw("T", 72), ap("K", 0, 72), ap("P", 0, 72), eq)
-        tt(fw("H", 72), ap("K", 0, 72), fw("G", 72), mul)
-        tt(fw("Ha", 72), fw("H", 72), fw("C", 72), add)
-        tt(fw("Hb", 72), fw("Ha", 72), fw("T", 72), mul)
-        tt(fw("Hc", 36), fw("Hb", 72, 0, 36), fw("Hb", 72, 36, 72), add)
-        tt(iw("sel", 36), fw("Hc", 36), fw("BX", 36), add)
-        ts(ap("sk"), iw("sel", 36), 13, A.arith_shift_right)
-        ts(iw("sc", 36), iw("sel", 36), 8191, A.bitwise_and)
-        tt(ap("R"), ind(ap("sk"), ap("exo")), ap("DIAG"), mul)
-        mm(ap("U", 512, 704), ap("BDb"), ap("R"), True, True)
-        cp(ap("cl16"), iw("sc", 36))
-        cp(ap("kA"), ap("sk", 12, 24))
-        for i in range(16):
-            mm(ap("U", (i, 192, 16)), blk("Vi", i), ap("kA"), True, True)
-        ts(ap("EQ", 0, 192), ap("U", 512, 704), kp, eq, 8192.0, mul)
-        tt(ap("Bv", 0, 192), ind(ap("pf"), ap("cl16", 0, 12)), ap("EQ", 0, 192), sub)
-        ts(ap("Qs"), ap("Bv", 0, 192), 0.0, A.min)
-        mm(ap("Wp", 0, 192), ap("BD32"), ap("Qs"), True, False)
-        mm(ap("Wp", 0, 192), ap("Ib"), ap("EQ", 384, 576), False, True)
-        ts(ap("EQ", 192, 384), ap("U", 0, 192), kp, eq, 8192.0, mul)
-        mm(ap("U", 192, 384), ap("BD32"), ap("Qs"), True, False)
-        mm(ap("U", 192, 384), ap("Ib"), ap("EQ", 192, 384), False, True)
-        tt(ap("Bv", 192, 384), ind(ap("pf"), ap("cl16", 12, 24)), ap("EQ", 192, 384), sub)
-        tt(ap("newv", 192, 384), ap("Bv", 384, 576), ap("Wp", 0, 192), A.max)
-        tt(ap("newv", 0, 192), ap("Bv", 192, 384), ap("U", 192, 384), A.max)
-        pfo = ind(ap("pf"), ap("cl16", 12, 36))
-        emit("v", [ap("newv"), ap("cl16", 12, 36)], [ap("pf")], lambda: g.vector.tensor_copy(pfo[0], ap("newv")[0]))
+        def book1():
+            tt(w("o1"), k("k1"), k("p1"), A.not_equal)
+            tt(w("PO2"), w("POS"), w("o1"), mul)
+            if not last:
+                cp(seg(KN, SEG, "c1", "p1", None), ap("pkg%d" % (t + 1), 192, 216))
+                cp(ap("CL0"), seg(KN, SEG, "c1", None, None))
+
+        def book2():
+            X1, X2, X3a, X3b = k("c1", "k1"), k("c2", "k2"), k("c3", "p1"), k("c3", "k1")
+            for i in range(16):
+                mm(pb(1, 448, 472), blk("Wz", i), ap("RS", (i, 384, 16)), i == 0, i == 15)
+            ts(ap("yi"), pb(1, 448, 472), 2.0 ** -16, mul, Zc, add)
+            tt(w("ne"), k("k2"), k("k1"), A.not_equal)
+            tt(w("T"), k("k2"), k("p1"), eq)
+            tt(w("Tb"), k("k2"), k("p1"), eq)
+            tt(w("oa"), w("o1"), w("ne"), mul)
+            tt(w("da", "db"), X3a, X1, sub)
+            tt(ap("O2"), w("oa"), w("T"), A.is_gt)
+            ts(w("y1", "y2"), ap("yi"), 1, A.bitwise_and)
+            ts(w("y1b", "y2b"), ap("yi"), 1, A.bitwise_and)
+            tt(w("ea", "eb"), X2, X1, sub)
+            tt(w("PO3"), w("POS"), ap("O2"), mul)
+            tt(nd("W4", (0, 2, 1), (5, 8, 1), (0, NJ, 1)), nd(KC, (0, 2, 1), (3, 6, 1), (0, NJ, 1)), pos, add)
+            tt(w("fa", "fb"), X3b, X2, sub)
+            tt(ab(0, 12), w("y1", "y1b"), w("da", "db"), mul)
+            tt(w("ga", "gb"), w("y1", "y1b"), w("ea", "eb"), mul)
+            tt(w("ha", "hb"), w("y2", "y2b"), w("fa", "fb"), mul)
+            ts(w("qa", "qb"), w("T", "Tb"), -16.0, mul, 16.0, add)
+            tt(ab(12, 24), w("da", "db"), ab(0, 12), sub)
+            tt(w("ma", "mb"), w("ga", "gb"), w("T", "Tb"), mul)
+            tt(ab(30, 42), w("ha", "hb"), w("ea", "eb"), add)
+            tt(bs(18, 30), k("k1", "k2"), w("qa", "qb"), add)
+            ts(ab(18, 24), ab(18, 24), -16.0, add)
+            tt(bs(0, 12), X1, w("ma", "mb"), add)
+            cp(ab(42, 48), w("da"))
+            cp(bs(12, 18), k("c1"))
+
+        def close(b):
+            def sl(lo, hi):
+                return ap("SL", 32 * b + lo, 32 * b + hi)
+            e, h, o, q = 16 * b, 64 * b, 192 * b, ap("Q", NC * b, NC * b + NC)
+            tt(ap("E", e, e + 6), k("L3", None, b), w("P1", None, b), eq)
+            tt(ap("E", e + 6, e + 12), k("L3", None, b), w("P2", None, b), eq)
+            tt(ap("H", h, h + 64), ind(ap("E", e, e + 12), ap("rep")), nd("AB", (b, b + 1, 1), (0, 64, 1)), mul)
+            if not last:
+                tt(ap("E3", NJ * b, NJ * b + NJ), k("L3", None, b), w("P3", None, b), eq)
+            tt(ap("S1", 32 * b, 32 * b + 30), ap("H", h, h + 30), ap("H", h + 30, h + 60), add)
+            tt(ap("S2", 32 * b, 32 * b + 30), ap("S1", 32 * b, 32 * b + 30), nd("BS", (b, b + 1, 1), (0, 30, 1)), add)
+            cp(sl(0, 30), ap("S2", 32 * b, 32 * b + 30))
+            act(ap("EQD", NC * b, NC * b + NC), ind(ap("tab"), sl(6, 12)), AF.Copy)
+            act(ap("EQ", o, o + 192), ind(ap("tab"), sl(18, 30)), AF.Copy, M)
+            tt(q, ind(ap("pf"), sl(0, 6)), ap("EQD", NC * b, NC * b + NC), mul)
+            mm(pb(b, 256, 448), ap("Ib"), ap("nM"), True, False)
+            mm(pb(b, 256, 352), ap("BD32"), q, False, False)
+            mm(pb(b, 352, 448), ap("BD32"), q, False, False)
+            mm(pb(b, 256, 448), ap("Ib"), ap("EQ", o, o + 192), False, True)
+            tt(ap("Bv", o, o + NC), ind(ap("pf"), sl(12, 18)), ap("EQ", o, o + NC), sub)
+            tt(ap("Bv", o + NC, o + 192), ind(ap("pf"), court(1, b)), ap("EQ", o + NC, o + 192), sub)
+            tt(ap("newv", o, o + 192), ap("Bv", o, o + 192), pb(b, 256, 448), A.max)
+            scatter(ap("pf"), sl(12, 18), ap("newv", o, o + NC))
+            scatter(ap("pf"), court(1, b), ap("newv", o + NC, o + 192))
+
+        def count():
+            z = pb(1, 472, 484)
+            for n, r in enumerate((ap("O2"), ap("E3"), ap("E", 0, 12), ap("E", 16, 28))):
+                mm(z, ap("onesb", 0, 128), r, n == 0, n == 3)
+            vector(Zn, [z], 1, lambda: g.vector.tensor_reduce(Zn[0], z[0], X, add))
+            tt(Zc, Zc, Zn, add)
+
+        for s in range(3):
+            for b in range(2):
+                if s:
+                    least(s - 1, b)
+                if (s, b) == (1, 1):
+                    book1()
+                    if t:
+                        count()
+                if (s, b) == (2, 1):
+                    book2()
+                keys(s, b)
+        for b in range(2):
+            least(2, b)
+            close(b)
+
+    for t in range(VI):
+        visit(t)
+    dma("y", "dyf", T.yf[:], ap("yfs")[0], [ap("yfs")], [])
 
     for q in range(4):
-        o, u = 512 * q, 512 * (q % 2)
-        ts(ap("U", u, u + 512), ap("pf", 2048 + o, 2560 + o), 4096.0, mul)
-        tt(ap("yps", o, o + 512), ap("pf", o, o + 512), ap("U", u, u + 512), add)
+        o = 512 * q
+        ts(ap("sub", o, o + 512), ap("pf", 2048 + o, 2560 + o), 4096.0, mul)
+        tt(ap("yps", o, o + 512), ap("pf", o, o + 512), ap("sub", o, o + 512), add)
         dma("y", "dy%d" % q, T.yp[:, o:o + 512], ap("yps", o, o + 512)[0], [ap("yps", o, o + 512)], [])
-    for sem in SEMAPHORES:
-        if total.get(sem, 0) > know["g"].get(sem, 0):
-            g.wait_ge(T.sem[sem], total[sem])
+    issue(g, T, ops)

@@ -2,36 +2,44 @@ from concourse.mybir import dt, AluOpType, AxisListType, ActivationFunctionType
 
 N = 8
 VI = 4
-NJ, NC = 6, 96
-SG = [[32, 16], [32, 32], [32, 48]]
+NB = 3
+NJ, NC = 12 // NB, 192 // NB
+RK = (15 * NJ + 15) // 16
+RING = 8 - NB
+SG = [[32, 16, 0], [24, 24, 24], [24, 32, 32]]
 VC = 32
+OUT = [0, 256, 640, 1088, 1600, 2048]
 M = 8192.0
-CY, PE, GA, SC, WAKE, DL, RL, BW = 0.92, 0.46, 1.56, 3.8, 100, 2000, 3000, 250
+CY, PE, GA, SC, WAKE, DL, RL, BW = 0.87, 0.46, 1.56, 3.8, 180, 2000, 3000, 250
 F32, BF, I32T, U16 = "float32", "bfloat16", "int32", "uint16"
 SIZES = {
     F32: "pkg0 216 pkg1 216 pkg2 216 pkg3 216 ones32 128 I32 128 BD32 128 Wz32 144 cols 8 KU 224 TA 416 "
-         "OH 192 Q0 192 rst 96 run0 96 run1 96 tab 32 Q 192 Bv 384 yps 2048 H 128 S1 64 S2 64",
-    BF: "rtb 4096 fxs 192 fin 768 fo 768 fw 768 yfs 192 onesb 144 Ib 128 nI 128 Wz 144 En 1536 nM 192 "
-        "GC00 1552 GC01 1552 GC10 1552 GC11 1552 RS 384 R3 192 EQD 192 EQ 384 E 32 E3 12 O2 12",
-    I32T: "pks 2048 pf 4096 jcs 192 pidx 4 tl 36 i32 32 mi 12 m0 12 r4 12 yi 24 newv 384",
-    U16: "rep 4 TL 12 N16 192 CL0 12 CL1 24 CL2 24 L3 12 SL 64",
+         "OH 192 Q0 192 rst 96 K3 96 tri 96 tab 32 Q 192 Bv 384 yps 2048 H 288 S 288",
+    BF: "rtb 4096 fxs 192 fin 1152 fo 1152 fw 1152 yfs 192 onesb 144 Ib 128 nI 128 Wz 144 En 1536 nM 192 "
+        "RS 384 R3 192 EQD 192 EQ 384 E 96 E3 12 O2 12",
+    I32T: "pks 2048 pf 4096 jcs 192 pidx 4 tl 36 i32 32 run 192 m0 12 r4 24 yi 24 newv 384",
+    U16: "rep 6 TL 12 N16 192 CL0 12 CL1 24 CL2 24 L3 12 SL 96",
 }
-SEG = "c1 c2 c3 p1 k1 k2 k3 L1 L2 L3".split()
-WSEG = "POS POSb POSc PO2 PO3 P1 P2 P3 o1 oa ne T Tb da db ea eb fa fb ga gb ha hb ma mb qa qb".split()
+SEG = "c1 c2 c3 p1 k1 k2 L1 L2 L3 Lm".split()
+WSEG = "POS PO2 PO3 P1 P2 P3 o1 oa ne T Tb da db ea eb fa fb ga gb ha hb ma mb qa qb".split()
 YSEG = "y1 y1b y2 y2b".split()
 SCRATCH = {
     "sr8": ("sbuf", [8, 192], I32T), "srb": ("sbuf", [8, 192], BF), "Sel": ("sbuf", [8, 128], BF),
-    "D0": ("sbuf", [128, NJ, 256], BF), "D1": ("sbuf", [128, NJ, 256], BF),
-    "KC0": ("sbuf", [128, 2, len(SEG), NJ], I32T), "KC1": ("sbuf", [128, 2, len(SEG), NJ], I32T),
-    "W4": ("sbuf", [128, 2, len(WSEG), NJ], F32), "Y4": ("sbuf", [128, 2, len(YSEG), NJ], I32T),
-    "AB": ("sbuf", [128, 2, 64], F32), "BS": ("sbuf", [128, 2, 32], F32),
-    "sub": ("psum", [128, 3072], F32), "pb0": ("psum", [128, 512], F32), "pb1": ("psum", [128, 512], F32),
+    "KC0": ("sbuf", [128, NB, len(SEG), NJ], I32T), "KC1": ("sbuf", [128, NB, len(SEG), NJ], I32T),
+    "W4": ("sbuf", [128, NB, len(WSEG), NJ], F32), "Y4": ("sbuf", [128, NB, len(YSEG), NJ], I32T),
+    "AB": ("sbuf", [128, NB, 16 * RK], F32), "sub": ("psum", [128, 512 * RING], F32),
 }
+for _b in range(NB):
+    SCRATCH["pb%d" % _b] = ("psum", [128, 512], F32)
+    SCRATCH["D%d" % _b] = ("sbuf", [128, NJ, 256], BF)
+    for _h in range(2):
+        SCRATCH["GC%d%d" % (_b, _h)] = ("sbuf", [128, 16 + 16 * NC], BF)
 for _ty in SIZES:
     _l = SIZES[_ty].split()
     for _i in range(0, len(_l), 2):
         SCRATCH[_l[_i]] = ("sbuf", [128, int(_l[_i + 1])], _ty)
-SEMAPHORES = "cv cs ct cg ls pk1 pk2 pk3 fa0 fa1 fa2 fa3 fa4 fa5 dj ds df dp0 dp1 dp2 dp3 dr dyf dy0 dy1 dy2 dy3".split()
+SEMAPHORES = ("cv cs ct cg ls pk1 pk2 pk3 dj ds df dp0 dp1 dp2 dp3 dr dyf".split() + ["fa%d" % _n for _n in range(3 * NB)]
+              + ["dy%d" % _n for _n in range(len(OUT) - 1)])
 WIDTH = {F32: 4, BF: 2, I32T: 4, U16: 2}
 
 
@@ -56,7 +64,7 @@ def issue(g, T, ops):
     fore, back = [[] for _ in ops], [[] for _ in ops]
     for n, o in enumerate(ops):
         for p in o["dep"] + o["soft"]:
-            gap = ops[p]["lat"] + (0 if p in o["soft"] else WAKE)
+            gap = 0 if p in o["soft"] else ops[p]["lat"] + WAKE
             fore[n].append((p, ops[p]["cost"] + gap))
             back[p].append((n, o["cost"] + gap))
     start = place(ops, fore, [(n, n) for n in range(len(ops))])
@@ -91,7 +99,7 @@ def rank_program(g, core, T, topo):
         return
     A, AF, X = AluOpType, ActivationFunctionType, AxisListType.X
     add, sub, mul, eq = A.add, A.subtract, A.mult, A.is_equal
-    ops, wrote, read, sent, loaded = [], {}, {}, {}, [0, None]
+    ops, wrote, read, turn, loaded = [], {}, {}, [0], [0, None]
 
     def ap(name, a=None, b=None, P=None):
         shape = SCRATCH[name][1]
@@ -104,9 +112,9 @@ def rank_program(g, core, T, topo):
         runs = [0]
         for d, (lo, hi, st) in enumerate(ix[:-1]):
             runs = [(r + i) * shape[d + 2] for r in runs for i in range(lo, hi, st)]
-        lo, hi, _ = ix[-1]
+        lo, hi, st = ix[-1]
         view = T[name][(slice(0, 128),) + tuple(l if h == l + 1 else slice(l, h, s) for l, h, s in ix)]
-        return (view, [(name, r + lo, r + hi, 1) for r in runs])
+        return (view, [(name, r + lo, r + hi, st) for r in runs])
 
     def ind(win, off):
         return (win[0].indirect(off[0]), win[1] + off[1], True)
@@ -148,11 +156,11 @@ def rank_program(g, core, T, topo):
     def load(q, sem, buf, x):
         dma(q, sem, buf[0], x, [], [buf])
 
-    def send(dst, src_core, dst_ap, src, rsem):
+    def send(dst, src_core, dst_ap, src, rsem, lat=RL):
         rid, pid, _ = topo.addr(dst)
         me = record("g", [src], [], lambda: g.remote_dma(dst_ap[0], src[0], T.sem[rsem], T.sem["ls"], pid, rid, topo.mask(core, dst)),
                     300, "ls", len(topo.engines(core, dst)))
-        record(None, [], [dst_ap], None, 0, rsem, len(topo.engines(src_core, core)), RL, [me])
+        record(None, [], [dst_ap], None, 0, rsem, len(topo.engines(src_core, core)), lat, [me])
 
     def vector(out, ins, per, call, more=()):
         if len(ins) and len(ins[0]) == 3:
@@ -174,6 +182,9 @@ def rank_program(g, core, T, topo):
 
     def cp(out, a):
         vector(out, [a], 1, lambda: g.vector.tensor_copy(out[0], a[0]))
+
+    def scan(out, a, b, op0, op1):
+        vector(out, [a, b], 1, lambda: g.vector.tensor_tensor_scan(out[0], a[0], b[0], 0.0, op0, op1))
 
     def scatter(win, off, a):
         o = ind(win, off)
@@ -198,7 +209,7 @@ def rank_program(g, core, T, topo):
     def seg(buf, names, a, c, b):
         i = names.index(a)
         j = i if c is None else names.index(c)
-        return nd(buf, (0, 2, 1) if b is None else (b, b + 1, 1), (i, j + 1, max(j - i, 1)), (0, NJ, 1))
+        return nd(buf, (0, NB, 1) if b is None else (b, b + 1, 1), (i, j + 1, max(j - i, 1)), (0, NJ, 1))
 
     def w(a, c=None, b=None):
         return seg("Y4", YSEG, a, c, b) if a in YSEG else seg("W4", WSEG, a, c, b)
@@ -212,11 +223,8 @@ def rank_program(g, core, T, topo):
     def ft(name, n):
         return ap(name, 128 * n, 128 * n + 128, NC)
 
-    def ab(lo, hi):
-        return nd("AB", (0, 2, 1), (lo, hi, 1))
-
-    def bs(lo, hi):
-        return nd("BS", (0, 2, 1), (lo, hi, 1))
+    def ab(r, lo, hi):
+        return nd("AB", (0, NB, 1), (3 * NJ * lo + r, 3 * NJ * hi, 3))
 
     def ring(d):
         return T.cores[(rank + d) % N]
@@ -229,7 +237,6 @@ def rank_program(g, core, T, topo):
     load("y", "dr", ap("rtb"), T.rt[:])
 
     kp, kp4096, kp16, par, Zc, Zn = [ap("cols", c, c + 1) for c in range(6)]
-    pos = nd("W4", (0, 2, 1), (0, 3, 1), (0, NJ, 1))
     sel = ap("Sel")
     fill(ap("onesb"), 1.0)
     fill(ap("ones32"), 1.0)
@@ -239,10 +246,11 @@ def rank_program(g, core, T, topo):
     iota(ap("i32"), [[1, 32]], 0, 0)
     iota(ap("tl", 0, 12), [[0, 6], [1, 2]], 0, 0)
     asel(ap("I32"), ap("ones32"), [[-1, 128]], eq, 0, 1)
-    iota(pos, [[0, 6], [256, NJ]], 0, 0)
+    iota(w("POS"), [[0, NB], [256, NJ]], 0, 0)
+    iota(ap("K3", 0, NC), [[256, NJ], [4097, 16]], 0, 0)
     mm(pb(0, 0, 128), sel, sel, True, True)
-    fill(ap("En"), -1.0)
-    asel(ap("En"), ap("En"), [[1, NC], [0, 16]], eq, 0, -1)
+    fill(ap("En", 0, 16 * NC), -1.0)
+    asel(ap("En", 0, 16 * NC), ap("En", 0, 16 * NC), [[1, NC], [0, 16]], eq, 0, -1)
     ts(ap("pidx", 1, 2), ap("pidx", 0, 1), 15, A.bitwise_and)
     ts(ap("pidx", 2, 3), ap("pidx", 0, 1), 4, A.arith_shift_right, 1, A.bitwise_and)
     cp(kp, ap("pidx", 1, 2))
@@ -255,24 +263,29 @@ def rank_program(g, core, T, topo):
     act(ap("Wz"), ap("Wz32"), AF.Copy, 65536.0)
     act(ap("Ib"), ap("I32"), AF.Copy)
     act(ap("nI"), ap("I32"), AF.Copy, -1.0)
-    for b in range(2):
+    for b in range(NB):
         for h in range(2):
             fill(ap("GC%d%d" % (b, h), 0, 16), 0.0)
     fill(ap("rst"), 0.0)
     fill(ap("rst", (0, NC, 16)), 33554432.0)
-    ts(pos, pos, kp16, add)
+    fill(ap("tri"), 1.0)
+    fill(ap("tri", (0, 96, 3)), 0.0)
+    ts(w("POS"), w("POS"), kp16, add)
+    ts(ap("K3", 0, NC), ap("K3", 0, NC), kp16, add)
     fill(Zc, 0.0)
     ts(ap("tab"), ap("i32"), kp, eq)
     fill(ap("nM"), -M)
-    fill(ap("fo"), 0.0)
-    fill(ab(0, 64), -16.0)
-    n, q, u = ap("r4", 0, 4), ap("r4", 4, 8), ap("r4", 8, 12)
-    ts(n, ap("i32", (0, 16, 4)), 4.0, mul, kp, add)
-    ts(q, n, -2.5, add, 1.0 / 6, mul)
-    ts(u, n, 30.0, A.is_ge)
-    tt(q, q, u, sub)
-    ts(q, q, -6.0, mul)
-    tt(n, n, q, add)
+    fill(ap("fo", 0, 384 * NB), 0.0)
+    fill(ap("E"), 1.0)
+    fill(nd("AB", (0, NB, 1), (0, 16 * RK, 1)), -16.0)
+    n, a, q, u = [ap("r4", 6 * c, 6 * c + 6) for c in range(4)]
+    ts(n, ap("i32", 0, 6), 16.0, mul, kp, add)
+    ts(a, n, -1.0, add, 1.0 / 3, mul)
+    ts(q, a, (1 - NJ) / 2, add, 1.0 / NJ, mul)
+    ts(u, a, 1.0 - 3 * NJ, mul)
+    tt(n, n, q, sub)
+    ts(n, n, 1.0 * NJ, mul)
+    tt(n, n, u, add)
     cp(ap("rep"), n)
 
     fill(ap("KU", 0, 16), 0.0)
@@ -288,9 +301,9 @@ def rank_program(g, core, T, topo):
     ts(seg("KC0", SEG, "c1", None, None), ap("m0"), 4095, A.bitwise_and)
     ts(seg("KC0", SEG, "p1", None, None), ap("m0"), 12, A.arith_shift_right)
     cp(ap("CL0"), seg("KC0", SEG, "c1", None, None))
-    for b in range(2):
+    for b in range(NB):
         mm(pb(0, 128, 256, NC), ap("fxs", NC * b, NC * b + NC), ap("Ib"), True, True)
-        act(ft("fw", 4 + b), pb(0, 128, 256, NC), AF.Copy)
+        act(ft("fw", 2 * NB + b), pb(0, 128, 256, NC), AF.Copy)
     for o, a in ((ap("TA", 0, 192), ap("KU", 16, 208)), (ap("TA", 192, 416), ap("KU"))):
         vector(o, [a], 1, lambda o=o, a=a: g.vector.transpose(o[0], a[0]))
     ts(ap("tl", 12, 24), ap("tl", 0, 12), par, A.not_equal, 208.0, mul)
@@ -300,56 +313,57 @@ def rank_program(g, core, T, topo):
     act(ap("pkg0", 0, 192), ind(ap("TA"), ap("TL")), AF.Copy)
     cp(ap("pkg0", 192, 216), seg("KC0", SEG, "c1", "p1", None))
     for t in range(1, VI):
-        send(ring(t), ring(-t), ap("pkg%d" % t), ap("pkg0"), "pk%d" % t)
+        send(ring(t), ring(-t), ap("pkg%d" % t), ap("pkg0"), "pk%d" % t, 4 * RL)
     for h in range(0, 2048, 512):
         ts(ap("pf", h, h + 512), ap("pks", h, h + 512), 4095, A.bitwise_and)
         ts(ap("pf", 2048 + h, 2560 + h), ap("pks", h, h + 512), 12, A.arith_shift_right)
 
     def visit(t):
         KC, KN, last = "KC%d" % (t % 2), "KC%d" % ((t + 1) % 2), t + 1 == VI
-        facts = [ft("fw", 4 + b) if t == 0 else ft("fin", 2 * (t - 1) + b) for b in range(2)]
+        facts = [ft("fw", 2 * NB + b) if t == 0 else ft("fin", NB * (t - 1) + b) for b in range(NB)]
 
         def k(a, c=None, b=None):
             return seg(KC, SEG, a, c, b)
 
         def court(s, b):
-            return ap("CL0", NJ * b, NJ * b + NJ) if s == 0 else ap("CL%d" % s, 12 * b, 12 * b + NJ)
+            return ap("CL0", NJ * b, NJ * b + NJ) if s == 0 else ap("CL%d" % s, 2 * NJ * b, 2 * NJ * b + NJ)
 
         def keys(s, b):
             gc, D = "GC%d%d" % (b, (t + s) % 2), "D%d" % b
             cp(ap("N16", NC * b, NC * b + NC), ind(ap("pf"), court(s, b)))
             nv = NC - SG[s][b]
-            cut = list(range(0, nv, VC)) + [nv] + [x for x in (32, 64) if x > nv] + [NC]
+            cut = list(range(0, nv, VC)) + [nv] + [x for x in range(32, NC, 32) if x > nv] + [NC]
             for x0, x1 in zip(cut, cut[1:]):
                 o, a = ap(gc, 16 + 16 * x0, 16 + 16 * x1), ind(ap("rtb"), ap("N16", NC * b + x0, NC * b + x1))
                 if x0 < nv:
                     cp(o, a)
                 elif x0 < x1:
                     act(o, a, AF.Copy)
-            for c in range(3):
-                bank = ap("sub", 1536 * b + 512 * c, 1536 * b + 512 * c + 512)
+            for c in range(NJ // 2):
+                bank = ap("sub", 512 * turn[0], 512 * turn[0] + 512)
+                turn[0] = (turn[0] + 1) % RING
                 mm(bank, facts[b], ap("En", 512 * c, 512 * c + 512, NC), True, False)
                 mm(bank, ap("Ib"), ap(gc, 16 + 512 * c, 528 + 512 * c), False, True)
                 act(nd(D, (2 * c, 2 * c + 2, 1), (0, 256, 1)), bank, AF.Abs)
-            mm(pb(b, 0, NC), ap("I32"), ap("pkg%d" % t, NC * b, NC * b + NC), True, False)
+            mm(pb(b, 0, NC), ap("I32"), ap("pkg%d" % t, NC * b, NC * b + NC) if s < 2 else ap("K3", 0, NC), True, False)
             for i in range(16):
                 mm(pb(b, 0, NC), blk("Wz", i), nd(D, (0, NJ, 1), (16 * i, 16 * i + 16, 1)), False, i == 15)
 
         def least(s, b):
-            kr, run, mi = pb(b, 0, NC), ap("run%d" % b), ap("mi", NJ * b, NJ * b + NJ)
-            vector(run, [kr, ap("rst")], 1, lambda: g.vector.tensor_tensor_scan(run[0], ap("rst")[0], kr[0], 0.0, A.max, A.min))
-            cp(mi, ap("run%d" % b, (15, NC, 16)))
-            kn, Ln = "k%d" % (s + 1), "L%d" % (s + 1)
-            ts(k(kn, None, b), mi, 12, A.arith_shift_right, 15, A.bitwise_and)
+            mi = ap("run", (NC * b + 15, NC * b + NC, 16))
+            scan(ap("run", NC * b, NC * b + NC), ap("rst", 0, NC), pb(b, 0, NC), A.max, A.min)
             if s < 2:
-                ts(k("c%d" % (s + 2), None, b), mi, 4095, A.bitwise_and)
-            tt(k(Ln, None, b), k(kn, None, b), w(("POS", "PO2", "PO3")[s], None, b), add)
-            if s < 2:
-                cp(ap("CL%d" % (s + 1), 12 * b, 12 * b + 12), k("c%d" % (s + 2), Ln, b))
-                L, r = ap("CL%d" % (s + 1), 12 * b + NJ, 12 * b + 12), ap("RS", 192 * b + NC * s, 192 * b + NC * s + NC)
+                kn, cn, Ln = [k(a % (s + c), None, b) for a, c in (("k%d", 1), ("c%d", 2), ("L%d", 1))]
+                L, r = ap("CL%d" % (s + 1), 2 * NJ * b + NJ, 2 * NJ * (b + 1)), ap("RS", NC * (2 * b + s), NC * (2 * b + s + 1))
+                ts(cn, mi, 4095, A.bitwise_and)
+                ts(kn, mi, 12, A.arith_shift_right, 15, A.bitwise_and)
+                cp(court(s + 1, b), cn)
+                tt(Ln, kn, w(("POS", "PO2")[s], None, b), add)
             else:
-                L, r = ap("L3", NJ * b, NJ * b + NJ), ap("R3", NC * b, NC * b + NC)
-                cp(L, k(Ln, None, b))
+                L, r, Ln = ap("L3", NJ * b, NJ * b + NJ), ap("R3", NC * b, NC * b + NC), k("Lm", None, b)
+                ts(k("L3", None, b), mi, 4095, A.bitwise_and)
+                tt(Ln, k("L3", None, b), ap("O2", NJ * b, NJ * b + NJ), mul)
+            cp(L, Ln)
             act(r, ind(ap("GC%d%d" % (b, (t + s) % 2)), L), AF.Copy)
             if s == 2 and last:
                 mm(pb(b, 128, 128 + NC), facts[b], ap("nI", 0, NC, NC), True, False)
@@ -358,10 +372,10 @@ def rank_program(g, core, T, topo):
                 return
             mm(pb(b, 128, 256, NC), ap("nI", 0, NC, NC), facts[b], True, False)
             mm(pb(b, 128, 256, NC), r, ap("Ib"), False, True)
-            facts[b] = ft("fw", 2 * s + b) if s < 2 else ft("fo", 2 * t + b)
+            facts[b] = ft("fw", NB * s + b) if s < 2 else ft("fo", NB * t + b)
             act(facts[b], pb(b, 128, 256, NC), AF.Abs)
             if s == 2:
-                n = 2 * t + b
+                n = NB * t + b
                 send(ring(1), ring(-1), ap("fin", 128 * n, 128 * n + 128), ap("fo", 128 * n, 128 * n + 128), "fa%d" % n)
 
         def book1():
@@ -374,8 +388,8 @@ def rank_program(g, core, T, topo):
         def book2():
             X1, X2, X3a, X3b = k("c1", "k1"), k("c2", "k2"), k("c3", "p1"), k("c3", "k1")
             for i in range(16):
-                mm(pb(1, 448, 472), blk("Wz", i), ap("RS", (i, 384, 16)), i == 0, i == 15)
-            ts(ap("yi"), pb(1, 448, 472), 2.0 ** -16, mul, Zc, add)
+                mm(pb(NB - 1, 448, 472), blk("Wz", i), ap("RS", (i, 384, 16)), i == 0, i == 15)
+            ts(ap("yi"), pb(NB - 1, 448, 472), 2.0 ** -16, mul, Zc, add)
             tt(w("ne"), k("k2"), k("k1"), A.not_equal)
             tt(w("T"), k("k2"), k("p1"), eq)
             tt(w("Tb"), k("k2"), k("p1"), eq)
@@ -386,65 +400,68 @@ def rank_program(g, core, T, topo):
             ts(w("y1b", "y2b"), ap("yi"), 1, A.bitwise_and)
             tt(w("ea", "eb"), X2, X1, sub)
             tt(w("PO3"), w("POS"), ap("O2"), mul)
-            tt(nd("W4", (0, 2, 1), (5, 8, 1), (0, NJ, 1)), nd(KC, (0, 2, 1), (3, 6, 1), (0, NJ, 1)), pos, add)
+            for a, c in (("P1", "p1"), ("P2", "k1"), ("P3", "k2")):
+                tt(w(a), k(c), w("PO3"), add)
             tt(w("fa", "fb"), X3b, X2, sub)
-            tt(ab(0, 12), w("y1", "y1b"), w("da", "db"), mul)
+            tt(ab(0, 0, 2), w("y1", "y1b"), w("da", "db"), mul)
             tt(w("ga", "gb"), w("y1", "y1b"), w("ea", "eb"), mul)
             tt(w("ha", "hb"), w("y2", "y2b"), w("fa", "fb"), mul)
             ts(w("qa", "qb"), w("T", "Tb"), -16.0, mul, 16.0, add)
-            tt(ab(12, 24), w("da", "db"), ab(0, 12), sub)
+            tt(ab(0, 2, 4), w("da", "db"), ab(0, 0, 2), sub)
             tt(w("ma", "mb"), w("ga", "gb"), w("T", "Tb"), mul)
-            tt(ab(30, 42), w("ha", "hb"), w("ea", "eb"), add)
-            tt(bs(18, 30), k("k1", "k2"), w("qa", "qb"), add)
-            ts(ab(18, 24), ab(18, 24), -16.0, add)
-            tt(bs(0, 12), X1, w("ma", "mb"), add)
-            cp(ab(42, 48), w("da"))
-            cp(bs(12, 18), k("c1"))
+            tt(ab(1, 0, 2), w("ha", "hb"), w("ea", "eb"), add)
+            tt(ab(2, 3, 5), k("k1", "k2"), w("qa", "qb"), add)
+            ts(ab(0, 3, 4), ab(0, 3, 4), -16.0, add)
+            tt(ab(2, 0, 2), X1, w("ma", "mb"), add)
+            cp(ab(1, 2, 3), w("da"))
+            cp(ab(2, 2, 3), k("c1"))
 
         def close(b):
             def sl(lo, hi):
-                return ap("SL", 32 * b + lo, 32 * b + hi)
-            e, h, o, q = 16 * b, 64 * b, 192 * b, ap("Q", NC * b, NC * b + NC)
-            tt(ap("E", e, e + 6), k("L3", None, b), w("P1", None, b), eq)
-            tt(ap("E", e + 6, e + 12), k("L3", None, b), w("P2", None, b), eq)
-            tt(ap("H", h, h + 64), ind(ap("E", e, e + 12), ap("rep")), nd("AB", (b, b + 1, 1), (0, 64, 1)), mul)
+                return ap("SL", 32 * b + NJ * lo, 32 * b + NJ * hi)
+            e, h, o, u, q = 32 * b, 96 * b, 2 * NC * b, 15 * NJ, ap("Q", NC * b, NC * b + NC)
+            tt(ap("E", e, e + NJ), k("L3", None, b), w("P1", None, b), eq)
+            tt(ap("E", e + NJ, e + 2 * NJ), k("L3", None, b), w("P2", None, b), eq)
+            tt(ap("H", h, h + 16 * RK), ind(ap("E", e, e + 3 * NJ), ap("rep", 0, RK)), nd("AB", (b, b + 1, 1), (0, 16 * RK, 1)), mul)
             if not last:
                 tt(ap("E3", NJ * b, NJ * b + NJ), k("L3", None, b), w("P3", None, b), eq)
-            tt(ap("S1", 32 * b, 32 * b + 30), ap("H", h, h + 30), ap("H", h + 30, h + 60), add)
-            tt(ap("S2", 32 * b, 32 * b + 30), ap("S1", 32 * b, 32 * b + 30), nd("BS", (b, b + 1, 1), (0, 30, 1)), add)
-            cp(sl(0, 30), ap("S2", 32 * b, 32 * b + 30))
-            act(ap("EQD", NC * b, NC * b + NC), ind(ap("tab"), sl(6, 12)), AF.Copy)
-            act(ap("EQ", o, o + 192), ind(ap("tab"), sl(18, 30)), AF.Copy, M)
-            tt(q, ind(ap("pf"), sl(0, 6)), ap("EQD", NC * b, NC * b + NC), mul)
-            mm(pb(b, 256, 448), ap("Ib"), ap("nM"), True, False)
-            mm(pb(b, 256, 352), ap("BD32"), q, False, False)
-            mm(pb(b, 352, 448), ap("BD32"), q, False, False)
-            mm(pb(b, 256, 448), ap("Ib"), ap("EQ", o, o + 192), False, True)
-            tt(ap("Bv", o, o + NC), ind(ap("pf"), sl(12, 18)), ap("EQ", o, o + NC), sub)
-            tt(ap("Bv", o + NC, o + 192), ind(ap("pf"), court(1, b)), ap("EQ", o + NC, o + 192), sub)
-            tt(ap("newv", o, o + 192), ap("Bv", o, o + 192), pb(b, 256, 448), A.max)
-            scatter(ap("pf"), sl(12, 18), ap("newv", o, o + NC))
-            scatter(ap("pf"), court(1, b), ap("newv", o + NC, o + 192))
+            scan(ap("S", h, h + u), ap("tri", 0, u), ap("H", h, h + u), mul, add)
+            cp(sl(0, 5), ap("S", (h + 2, h + u, 3)))
+            act(ap("EQD", NC * b, NC * b + NC), ind(ap("tab"), sl(1, 2)), AF.Copy)
+            act(ap("EQ", o, o + 2 * NC), ind(ap("tab"), sl(3, 5)), AF.Copy, M)
+            tt(q, ind(ap("pf"), sl(0, 1)), ap("EQD", NC * b, NC * b + NC), mul)
+            both = pb(b, 256, 256 + 2 * NC)
+            mm(both, ap("Ib"), ap("nM", 0, 2 * NC), True, False)
+            mm(pb(b, 256, 256 + NC), ap("BD32"), q, False, False)
+            mm(pb(b, 256 + NC, 256 + 2 * NC), ap("BD32"), q, False, False)
+            mm(both, ap("Ib"), ap("EQ", o, o + 2 * NC), False, True)
+            tt(ap("Bv", o, o + NC), ind(ap("pf"), sl(2, 3)), ap("EQ", o, o + NC), sub)
+            tt(ap("Bv", o + NC, o + 2 * NC), ind(ap("pf"), court(1, b)), ap("EQ", o + NC, o + 2 * NC), sub)
+            tt(ap("newv", o, o + 2 * NC), ap("Bv", o, o + 2 * NC), both, A.max)
+            scatter(ap("pf"), sl(2, 3), ap("newv", o, o + NC))
+            scatter(ap("pf"), court(1, b), ap("newv", o + NC, o + 2 * NC))
 
         def count():
-            z = pb(1, 472, 484)
-            for n, r in enumerate((ap("O2"), ap("E3"), ap("E", 0, 12), ap("E", 16, 28))):
-                mm(z, ap("onesb", 0, 128), r, n == 0, n == 3)
+            z = pb(NB - 1, 472, 484)
+            mm(z, ap("onesb", 0, 128), ap("O2"), True, False)
+            for b in range(NB):
+                mm(pb(NB - 1, 472, 472 + 2 * NJ), ap("onesb", 0, 128), ap("E", 32 * b, 32 * b + 2 * NJ), False, False)
+            mm(z, ap("onesb", 0, 128), ap("E3"), False, True)
             vector(Zn, [z], 1, lambda: g.vector.tensor_reduce(Zn[0], z[0], X, add))
             tt(Zc, Zc, Zn, add)
 
         for s in range(3):
-            for b in range(2):
+            for b in range(NB):
                 if s:
                     least(s - 1, b)
-                if (s, b) == (1, 1):
+                if (s, b) == (1, NB - 1):
                     book1()
                     if t:
                         count()
-                if (s, b) == (2, 1):
+                if (s, b) == (2, NB - 1):
                     book2()
                 keys(s, b)
-        for b in range(2):
+        for b in range(NB):
             least(2, b)
             close(b)
 
@@ -452,9 +469,14 @@ def rank_program(g, core, T, topo):
         visit(t)
     dma("y", "dyf", T.yf[:], ap("yfs")[0], [ap("yfs")], [])
 
-    for q in range(4):
-        o = 512 * q
-        ts(ap("sub", o, o + 512), ap("pf", 2048 + o, 2560 + o), 4096.0, mul)
-        tt(ap("yps", o, o + 512), ap("pf", o, o + 512), ap("sub", o, o + 512), add)
-        dma("y", "dy%d" % q, T.yp[:, o:o + 512], ap("yps", o, o + 512)[0], [ap("yps", o, o + 512)], [])
+    def high(n):
+        ts(ap("sub", 512 * (n % RING), 512 * (n % RING) + OUT[n + 1] - OUT[n]), ap("pf", 2048 + OUT[n], 2048 + OUT[n + 1]), 4096.0, mul)
+    high(0)
+    for n in range(len(OUT) - 1):
+        lo, hi = OUT[n], OUT[n + 1]
+        if hi < 2048:
+            high(n + 1)
+        tt(ap("yps", lo, hi), ap("pf", lo, hi), ap("sub", 512 * (n % RING), 512 * (n % RING) + hi - lo), add)
+        ops[-1]["soft"].append(len(ops) - 2) if hi < 2048 else None
+        dma("y", "dy%d" % n, T.yp[:, lo:hi], ap("yps", lo, hi)[0], [ap("yps", lo, hi)], [])
     issue(g, T, ops)

@@ -4,25 +4,25 @@ N = 8
 VI = 4
 NB = 3
 NJ, NC = 12 // NB, 192 // NB
-RK = (15 * NJ + 15) // 16
+RK = (18 * NJ + 15) // 16
 RING = 8 - NB
-SG = [[32, 16, 0], [24, 24, 24], [24, 32, 32]]
+SG = [[32, 32, 16], [24, 24, 24], [16, 32, 48]]
 VC = 32
-OUT = [0, 256, 640, 1088, 1600, 2048]
+OUT = [0, 256, 896, 2048]
 M = 8192.0
-CY, PE, GA, SC, WAKE, DL, RL, BW = 0.87, 0.46, 1.56, 3.8, 180, 2000, 3000, 250
+CY, PE, GA, SC, WAKE, DL, RL, BW = 0.87, 0.44, 1.56, 3.8, 220, 2000, 4000, 400
 F32, BF, I32T, U16 = "float32", "bfloat16", "int32", "uint16"
 SIZES = {
     F32: "pkg0 216 pkg1 216 pkg2 216 pkg3 216 ones32 128 I32 128 BD32 128 Wz32 144 cols 8 KU 224 TA 416 "
-         "OH 192 Q0 192 rst 96 K3 96 tri 96 tab 32 Q 192 Bv 384 yps 2048 H 288 S 288",
+         "OH 192 Q0 192 rst 96 K3 96 tri 108 tab 32 Q 192 Bv 384 PS 384 pf 4288 yps 2048 H 336 S 336",
     BF: "rtb 4096 fxs 192 fin 1152 fo 1152 fw 1152 yfs 192 onesb 144 Ib 128 nI 128 Wz 144 En 1536 nM 192 "
         "RS 384 R3 192 EQD 192 EQ 384 E 96 E3 12 O2 12",
-    I32T: "pks 2048 pf 4096 jcs 192 pidx 4 tl 36 i32 32 run 192 m0 12 r4 24 yi 24 newv 384",
-    U16: "rep 6 TL 12 N16 192 CL0 12 CL1 24 CL2 24 L3 12 SL 96",
+    I32T: "pks 2048 pu 4096 jcs 192 pidx 4 tl 36 i32 32 run 576 m0 12 r4 32 d1 12 d2 12",
+    U16: "rep 8 TL 12 N16 192 CL0 12 CL1 24 CL2 24 L3 12 SL 108",
 }
 SEG = "c1 c2 c3 p1 k1 k2 L1 L2 L3 Lm".split()
-WSEG = "POS PO2 PO3 P1 P2 P3 o1 oa ne T Tb da db ea eb fa fb ga gb ha hb ma mb qa qb".split()
-YSEG = "y1 y1b y2 y2b".split()
+WSEG = "POS DUM dm PO2 PO3 P1 P2 P3 o1 oa ne T Tb da db ea eb fa fb ga gb ha hb ma mb qa qb".split()
+YSEG = "y1 y1b y2 y2b z1 z2".split()
 SCRATCH = {
     "sr8": ("sbuf", [8, 192], I32T), "srb": ("sbuf", [8, 192], BF), "Sel": ("sbuf", [8, 128], BF),
     "KC0": ("sbuf", [128, NB, len(SEG), NJ], I32T), "KC1": ("sbuf", [128, NB, len(SEG), NJ], I32T),
@@ -38,7 +38,7 @@ for _ty in SIZES:
     _l = SIZES[_ty].split()
     for _i in range(0, len(_l), 2):
         SCRATCH[_l[_i]] = ("sbuf", [128, int(_l[_i + 1])], _ty)
-SEMAPHORES = ("cv cs ct cg ls pk1 pk2 pk3 dj ds df dp0 dp1 dp2 dp3 dr dyf".split() + ["fa%d" % _n for _n in range(3 * NB)]
+SEMAPHORES = ("cv cs ct cg ls pk1 pk2 pk3 dj ds df dp0 dp1 dr dyf".split() + ["fa%d" % _n for _n in range(3 * NB)]
               + ["dy%d" % _n for _n in range(len(OUT) - 1)])
 WIDTH = {F32: 4, BF: 2, I32T: 4, U16: 2}
 
@@ -186,9 +186,9 @@ def rank_program(g, core, T, topo):
     def scan(out, a, b, op0, op1):
         vector(out, [a, b], 1, lambda: g.vector.tensor_tensor_scan(out[0], a[0], b[0], 0.0, op0, op1))
 
-    def scatter(win, off, a):
+    def scatter(win, off, a, b):
         o = ind(win, off)
-        record("v", [a, off], [win], lambda: g.vector.tensor_copy(o[0], a[0]), 50 + CY * SC * cols(a))
+        record("v", [a, b, off], [win], lambda: g.vector.tensor_tensor(o[0], a[0], b[0], A.max), 50 + CY * SC * cols(a))
 
     def fill(out, c):
         vector(out, [], 1, lambda: g.vector.memset(out[0], c))
@@ -232,8 +232,8 @@ def rank_program(g, core, T, topo):
     load("y", "dj", ap("jcs"), T.jc[:])
     load("s", "ds", ap("sr8"), T.sr[:])
     load("s", "df", ap("fxs"), T.fx[:])
-    for h in range(4):
-        load("y", "dp%d" % h, ap("pks", 512 * h, 512 * h + 512), T.pk[:, 512 * h:512 * h + 512])
+    for h in range(2):
+        load("y", "dp%d" % h, ap("pks", 1024 * h, 1024 * h + 1024), T.pk[:, 1024 * h:1024 * h + 1024])
     load("y", "dr", ap("rtb"), T.rt[:])
 
     kp, kp4096, kp16, par, Zc, Zn = [ap("cols", c, c + 1) for c in range(6)]
@@ -247,9 +247,10 @@ def rank_program(g, core, T, topo):
     iota(ap("tl", 0, 12), [[0, 6], [1, 2]], 0, 0)
     asel(ap("I32"), ap("ones32"), [[-1, 128]], eq, 0, 1)
     iota(w("POS"), [[0, NB], [256, NJ]], 0, 0)
+    iota(w("DUM"), [[16, 12]], 4096, 0)
     iota(ap("K3", 0, NC), [[256, NJ], [4097, 16]], 0, 0)
     mm(pb(0, 0, 128), sel, sel, True, True)
-    fill(ap("En", 0, 16 * NC), -1.0)
+    iota(ap("En", 0, 16 * NC), [[0, 16 * NC]], -1, 0)
     asel(ap("En", 0, 16 * NC), ap("En", 0, 16 * NC), [[1, NC], [0, 16]], eq, 0, -1)
     ts(ap("pidx", 1, 2), ap("pidx", 0, 1), 15, A.bitwise_and)
     ts(ap("pidx", 2, 3), ap("pidx", 0, 1), 4, A.arith_shift_right, 1, A.bitwise_and)
@@ -265,21 +266,24 @@ def rank_program(g, core, T, topo):
     act(ap("nI"), ap("I32"), AF.Copy, -1.0)
     for b in range(NB):
         for h in range(2):
-            fill(ap("GC%d%d" % (b, h), 0, 16), 0.0)
-    fill(ap("rst"), 0.0)
-    fill(ap("rst", (0, NC, 16)), 33554432.0)
-    fill(ap("tri"), 1.0)
-    fill(ap("tri", (0, 96, 3)), 0.0)
+            act(ap("GC%d%d" % (b, h), 0, 16), ap("onesb", 0, 16), AF.Copy, 0.0)
+    asel(ap("rst"), ap("ones32", 0, 96), [[0, 6], [1, 16]], eq, 0, 0)
+    act(ap("rst"), ap("rst"), AF.Copy, 33554432.0)
+    iota(nd("AB", (0, NB, 1), (0, 16 * RK, 1)), [[0, 16 * RK * NB]], -16, 0)
+    asel(ap("tri"), ap("ones32", 0, 108), [[0, 36], [1, 3]], A.is_gt, 0, 0)
     ts(w("POS"), w("POS"), kp16, add)
     ts(ap("K3", 0, NC), ap("K3", 0, NC), kp16, add)
     fill(Zc, 0.0)
+    ts(w("DUM"), w("DUM"), kp, add)
+    iota(ap("pf", 4096, 4288), [[0, 192]], 0, 0)
+    iota(ab(0, 3, 4), [[0, 12]], 0, 0)
+    iota(ab(1, 3, 4), [[0, 12]], 0, 0)
     ts(ap("tab"), ap("i32"), kp, eq)
-    fill(ap("nM"), -M)
-    fill(ap("fo", 0, 384 * NB), 0.0)
-    fill(ap("E"), 1.0)
-    fill(nd("AB", (0, NB, 1), (0, 16 * RK, 1)), -16.0)
-    n, a, q, u = [ap("r4", 6 * c, 6 * c + 6) for c in range(4)]
-    ts(n, ap("i32", 0, 6), 16.0, mul, kp, add)
+    act(ap("nM", 0, 2 * NC), ap("onesb", 0, 2 * NC), AF.Copy, -M)
+    iota(ap("fo", 0, 384 * NB), [[0, 384 * NB]], 0, 0)
+    act(ap("E"), ap("onesb", 0, 96), AF.Copy)
+    n, a, q, u = [ap("r4", 8 * c, 8 * c + 8) for c in range(4)]
+    ts(n, ap("i32", 0, 8), 16.0, mul, kp, add)
     ts(a, n, -1.0, add, 1.0 / 3, mul)
     ts(q, a, (1 - NJ) / 2, add, 1.0 / NJ, mul)
     ts(u, a, 1.0 - 3 * NJ, mul)
@@ -290,7 +294,7 @@ def rank_program(g, core, T, topo):
 
     fill(ap("KU", 0, 16), 0.0)
     fill(ap("KU", 208, 224), 0.0)
-    cp(ap("srb"), ap("sr8"))
+    act(ap("srb"), ap("sr8"), AF.Copy)
     ts(ap("KU", 16, 208), ap("jcs"), kp4096, add)
     mm(pb(1, 0, 192), sel, ap("srb"), True, True)
     ts(ap("OH"), pb(1, 0, 192), kp, eq)
@@ -313,10 +317,12 @@ def rank_program(g, core, T, topo):
     act(ap("pkg0", 0, 192), ind(ap("TA"), ap("TL")), AF.Copy)
     cp(ap("pkg0", 192, 216), seg("KC0", SEG, "c1", "p1", None))
     for t in range(1, VI):
-        send(ring(t), ring(-t), ap("pkg%d" % t), ap("pkg0"), "pk%d" % t, 4 * RL)
+        send(ring(t), ring(-t), ap("pkg%d" % t), ap("pkg0"), "pk%d" % t, 3 * RL)
     for h in range(0, 2048, 512):
-        ts(ap("pf", h, h + 512), ap("pks", h, h + 512), 4095, A.bitwise_and)
-        ts(ap("pf", 2048 + h, 2560 + h), ap("pks", h, h + 512), 12, A.arith_shift_right)
+        ts(ap("pu", h, h + 512), ap("pks", h, h + 512), 4095, A.bitwise_and)
+        ts(ap("pu", 2048 + h, 2560 + h), ap("pks", h, h + 512), 12, A.arith_shift_right)
+        act(ap("pf", h, h + 512), ap("pu", h, h + 512), AF.Copy)
+        act(ap("pf", 2048 + h, 2560 + h), ap("pu", 2048 + h, 2560 + h), AF.Copy)
 
     def visit(t):
         KC, KN, last = "KC%d" % (t % 2), "KC%d" % ((t + 1) % 2), t + 1 == VI
@@ -330,7 +336,7 @@ def rank_program(g, core, T, topo):
 
         def keys(s, b):
             gc, D = "GC%d%d" % (b, (t + s) % 2), "D%d" % b
-            cp(ap("N16", NC * b, NC * b + NC), ind(ap("pf"), court(s, b)))
+            cp(ap("N16", NC * b, NC * b + NC), ind(ap("pf" if t else "pu"), court(s, b)))
             nv = NC - SG[s][b]
             cut = list(range(0, nv, VC)) + [nv] + [x for x in range(32, NC, 32) if x > nv] + [NC]
             for x0, x1 in zip(cut, cut[1:]):
@@ -350,11 +356,12 @@ def rank_program(g, core, T, topo):
                 mm(pb(b, 0, NC), blk("Wz", i), nd(D, (0, NJ, 1), (16 * i, 16 * i + 16, 1)), False, i == 15)
 
         def least(s, b):
-            mi = ap("run", (NC * b + 15, NC * b + NC, 16))
-            scan(ap("run", NC * b, NC * b + NC), ap("rst", 0, NC), pb(b, 0, NC), A.max, A.min)
+            o = 192 * s + NC * b
+            mi = ap("run", (o + 15, o + NC, 16))
+            scan(ap("run", o, o + NC), ap("rst", 0, NC), pb(b, 0, NC), A.max, A.min)
             if s < 2:
                 kn, cn, Ln = [k(a % (s + c), None, b) for a, c in (("k%d", 1), ("c%d", 2), ("L%d", 1))]
-                L, r = ap("CL%d" % (s + 1), 2 * NJ * b + NJ, 2 * NJ * (b + 1)), ap("RS", NC * (2 * b + s), NC * (2 * b + s + 1))
+                L, r = ap("CL%d" % (s + 1), 2 * NJ * b + NJ, 2 * NJ * (b + 1)), ap("RS", o, o + NC)
                 ts(cn, mi, 4095, A.bitwise_and)
                 ts(kn, mi, 12, A.arith_shift_right, 15, A.bitwise_and)
                 cp(court(s + 1, b), cn)
@@ -381,23 +388,31 @@ def rank_program(g, core, T, topo):
         def book1():
             tt(w("o1"), k("k1"), k("p1"), A.not_equal)
             tt(w("PO2"), w("POS"), w("o1"), mul)
+            tt(w("dm"), k("k1"), k("p1"), eq)
+            tt(w("dm"), w("dm"), w("DUM"), mul)
+            if t:
+                count()
+            for i in range(16):
+                mm(pb(NB - 1, 448, 460), blk("Wz", i), ap("RS", (i, 192, 16)), i == 0, i == 15)
+            ts(w("z1"), pb(NB - 1, 448, 460), 2.0 ** -16, mul, Zc, add)
+            ts(ap("d1"), ap("run", (15, 192, 16)), 16, A.arith_shift_right)
+            ts(ap("d1"), ap("d1"), Zc, add)
             if not last:
                 cp(seg(KN, SEG, "c1", "p1", None), ap("pkg%d" % (t + 1), 192, 216))
                 cp(ap("CL0"), seg(KN, SEG, "c1", None, None))
 
         def book2():
             X1, X2, X3a, X3b = k("c1", "k1"), k("c2", "k2"), k("c3", "p1"), k("c3", "k1")
-            for i in range(16):
-                mm(pb(NB - 1, 448, 472), blk("Wz", i), ap("RS", (i, 384, 16)), i == 0, i == 15)
-            ts(ap("yi"), pb(NB - 1, 448, 472), 2.0 ** -16, mul, Zc, add)
+            ts(ap("d2"), ap("run", (207, 384, 16)), 16, A.arith_shift_right)
+            tt(w("z2"), ap("d1"), ap("d2"), add)
             tt(w("ne"), k("k2"), k("k1"), A.not_equal)
             tt(w("T"), k("k2"), k("p1"), eq)
             tt(w("Tb"), k("k2"), k("p1"), eq)
             tt(w("oa"), w("o1"), w("ne"), mul)
             tt(w("da", "db"), X3a, X1, sub)
             tt(ap("O2"), w("oa"), w("T"), A.is_gt)
-            ts(w("y1", "y2"), ap("yi"), 1, A.bitwise_and)
-            ts(w("y1b", "y2b"), ap("yi"), 1, A.bitwise_and)
+            ts(w("y1", "y2"), w("z1", "z2"), 1, A.bitwise_and)
+            ts(w("y1b", "y2b"), w("z1", "z2"), 1, A.bitwise_and)
             tt(w("ea", "eb"), X2, X1, sub)
             tt(w("PO3"), w("POS"), ap("O2"), mul)
             for a, c in (("P1", "p1"), ("P2", "k1"), ("P3", "k2")):
@@ -407,39 +422,42 @@ def rank_program(g, core, T, topo):
             tt(w("ga", "gb"), w("y1", "y1b"), w("ea", "eb"), mul)
             tt(w("ha", "hb"), w("y2", "y2b"), w("fa", "fb"), mul)
             ts(w("qa", "qb"), w("T", "Tb"), -16.0, mul, 16.0, add)
-            tt(ab(0, 2, 4), w("da", "db"), ab(0, 0, 2), sub)
+            tt(ab(0, 2, 3), w("da"), ab(0, 0, 1), sub)
+            tt(w("oa"), w("db"), ab(0, 1, 2), sub)
             tt(w("ma", "mb"), w("ga", "gb"), w("T", "Tb"), mul)
             tt(ab(1, 0, 2), w("ha", "hb"), w("ea", "eb"), add)
-            tt(ab(2, 3, 5), k("k1", "k2"), w("qa", "qb"), add)
-            ts(ab(0, 3, 4), ab(0, 3, 4), -16.0, add)
+            tt(ab(2, 4, 6), k("k1", "k2"), w("qa", "qb"), add)
+            ts(ab(0, 4, 5), w("oa"), -16.0, add)
             tt(ab(2, 0, 2), X1, w("ma", "mb"), add)
             cp(ab(1, 2, 3), w("da"))
-            cp(ab(2, 2, 3), k("c1"))
+            tt(ab(2, 2, 3), k("c1"), w("dm"), A.max)
+            cp(ab(2, 3, 4), k("c2"))
 
         def close(b):
             def sl(lo, hi):
-                return ap("SL", 32 * b + NJ * lo, 32 * b + NJ * hi)
-            e, h, o, u, q = 32 * b, 96 * b, 2 * NC * b, 15 * NJ, ap("Q", NC * b, NC * b + NC)
+                return ap("SL", 36 * b + NJ * lo, 36 * b + NJ * hi)
+            e, h, o, u, q = 32 * b, 112 * b, 2 * NC * b, 18 * NJ, ap("Q", NC * b, NC * b + NC)
             tt(ap("E", e, e + NJ), k("L3", None, b), w("P1", None, b), eq)
             tt(ap("E", e + NJ, e + 2 * NJ), k("L3", None, b), w("P2", None, b), eq)
             tt(ap("H", h, h + 16 * RK), ind(ap("E", e, e + 3 * NJ), ap("rep", 0, RK)), nd("AB", (b, b + 1, 1), (0, 16 * RK, 1)), mul)
-            if not last:
-                tt(ap("E3", NJ * b, NJ * b + NJ), k("L3", None, b), w("P3", None, b), eq)
+            if not last and b == NB - 1:
+                tt(ap("E3"), k("L3"), w("P3"), eq)
             scan(ap("S", h, h + u), ap("tri", 0, u), ap("H", h, h + u), mul, add)
-            cp(sl(0, 5), ap("S", (h + 2, h + u, 3)))
+            cp(sl(0, 6), ap("S", (h + 2, h + u, 3)))
             act(ap("EQD", NC * b, NC * b + NC), ind(ap("tab"), sl(1, 2)), AF.Copy)
-            act(ap("EQ", o, o + 2 * NC), ind(ap("tab"), sl(3, 5)), AF.Copy, M)
+            act(ap("EQ", o, o + 2 * NC), ind(ap("tab"), sl(4, 6)), AF.Copy, M)
             tt(q, ind(ap("pf"), sl(0, 1)), ap("EQD", NC * b, NC * b + NC), mul)
             both = pb(b, 256, 256 + 2 * NC)
             mm(both, ap("Ib"), ap("nM", 0, 2 * NC), True, False)
             mm(pb(b, 256, 256 + NC), ap("BD32"), q, False, False)
             mm(pb(b, 256 + NC, 256 + 2 * NC), ap("BD32"), q, False, False)
             mm(both, ap("Ib"), ap("EQ", o, o + 2 * NC), False, True)
-            tt(ap("Bv", o, o + NC), ind(ap("pf"), sl(2, 3)), ap("EQ", o, o + NC), sub)
-            tt(ap("Bv", o + NC, o + 2 * NC), ind(ap("pf"), court(1, b)), ap("EQ", o + NC, o + 2 * NC), sub)
-            tt(ap("newv", o, o + 2 * NC), ap("Bv", o, o + 2 * NC), both, A.max)
-            scatter(ap("pf"), sl(2, 3), ap("newv", o, o + NC))
-            scatter(ap("pf"), court(1, b), ap("newv", o + NC, o + 2 * NC))
+            tt(ap("Bv", o, o + 2 * NC), ind(ap("pf"), sl(2, 4)), ap("EQ", o, o + 2 * NC), sub)
+            act(ap("PS", o, o + 2 * NC), both, AF.Copy)
+
+        def change(b):
+            o = 2 * NC * b
+            scatter(ap("pf"), ap("SL", 36 * b + 2 * NJ, 36 * b + 4 * NJ), ap("Bv", o, o + 2 * NC), ap("PS", o, o + 2 * NC))
 
         def count():
             z = pb(NB - 1, 472, 484)
@@ -456,27 +474,26 @@ def rank_program(g, core, T, topo):
                     least(s - 1, b)
                 if (s, b) == (1, NB - 1):
                     book1()
-                    if t:
-                        count()
                 if (s, b) == (2, NB - 1):
                     book2()
                 keys(s, b)
         for b in range(NB):
             least(2, b)
             close(b)
+            if b:
+                change(b - 1)
+        change(NB - 1)
 
     for t in range(VI):
         visit(t)
     dma("y", "dyf", T.yf[:], ap("yfs")[0], [ap("yfs")], [])
 
-    def high(n):
-        ts(ap("sub", 512 * (n % RING), 512 * (n % RING) + OUT[n + 1] - OUT[n]), ap("pf", 2048 + OUT[n], 2048 + OUT[n + 1]), 4096.0, mul)
-    high(0)
     for n in range(len(OUT) - 1):
-        lo, hi = OUT[n], OUT[n + 1]
-        if hi < 2048:
-            high(n + 1)
-        tt(ap("yps", lo, hi), ap("pf", lo, hi), ap("sub", 512 * (n % RING), 512 * (n % RING) + hi - lo), add)
-        ops[-1]["soft"].append(len(ops) - 2) if hi < 2048 else None
-        dma("y", "dy%d" % n, T.yp[:, lo:hi], ap("yps", lo, hi)[0], [ap("yps", lo, hi)], [])
+        for lo in range(OUT[n], OUT[n + 1], 384):
+            hi, o = min(lo + 384, OUT[n + 1]), 512 * turn[0]
+            turn[0] = (turn[0] + 1) % RING
+            act(ap("sub", o, o + hi - lo), ap("pf", 2048 + lo, 2048 + hi), AF.Copy, 4096.0)
+            tt(ap("yps", lo, hi), ap("pf", lo, hi), ap("sub", o, o + hi - lo), add)
+        piece = ap("yps", OUT[n], OUT[n + 1])
+        dma("y", "dy%d" % n, T.yp[:, OUT[n]:OUT[n + 1]], piece[0], [piece], [])
     issue(g, T, ops)

@@ -4,16 +4,17 @@ N = 8
 VI = 4
 NB = 3
 NJ, NC = 12 // NB, 192 // NB
-RK = (18 * NJ + 15) // 16
+RK = (12 * NJ + 15) // 16
 RING = 8 - NB
-SG = [[32, 32, 16], [24, 24, 24], [16, 32, 48]]
+SG = [[30, 26, 8], [44, 28, 32], [16, 26, 32]]
 VC = 32
-OUT = [0, 256, 896, 2048]
+OUT = [0, 512, 1280, 2048]
 M = 8192.0
-CY, PE, GA, SC, WAKE, DL, RL, BW = 0.87, 0.44, 1.56, 3.8, 220, 2000, 4000, 400
+CY, PE, GA, SC, WAKE, DL, RL, BW = 0.87, 0.44, 1.56, 3.8, 260, 1500, 6000, 400
+PL = 16000
 F32, BF, I32T, U16 = "float32", "bfloat16", "int32", "uint16"
 SIZES = {
-    F32: "pkg0 216 pkg1 216 pkg2 216 pkg3 216 ones32 128 I32 128 BD32 128 Wz32 144 cols 8 KU 224 TA 416 "
+    F32: "pkg0 216 pkg1 216 pkg2 216 pkg3 216 ones32 128 I32 128 I4k 128 BD32 128 Wz32 144 cols 8 KU 224 TA 416 "
          "OH 192 Q0 192 rst 96 K3 96 tri 108 tab 32 Q 192 Bv 384 PS 384 pf 4288 yps 2048 H 336 S 336",
     BF: "rtb 4096 fxs 192 fin 1152 fo 1152 fw 1152 yfs 192 onesb 144 Ib 128 nI 128 Wz 144 En 1536 nM 192 "
         "RS 384 R3 192 EQD 192 EQ 384 E 96 E3 12 O2 12",
@@ -27,7 +28,7 @@ SCRATCH = {
     "sr8": ("sbuf", [8, 192], I32T), "srb": ("sbuf", [8, 192], BF), "Sel": ("sbuf", [8, 128], BF),
     "KC0": ("sbuf", [128, NB, len(SEG), NJ], I32T), "KC1": ("sbuf", [128, NB, len(SEG), NJ], I32T),
     "W4": ("sbuf", [128, NB, len(WSEG), NJ], F32), "Y4": ("sbuf", [128, NB, len(YSEG), NJ], I32T),
-    "AB": ("sbuf", [128, NB, 16 * RK], F32), "sub": ("psum", [128, 512 * RING], F32),
+    "AB": ("sbuf", [128, NB, 18 * NJ], F32), "sub": ("psum", [128, 512 * RING], F32),
 }
 for _b in range(NB):
     SCRATCH["pb%d" % _b] = ("psum", [128, 512], F32)
@@ -99,7 +100,7 @@ def rank_program(g, core, T, topo):
         return
     A, AF, X = AluOpType, ActivationFunctionType, AxisListType.X
     add, sub, mul, eq = A.add, A.subtract, A.mult, A.is_equal
-    ops, wrote, read, turn, loaded = [], {}, {}, [0], [0, None]
+    ops, wrote, read, made, turn, loaded = [], {}, {}, [], [0], [0, None]
 
     def ap(name, a=None, b=None, P=None):
         shape = SCRATCH[name][1]
@@ -156,10 +157,10 @@ def rank_program(g, core, T, topo):
     def load(q, sem, buf, x):
         dma(q, sem, buf[0], x, [], [buf])
 
-    def send(dst, src_core, dst_ap, src, rsem, lat=RL):
+    def send(dst, src_core, dst_ap, src, rsem, lat=RL, soft=()):
         rid, pid, _ = topo.addr(dst)
         me = record("g", [src], [], lambda: g.remote_dma(dst_ap[0], src[0], T.sem[rsem], T.sem["ls"], pid, rid, topo.mask(core, dst)),
-                    300, "ls", len(topo.engines(core, dst)))
+                    300, "ls", len(topo.engines(core, dst)), soft=soft)
         record(None, [], [dst_ap], None, 0, rsem, len(topo.engines(src_core, core)), lat, [me])
 
     def vector(out, ins, per, call, more=()):
@@ -200,11 +201,17 @@ def rank_program(g, core, T, topo):
         wide = 4 if SCRATCH[l[1][0][0]][2] == F32 else 1
         record("t", [l, r], [out], lambda: g.tensor.matmul(out[0], l[0], r[0], start, stop), PE * wide * max(min(64, cols(l)), cols(r)))
 
+    def gpsimd(reads, out, call, cost):
+        made.append(record("g", reads, [out], call, cost + 2 * CY * cols(out), soft=made[-1:]))
+
     def iota(out, pattern, base, cm):
-        record("g", [], [out], lambda: g.iota(out[0], pattern, base, cm, allow_small_or_imprecise_dtypes=True), 130 + 2 * CY * cols(out))
+        gpsimd([], out, lambda: g.iota(out[0], pattern, base, cm, allow_small_or_imprecise_dtypes=True), 130)
 
     def asel(out, a, pattern, op, base, cm):
-        record("g", [a], [out], lambda: g.affine_select(out[0], a[0], pattern, op, 0.0, base, cm), 170 + 2 * CY * cols(out))
+        gpsimd([a], out, lambda: g.affine_select(out[0], a[0], pattern, op, 0.0, base, cm), 170)
+
+    def gcp(out, a):
+        record("g", [a], [out], lambda: g.affine_select(out[0], a[0], [[0, cols(out)]], eq, 0.0, 0, 0), 170 + 2 * CY * cols(out))
 
     def seg(buf, names, a, c, b):
         i = names.index(a)
@@ -224,7 +231,7 @@ def rank_program(g, core, T, topo):
         return ap(name, 128 * n, 128 * n + 128, NC)
 
     def ab(r, lo, hi):
-        return nd("AB", (0, NB, 1), (3 * NJ * lo + r, 3 * NJ * hi, 3))
+        return nd("AB", (0, NB, 1), (6 * NJ * r + NJ * lo, 6 * NJ * r + NJ * hi, 1))
 
     def ring(d):
         return T.cores[(rank + d) % N]
@@ -250,6 +257,7 @@ def rank_program(g, core, T, topo):
     iota(w("DUM"), [[16, 12]], 4096, 0)
     iota(ap("K3", 0, NC), [[256, NJ], [4097, 16]], 0, 0)
     mm(pb(0, 0, 128), sel, sel, True, True)
+    asel(ap("rst"), ap("ones32", 0, 96), [[0, 6], [1, 16]], eq, 0, 0)
     iota(ap("En", 0, 16 * NC), [[0, 16 * NC]], -1, 0)
     asel(ap("En", 0, 16 * NC), ap("En", 0, 16 * NC), [[1, NC], [0, 16]], eq, 0, -1)
     ts(ap("pidx", 1, 2), ap("pidx", 0, 1), 15, A.bitwise_and)
@@ -263,14 +271,13 @@ def rank_program(g, core, T, topo):
     act(ap("BD32"), pb(0, 0, 128), AF.Copy)
     act(ap("Wz"), ap("Wz32"), AF.Copy, 65536.0)
     act(ap("Ib"), ap("I32"), AF.Copy)
+    act(ap("I4k"), ap("I32"), AF.Copy, 4096.0)
     act(ap("nI"), ap("I32"), AF.Copy, -1.0)
     for b in range(NB):
         for h in range(2):
             act(ap("GC%d%d" % (b, h), 0, 16), ap("onesb", 0, 16), AF.Copy, 0.0)
-    asel(ap("rst"), ap("ones32", 0, 96), [[0, 6], [1, 16]], eq, 0, 0)
     act(ap("rst"), ap("rst"), AF.Copy, 33554432.0)
-    iota(nd("AB", (0, NB, 1), (0, 16 * RK, 1)), [[0, 16 * RK * NB]], -16, 0)
-    asel(ap("tri"), ap("ones32", 0, 108), [[0, 36], [1, 3]], A.is_gt, 0, 0)
+    iota(nd("AB", (0, NB, 1), (0, 18 * NJ, 1)), [[0, 18 * NJ * NB]], -16, 0)
     ts(w("POS"), w("POS"), kp16, add)
     ts(ap("K3", 0, NC), ap("K3", 0, NC), kp16, add)
     fill(Zc, 0.0)
@@ -281,16 +288,11 @@ def rank_program(g, core, T, topo):
     ts(ap("tab"), ap("i32"), kp, eq)
     act(ap("nM", 0, 2 * NC), ap("onesb", 0, 2 * NC), AF.Copy, -M)
     iota(ap("fo", 0, 384 * NB), [[0, 384 * NB]], 0, 0)
-    act(ap("E"), ap("onesb", 0, 96), AF.Copy)
     n, a, q, u = [ap("r4", 8 * c, 8 * c + 8) for c in range(4)]
     ts(n, ap("i32", 0, 8), 16.0, mul, kp, add)
-    ts(a, n, -1.0, add, 1.0 / 3, mul)
-    ts(q, a, (1 - NJ) / 2, add, 1.0 / NJ, mul)
-    ts(u, a, 1.0 - 3 * NJ, mul)
-    tt(n, n, q, sub)
-    ts(n, n, 1.0 * NJ, mul)
-    tt(n, n, u, add)
-    cp(ap("rep"), n)
+    ts(a, n, NJ - 1, A.bitwise_and)
+    ts(q, n, 6.0 * NJ, A.is_ge, 1.0 * NJ, mul)
+    tt(ap("rep"), a, q, add)
 
     fill(ap("KU", 0, 16), 0.0)
     fill(ap("KU", 208, 224), 0.0)
@@ -316,8 +318,6 @@ def rank_program(g, core, T, topo):
     cp(ap("TL"), ap("tl", 24, 36))
     act(ap("pkg0", 0, 192), ind(ap("TA"), ap("TL")), AF.Copy)
     cp(ap("pkg0", 192, 216), seg("KC0", SEG, "c1", "p1", None))
-    for t in range(1, VI):
-        send(ring(t), ring(-t), ap("pkg%d" % t), ap("pkg0"), "pk%d" % t, 3 * RL)
     for h in range(0, 2048, 512):
         ts(ap("pu", h, h + 512), ap("pks", h, h + 512), 4095, A.bitwise_and)
         ts(ap("pu", 2048 + h, 2560 + h), ap("pks", h, h + 512), 12, A.arith_shift_right)
@@ -348,8 +348,11 @@ def rank_program(g, core, T, topo):
             for c in range(NJ // 2):
                 bank = ap("sub", 512 * turn[0], 512 * turn[0] + 512)
                 turn[0] = (turn[0] + 1) % RING
-                mm(bank, facts[b], ap("En", 512 * c, 512 * c + 512, NC), True, False)
-                mm(bank, ap("Ib"), ap(gc, 16 + 512 * c, 528 + 512 * c), False, True)
+                pair = [(facts[b], ap("En", 512 * c, 512 * c + 512, NC)), (ap("Ib"), ap(gc, 16 + 512 * c, 528 + 512 * c))]
+                if c == 0 or s == 1:
+                    pair.reverse()
+                mm(bank, *pair[0], True, False)
+                mm(bank, *pair[1], False, True)
                 act(nd(D, (2 * c, 2 * c + 2, 1), (0, 256, 1)), bank, AF.Abs)
             mm(pb(b, 0, NC), ap("I32"), ap("pkg%d" % t, NC * b, NC * b + NC) if s < 2 else ap("K3", 0, NC), True, False)
             for i in range(16):
@@ -365,13 +368,15 @@ def rank_program(g, core, T, topo):
                 ts(cn, mi, 4095, A.bitwise_and)
                 ts(kn, mi, 12, A.arith_shift_right, 15, A.bitwise_and)
                 cp(court(s + 1, b), cn)
-                tt(Ln, kn, w(("POS", "PO2")[s], None, b), add)
+                tt(L, kn, w(("POS", "PO2")[s], None, b), add)
             else:
                 L, r, Ln = ap("L3", NJ * b, NJ * b + NJ), ap("R3", NC * b, NC * b + NC), k("Lm", None, b)
                 ts(k("L3", None, b), mi, 4095, A.bitwise_and)
-                tt(Ln, k("L3", None, b), ap("O2", NJ * b, NJ * b + NJ), mul)
-            cp(L, Ln)
-            act(r, ind(ap("GC%d%d" % (b, (t + s) % 2)), L), AF.Copy)
+                tt(L, k("L3", None, b), ap("O2", NJ * b, NJ * b + NJ), mul)
+            if s < 2 or b < NB - 1:
+                cp(r, ind(ap("GC%d%d" % (b, (t + s) % 2)), L))
+            else:
+                act(r, ind(ap("GC%d%d" % (b, (t + s) % 2)), L), AF.Copy)
             if s == 2 and last:
                 mm(pb(b, 128, 128 + NC), facts[b], ap("nI", 0, NC, NC), True, False)
                 mm(pb(b, 128, 128 + NC), ap("Ib"), r, False, True)
@@ -398,7 +403,7 @@ def rank_program(g, core, T, topo):
             ts(ap("d1"), ap("run", (15, 192, 16)), 16, A.arith_shift_right)
             ts(ap("d1"), ap("d1"), Zc, add)
             if not last:
-                cp(seg(KN, SEG, "c1", "p1", None), ap("pkg%d" % (t + 1), 192, 216))
+                gcp(seg(KN, SEG, "c1", "p1", None), ap("pkg%d" % (t + 1), 192, 216))
                 cp(ap("CL0"), seg(KN, SEG, "c1", None, None))
 
         def book2():
@@ -407,12 +412,12 @@ def rank_program(g, core, T, topo):
             tt(w("z2"), ap("d1"), ap("d2"), add)
             tt(w("ne"), k("k2"), k("k1"), A.not_equal)
             tt(w("T"), k("k2"), k("p1"), eq)
-            tt(w("Tb"), k("k2"), k("p1"), eq)
+            gcp(w("Tb"), w("T"))
             tt(w("oa"), w("o1"), w("ne"), mul)
             tt(w("da", "db"), X3a, X1, sub)
             tt(ap("O2"), w("oa"), w("T"), A.is_gt)
             ts(w("y1", "y2"), w("z1", "z2"), 1, A.bitwise_and)
-            ts(w("y1b", "y2b"), w("z1", "z2"), 1, A.bitwise_and)
+            gcp(w("y1b", "y2b"), w("y1", "y2"))
             tt(w("ea", "eb"), X2, X1, sub)
             tt(w("PO3"), w("POS"), ap("O2"), mul)
             for a, c in (("P1", "p1"), ("P2", "k1"), ("P3", "k2")):
@@ -429,21 +434,21 @@ def rank_program(g, core, T, topo):
             tt(ab(2, 4, 6), k("k1", "k2"), w("qa", "qb"), add)
             ts(ab(0, 4, 5), w("oa"), -16.0, add)
             tt(ab(2, 0, 2), X1, w("ma", "mb"), add)
-            cp(ab(1, 2, 3), w("da"))
+            gcp(ab(1, 2, 3), w("da"))
             tt(ab(2, 2, 3), k("c1"), w("dm"), A.max)
-            cp(ab(2, 3, 4), k("c2"))
+            gcp(ab(2, 3, 4), k("c2"))
 
         def close(b):
             def sl(lo, hi):
                 return ap("SL", 36 * b + NJ * lo, 36 * b + NJ * hi)
-            e, h, o, u, q = 32 * b, 112 * b, 2 * NC * b, 18 * NJ, ap("Q", NC * b, NC * b + NC)
+            e, h, o, u, q = 32 * b, 112 * b, 2 * NC * b, 6 * NJ, ap("Q", NC * b, NC * b + NC)
             tt(ap("E", e, e + NJ), k("L3", None, b), w("P1", None, b), eq)
             tt(ap("E", e + NJ, e + 2 * NJ), k("L3", None, b), w("P2", None, b), eq)
-            tt(ap("H", h, h + 16 * RK), ind(ap("E", e, e + 3 * NJ), ap("rep", 0, RK)), nd("AB", (b, b + 1, 1), (0, 16 * RK, 1)), mul)
+            tt(ap("H", h, h + 16 * RK), ind(ap("E", e, e + 2 * NJ), ap("rep", 0, RK)), nd("AB", (b, b + 1, 1), (0, 16 * RK, 1)), mul)
             if not last and b == NB - 1:
                 tt(ap("E3"), k("L3"), w("P3"), eq)
-            scan(ap("S", h, h + u), ap("tri", 0, u), ap("H", h, h + u), mul, add)
-            cp(sl(0, 6), ap("S", (h + 2, h + u, 3)))
+            tt(ap("S", h, h + u), ap("H", h, h + u), nd("AB", (b, b + 1, 1), (2 * u, 3 * u, 1)), add)
+            tt(sl(0, 6), ap("S", h, h + u), ap("H", h + u, h + 2 * u), add)
             act(ap("EQD", NC * b, NC * b + NC), ind(ap("tab"), sl(1, 2)), AF.Copy)
             act(ap("EQ", o, o + 2 * NC), ind(ap("tab"), sl(4, 6)), AF.Copy, M)
             tt(q, ind(ap("pf"), sl(0, 1)), ap("EQD", NC * b, NC * b + NC), mul)
@@ -468,6 +473,8 @@ def rank_program(g, core, T, topo):
             vector(Zn, [z], 1, lambda: g.vector.tensor_reduce(Zn[0], z[0], X, add))
             tt(Zc, Zc, Zn, add)
 
+        if not last:
+            send(ring(t + 1), ring(-t - 1), ap("pkg%d" % (t + 1)), ap("pkg0"), "pk%d" % (t + 1), PL, [len(ops) - 1] if t else [])
         for s in range(3):
             for b in range(NB):
                 if s:
@@ -489,10 +496,13 @@ def rank_program(g, core, T, topo):
     dma("y", "dyf", T.yf[:], ap("yfs")[0], [ap("yfs")], [])
 
     for n in range(len(OUT) - 1):
-        for lo in range(OUT[n], OUT[n + 1], 384):
-            hi, o = min(lo + 384, OUT[n + 1]), 512 * turn[0]
+        for lo in range(OUT[n], OUT[n + 1], 256):
+            hi, o = lo + 256, 512 * turn[0]
             turn[0] = (turn[0] + 1) % RING
-            act(ap("sub", o, o + hi - lo), ap("pf", 2048 + lo, 2048 + hi), AF.Copy, 4096.0)
+            if lo % 768 == 256:
+                mm(ap("sub", o, o + 256), ap("I4k"), ap("pf", 2048 + lo, 2048 + hi), True, True)
+            else:
+                act(ap("sub", o, o + 256), ap("pf", 2048 + lo, 2048 + hi), AF.Copy, 4096.0)
             tt(ap("yps", lo, hi), ap("pf", lo, hi), ap("sub", o, o + hi - lo), add)
         piece = ap("yps", OUT[n], OUT[n + 1])
         dma("y", "dy%d" % n, T.yp[:, OUT[n]:OUT[n + 1]], piece[0], [piece], [])

from concourse.mybir import dt, AluOpType, AxisListType, ActivationFunctionType

N = 8
VI = 4
NB = 3
NJ, NC = 12 // NB, 192 // NB
RK = (12 * NJ + 15) // 16
RING = 8 - NB
SG = [[30, 26, 8], [44, 28, 32], [16, 26, 32]]
VC = 32
OUT = [0, 512, 1280, 2048]
M = 8192.0
CY, PE, GA, SC, WAKE, DL, RL, BW = 0.87, 0.44, 1.56, 3.8, 260, 1500, 6000, 400
PL = 16000
F32, BF, I32T, U16 = "float32", "bfloat16", "int32", "uint16"
SIZES = {
    F32: "pkg0 216 pkg1 216 pkg2 216 pkg3 216 ones32 128 I32 128 I4k 128 BD32 128 Wz32 144 cols 8 KU 224 TA 416 "
         "OH 192 Q0 192 rst 96 K3 96 tri 108 tab 32 Q 192 Bv 384 PS 384 pf 4288 yps 2048 H 336 S 336",
    BF: "rtb 4096 fxs 192 fin 1152 fo 1152 fw 1152 yfs 192 onesb 144 Ib 128 nI 128 Wz 144 En 1536 nM 192 "
        "RS 384 R3 192 EQD 192 EQ 384 E 96 E3 12 O2 12",
    I32T: "pks 2048 pu 4096 jcs 192 pidx 4 tl 36 i32 32 run 576 m0 12 r4 32 d1 12 d2 12",
    U16: "rep 8 TL 12 N16 192 CL0 12 CL1 24 CL2 24 L3 12 SL 108",
}
SEG = "c1 c2 c3 p1 k1 k2 L1 L2 L3 Lm".split()
WSEG = "POS DUM dm PO2 PO3 P1 P2 P3 o1 oa ne T Tb da db ea eb fa fb ga gb ha hb ma mb qa qb".split()
YSEG = "y1 y1b y2 y2b z1 z2".split()
SCRATCH = {
    "sr8": ("sbuf", [8, 192], I32T), "srb": ("sbuf", [8, 192], BF), "Sel": ("sbuf", [8, 128], BF),
    "KC0": ("sbuf", [128, NB, len(SEG), NJ], I32T), "KC1": ("sbuf", [128, NB, len(SEG), NJ], I32T),
    "W4": ("sbuf", [128, NB, len(WSEG), NJ], F32), "Y4": ("sbuf", [128, NB, len(YSEG), NJ], I32T),
    "AB": ("sbuf", [128, NB, 18 * NJ], F32), "sub": ("psum", [128, 512 * RING], F32),
}
for _b in range(NB):
    SCRATCH["pb%d" % _b] = ("psum", [128, 512], F32)
    SCRATCH["D%d" % _b] = ("sbuf", [128, NJ, 256], BF)
    for _h in range(2):
        SCRATCH["GC%d%d" % (_b, _h)] = ("sbuf", [128, 16 + 16 * NC], BF)
for _ty in SIZES:
    _l = SIZES[_ty].split()
    for _i in range(0, len(_l), 2):
        SCRATCH[_l[_i]] = ("sbuf", [128, int(_l[_i + 1])], _ty)
SEMAPHORES = ("cv cs ct cg ls pk1 pk2 pk3 dj ds df dp0 dp1 dr dyf".split() + ["fa%d" % _n for _n in range(3 * NB)]
              + ["dy%d" % _n for _n in range(len(OUT) - 1)])
WIDTH = {F32: 4, BF: 2, I32T: 4, U16: 2}


def place(ops, before, rank):
    busy, start = {}, {}
    for n in sorted(range(len(ops)), key=lambda n: rank[n]):
        o = ops[n]
        t = max([start[p] + gap for p, gap in before[n]] + [0.0])
        slots = busy.setdefault(o["q"], [])
        i = len(slots)
        while i and slots[i - 1][1] > t:
            i -= 1
        while i < len(slots) and o["q"] and slots[i][0] < t + o["cost"]:
            t = max(t, slots[i][1])
            i += 1
        slots.insert(i, (t, t + o["cost"]))
        start[n] = t
    return start


def issue(g, T, ops):
    fore, back = [[] for _ in ops], [[] for _ in ops]
    for n, o in enumerate(ops):
        for p in o["dep"] + o["soft"]:
            gap = 0 if p in o["soft"] else ops[p]["lat"] + WAKE
            fore[n].append((p, ops[p]["cost"] + gap))
            back[p].append((n, o["cost"] + gap))
    start = place(ops, fore, [(n, n) for n in range(len(ops))])
    late = place(ops, back, [(-start[n] - o["cost"], -n) for n, o in enumerate(ops)])
    start = place(ops, fore, [(-late[n] - o["cost"], n) for n, o in enumerate(ops)])
    seq = sorted(range(len(ops)), key=lambda n: (start[n], n))
    queues = {"v": g.vector, "s": g.scalar, "t": g.tensor, "g": g, "y": g.sync}
    know = {q: {} for q in queues}
    total, mark = {}, {}
    for n in seq:
        o = ops[n]
        k = know.get(o["q"], {})
        for sem, val, clock in sorted([mark[p] for p in o["dep"]], key=lambda e: (-len(e[2]), -e[1])):
            if k.get(sem, 0) < val:
                queues[o["q"]].wait_ge(T.sem[sem], val)
                for s2, v2 in clock.items():
                    k[s2] = max(k.get(s2, 0), v2)
        total[o["sem"]] = total.get(o["sem"], 0) + o["inc"]
        if o["call"]:
            r = o["call"]()
            if o["sem"] != "ls":
                r.then_inc(T.sem[o["sem"]], o["inc"])
        mark[n] = (o["sem"], total[o["sem"]], dict(k, **{o["sem"]: total[o["sem"]]}))
    for sem in SEMAPHORES:
        if total.get(sem, 0) > know["g"].get(sem, 0):
            g.wait_ge(T.sem[sem], total[sem])


def rank_program(g, core, T, topo):
    rank = T.rank_of(core)
    if rank is None:
        return
    A, AF, X = AluOpType, ActivationFunctionType, AxisListType.X
    add, sub, mul, eq = A.add, A.subtract, A.mult, A.is_equal
    ops, wrote, read, made, turn, loaded = [], {}, {}, [], [0], [0, None]

    def ap(name, a=None, b=None, P=None):
        shape = SCRATCH[name][1]
        p = slice(0, shape[0] if P is None else P)
        lo, hi, st = (0, shape[1], 1) if a is None else (a if isinstance(a, tuple) else (a, b, 1))
        return (T[name][p, slice(lo, hi) if st == 1 else slice(lo, hi, st)], [(name, lo, hi, st)])

    def nd(name, *ix):
        shape = SCRATCH[name][1]
        runs = [0]
        for d, (lo, hi, st) in enumerate(ix[:-1]):
            runs = [(r + i) * shape[d + 2] for r in runs for i in range(lo, hi, st)]
        lo, hi, st = ix[-1]
        view = T[name][(slice(0, 128),) + tuple(l if h == l + 1 else slice(l, h, s) for l, h, s in ix)]
        return (view, [(name, r + lo, r + hi, st) for r in runs])

    def ind(win, off):
        return (win[0].indirect(off[0]), win[1] + off[1], True)

    def cols(a):
        return sum(len(range(lo, hi, st)) for _, lo, hi, st in a[1])

    def record(q, reads, writes, call, cost, sem=None, inc=1, lat=0, soft=()):
        me, dep = len(ops), set()
        rw = [(x, False) for r in reads for x in r[1]] + [(x, True) for r in writes for x in r[1]]
        for (name, lo, hi, st), isw in rw:
            if SCRATCH[name][0] == "psum":
                lo, hi, st, isw = lo // 512 * 512, (hi + 511) // 512 * 512, 1, True
            for log in (wrote, read) if isw else (wrote,):
                keep = []
                for e in log.get(name, []):
                    meets = lo < e[1] and e[0] < hi and not (st > 1 and st == e[2] and (lo - e[0]) % st)
                    if meets and e[3] != me:
                        dep.add(e[3])
                    if not (isw and lo <= e[0] and e[1] <= hi and (st == 1 or (st == e[2] and (lo - e[0]) % st == 0))):
                        keep.append(e)
                log[name] = keep
            (wrote if isw else read).setdefault(name, []).append((lo, hi, st, me))
        inorder = [p for p in dep if q == "t" and ops[p]["q"] == "t"]
        ops.append({"q": q, "call": call, "cost": cost, "lat": lat, "sem": sem or "c" + q, "inc": inc,
                    "dep": [p for p in dep if p not in inorder], "soft": inorder + list(soft)})
        return me

    def dma(q, sem, out, in_, reads, writes):
        buf = (reads + writes)[0]
        queue = g.sync if q == "y" else g.scalar
        size = 128 * cols(buf) * WIDTH[SCRATCH[buf[1][0][0]][2]]
        loaded[0] = size + (loaded[0] if writes else 0)
        me = record(q, reads, writes, lambda: queue.dma_start(out, in_), 60, sem, 16, DL + loaded[0] / BW,
                    [loaded[1]] if q == "y" and loaded[1] is not None else [])
        if q == "y":
            loaded[1] = me

    def load(q, sem, buf, x):
        dma(q, sem, buf[0], x, [], [buf])

    def send(dst, src_core, dst_ap, src, rsem, lat=RL, soft=()):
        rid, pid, _ = topo.addr(dst)
        me = record("g", [src], [], lambda: g.remote_dma(dst_ap[0], src[0], T.sem[rsem], T.sem["ls"], pid, rid, topo.mask(core, dst)),
                    300, "ls", len(topo.engines(core, dst)), soft=soft)
        record(None, [], [dst_ap], None, 0, rsem, len(topo.engines(src_core, core)), lat, [me])

    def vector(out, ins, per, call, more=()):
        if len(ins) and len(ins[0]) == 3:
            cost = 50 + CY * GA * cols(out)
        else:
            if all(WIDTH[SCRATCH[a[1][0][0]][2]] == 2 for a in [out] + ins) and per == 1:
                per = 0.5
            cost = CY * max(64, per * cols(out))
        record("v", ins + list(more), [out], call, cost)

    def tt(out, a, b, op):
        per = 1.01 if "psum" in (SCRATCH[a[1][0][0]][0], SCRATCH[b[1][0][0]][0]) else 2
        vector(out, [a, b], per, lambda: g.vector.tensor_tensor(out[0], a[0], b[0], op))

    def ts(out, a, s1, op0, s2=None, op1=None):
        x1, x2 = [s[0] if isinstance(s, tuple) else s for s in (s1, s2)]
        more = [] if op1 is None else [op1]
        vector(out, [a], 1, lambda: g.vector.tensor_scalar(out[0], a[0], x1, x2, op0, *more), [s for s in (s1, s2) if isinstance(s, tuple)])

    def cp(out, a):
        vector(out, [a], 1, lambda: g.vector.tensor_copy(out[0], a[0]))

    def scan(out, a, b, op0, op1):
        vector(out, [a, b], 1, lambda: g.vector.tensor_tensor_scan(out[0], a[0], b[0], 0.0, op0, op1))

    def scatter(win, off, a, b):
        o = ind(win, off)
        record("v", [a, b, off], [win], lambda: g.vector.tensor_tensor(o[0], a[0], b[0], A.max), 50 + CY * SC * cols(a))

    def fill(out, c):
        vector(out, [], 1, lambda: g.vector.memset(out[0], c))

    def act(out, a, func, scale=1.0):
        record("s", [a], [out], lambda: g.scalar.activation(out[0], a[0], func, scale=scale), 65 + CY * cols(out) * (GA if len(a) == 3 else 1))

    def mm(out, l, r, start, stop):
        wide = 4 if SCRATCH[l[1][0][0]][2] == F32 else 1
        record("t", [l, r], [out], lambda: g.tensor.matmul(out[0], l[0], r[0], start, stop), PE * wide * max(min(64, cols(l)), cols(r)))

    def gpsimd(reads, out, call, cost):
        made.append(record("g", reads, [out], call, cost + 2 * CY * cols(out), soft=made[-1:]))

    def iota(out, pattern, base, cm):
        gpsimd([], out, lambda: g.iota(out[0], pattern, base, cm, allow_small_or_imprecise_dtypes=True), 130)

    def asel(out, a, pattern, op, base, cm):
        gpsimd([a], out, lambda: g.affine_select(out[0], a[0], pattern, op, 0.0, base, cm), 170)

    def gcp(out, a):
        record("g", [a], [out], lambda: g.affine_select(out[0], a[0], [[0, cols(out)]], eq, 0.0, 0, 0), 170 + 2 * CY * cols(out))

    def seg(buf, names, a, c, b):
        i = names.index(a)
        j = i if c is None else names.index(c)
        return nd(buf, (0, NB, 1) if b is None else (b, b + 1, 1), (i, j + 1, max(j - i, 1)), (0, NJ, 1))

    def w(a, c=None, b=None):
        return seg("Y4", YSEG, a, c, b) if a in YSEG else seg("W4", WSEG, a, c, b)

    def blk(name, i):
        return ap(name, 15 - i, 143 - i)

    def pb(b, lo, hi, P=None):
        return ap("pb%d" % b, lo, hi, P)

    def ft(name, n):
        return ap(name, 128 * n, 128 * n + 128, NC)

    def ab(r, lo, hi):
        return nd("AB", (0, NB, 1), (6 * NJ * r + NJ * lo, 6 * NJ * r + NJ * hi, 1))

    def ring(d):
        return T.cores[(rank + d) % N]

    load("y", "dj", ap("jcs"), T.jc[:])
    load("s", "ds", ap("sr8"), T.sr[:])
    load("s", "df", ap("fxs"), T.fx[:])
    for h in range(2):
        load("y", "dp%d" % h, ap("pks", 1024 * h, 1024 * h + 1024), T.pk[:, 1024 * h:1024 * h + 1024])
    load("y", "dr", ap("rtb"), T.rt[:])

    kp, kp4096, kp16, par, Zc, Zn = [ap("cols", c, c + 1) for c in range(6)]
    sel = ap("Sel")
    fill(ap("onesb"), 1.0)
    fill(ap("ones32"), 1.0)
    iota(ap("pidx", 0, 1), [[0, 1]], 0, 1)
    asel(sel, ap("onesb", 0, 128, P=8), [[1, 128]], A.is_ge, 0, -16)
    asel(sel, sel, [[-1, 128]], A.is_ge, 15, 16)
    iota(ap("i32"), [[1, 32]], 0, 0)
    iota(ap("tl", 0, 12), [[0, 6], [1, 2]], 0, 0)
    asel(ap("I32"), ap("ones32"), [[-1, 128]], eq, 0, 1)
    iota(w("POS"), [[0, NB], [256, NJ]], 0, 0)
    iota(w("DUM"), [[16, 12]], 4096, 0)
    iota(ap("K3", 0, NC), [[256, NJ], [4097, 16]], 0, 0)
    mm(pb(0, 0, 128), sel, sel, True, True)
    asel(ap("rst"), ap("ones32", 0, 96), [[0, 6], [1, 16]], eq, 0, 0)
    iota(ap("En", 0, 16 * NC), [[0, 16 * NC]], -1, 0)
    asel(ap("En", 0, 16 * NC), ap("En", 0, 16 * NC), [[1, NC], [0, 16]], eq, 0, -1)
    ts(ap("pidx", 1, 2), ap("pidx", 0, 1), 15, A.bitwise_and)
    ts(ap("pidx", 2, 3), ap("pidx", 0, 1), 4, A.arith_shift_right, 1, A.bitwise_and)
    cp(kp, ap("pidx", 1, 2))
    ts(kp4096, ap("pidx", 1, 2), 4096.0, mul)
    ts(kp16, ap("pidx", 1, 2), 16.0, mul, 16.0, add)
    cp(par, ap("pidx", 2, 3))
    fill(ap("Wz32"), 0.0)
    cp(ap("Wz32", (15, 143, 16)), pb(0, (0, 128, 16), None))
    act(ap("BD32"), pb(0, 0, 128), AF.Copy)
    act(ap("Wz"), ap("Wz32"), AF.Copy, 65536.0)
    act(ap("Ib"), ap("I32"), AF.Copy)
    act(ap("I4k"), ap("I32"), AF.Copy, 4096.0)
    act(ap("nI"), ap("I32"), AF.Copy, -1.0)
    for b in range(NB):
        for h in range(2):
            act(ap("GC%d%d" % (b, h), 0, 16), ap("onesb", 0, 16), AF.Copy, 0.0)
    act(ap("rst"), ap("rst"), AF.Copy, 33554432.0)
    iota(nd("AB", (0, NB, 1), (0, 18 * NJ, 1)), [[0, 18 * NJ * NB]], -16, 0)
    ts(w("POS"), w("POS"), kp16, add)
    ts(ap("K3", 0, NC), ap("K3", 0, NC), kp16, add)
    fill(Zc, 0.0)
    ts(w("DUM"), w("DUM"), kp, add)
    iota(ap("pf", 4096, 4288), [[0, 192]], 0, 0)
    iota(ab(0, 3, 4), [[0, 12]], 0, 0)
    iota(ab(1, 3, 4), [[0, 12]], 0, 0)
    ts(ap("tab"), ap("i32"), kp, eq)
    act(ap("nM", 0, 2 * NC), ap("onesb", 0, 2 * NC), AF.Copy, -M)
    iota(ap("fo", 0, 384 * NB), [[0, 384 * NB]], 0, 0)
    n, a, q, u = [ap("r4", 8 * c, 8 * c + 8) for c in range(4)]
    ts(n, ap("i32", 0, 8), 16.0, mul, kp, add)
    ts(a, n, NJ - 1, A.bitwise_and)
    ts(q, n, 6.0 * NJ, A.is_ge, 1.0 * NJ, mul)
    tt(ap("rep"), a, q, add)

    fill(ap("KU", 0, 16), 0.0)
    fill(ap("KU", 208, 224), 0.0)
    act(ap("srb"), ap("sr8"), AF.Copy)
    ts(ap("KU", 16, 208), ap("jcs"), kp4096, add)
    mm(pb(1, 0, 192), sel, ap("srb"), True, True)
    ts(ap("OH"), pb(1, 0, 192), kp, eq)
    tt(ap("Q0"), ap("OH"), ap("KU", 16, 208), mul)
    for i in range(16):
        mm(pb(1, 192, 204), blk("Wz32", i), ap("Q0", (i, 192, 16)), i == 0, i == 15)
    cp(ap("m0"), pb(1, 192, 204))
    ts(seg("KC0", SEG, "c1", None, None), ap("m0"), 4095, A.bitwise_and)
    ts(seg("KC0", SEG, "p1", None, None), ap("m0"), 12, A.arith_shift_right)
    cp(ap("CL0"), seg("KC0", SEG, "c1", None, None))
    for b in range(NB):
        mm(pb(0, 128, 256, NC), ap("fxs", NC * b, NC * b + NC), ap("Ib"), True, True)
        act(ft("fw", 2 * NB + b), pb(0, 128, 256, NC), AF.Copy)
    for o, a in ((ap("TA", 0, 192), ap("KU", 16, 208)), (ap("TA", 192, 416), ap("KU"))):
        vector(o, [a], 1, lambda o=o, a=a: g.vector.transpose(o[0], a[0]))
    ts(ap("tl", 12, 24), ap("tl", 0, 12), par, A.not_equal, 208.0, mul)
    ts(ap("tl", 24, 36), ap("i32", 0, 12), 16.0, mul, kp, add)
    tt(ap("tl", 24, 36), ap("tl", 24, 36), ap("tl", 12, 24), add)
    cp(ap("TL"), ap("tl", 24, 36))
    act(ap("pkg0", 0, 192), ind(ap("TA"), ap("TL")), AF.Copy)
    cp(ap("pkg0", 192, 216), seg("KC0", SEG, "c1", "p1", None))
    for h in range(0, 2048, 512):
        ts(ap("pu", h, h + 512), ap("pks", h, h + 512), 4095, A.bitwise_and)
        ts(ap("pu", 2048 + h, 2560 + h), ap("pks", h, h + 512), 12, A.arith_shift_right)
        act(ap("pf", h, h + 512), ap("pu", h, h + 512), AF.Copy)
        act(ap("pf", 2048 + h, 2560 + h), ap("pu", 2048 + h, 2560 + h), AF.Copy)

    def visit(t):
        KC, KN, last = "KC%d" % (t % 2), "KC%d" % ((t + 1) % 2), t + 1 == VI
        facts = [ft("fw", 2 * NB + b) if t == 0 else ft("fin", NB * (t - 1) + b) for b in range(NB)]

        def k(a, c=None, b=None):
            return seg(KC, SEG, a, c, b)

        def court(s, b):
            return ap("CL0", NJ * b, NJ * b + NJ) if s == 0 else ap("CL%d" % s, 2 * NJ * b, 2 * NJ * b + NJ)

        def keys(s, b):
            gc, D = "GC%d%d" % (b, (t + s) % 2), "D%d" % b
            cp(ap("N16", NC * b, NC * b + NC), ind(ap("pf" if t else "pu"), court(s, b)))
            nv = NC - SG[s][b]
            cut = list(range(0, nv, VC)) + [nv] + [x for x in range(32, NC, 32) if x > nv] + [NC]
            for x0, x1 in zip(cut, cut[1:]):
                o, a = ap(gc, 16 + 16 * x0, 16 + 16 * x1), ind(ap("rtb"), ap("N16", NC * b + x0, NC * b + x1))
                if x0 < nv:
                    cp(o, a)
                elif x0 < x1:
                    act(o, a, AF.Copy)
            for c in range(NJ // 2):
                bank = ap("sub", 512 * turn[0], 512 * turn[0] + 512)
                turn[0] = (turn[0] + 1) % RING
                pair = [(facts[b], ap("En", 512 * c, 512 * c + 512, NC)), (ap("Ib"), ap(gc, 16 + 512 * c, 528 + 512 * c))]
                if c == 0 or s == 1:
                    pair.reverse()
                mm(bank, *pair[0], True, False)
                mm(bank, *pair[1], False, True)
                act(nd(D, (2 * c, 2 * c + 2, 1), (0, 256, 1)), bank, AF.Abs)
            mm(pb(b, 0, NC), ap("I32"), ap("pkg%d" % t, NC * b, NC * b + NC) if s < 2 else ap("K3", 0, NC), True, False)
            for i in range(16):
                mm(pb(b, 0, NC), blk("Wz", i), nd(D, (0, NJ, 1), (16 * i, 16 * i + 16, 1)), False, i == 15)

        def least(s, b):
            o = 192 * s + NC * b
            mi = ap("run", (o + 15, o + NC, 16))
            scan(ap("run", o, o + NC), ap("rst", 0, NC), pb(b, 0, NC), A.max, A.min)
            if s < 2:
                kn, cn, Ln = [k(a % (s + c), None, b) for a, c in (("k%d", 1), ("c%d", 2), ("L%d", 1))]
                L, r = ap("CL%d" % (s + 1), 2 * NJ * b + NJ, 2 * NJ * (b + 1)), ap("RS", o, o + NC)
                ts(cn, mi, 4095, A.bitwise_and)
                ts(kn, mi, 12, A.arith_shift_right, 15, A.bitwise_and)
                cp(court(s + 1, b), cn)
                tt(L, kn, w(("POS", "PO2")[s], None, b), add)
            else:
                L, r, Ln = ap("L3", NJ * b, NJ * b + NJ), ap("R3", NC * b, NC * b + NC), k("Lm", None, b)
                ts(k("L3", None, b), mi, 4095, A.bitwise_and)
                tt(L, k("L3", None, b), ap("O2", NJ * b, NJ * b + NJ), mul)
            if s < 2 or b < NB - 1:
                cp(r, ind(ap("GC%d%d" % (b, (t + s) % 2)), L))
            else:
                act(r, ind(ap("GC%d%d" % (b, (t + s) % 2)), L), AF.Copy)
            if s == 2 and last:
                mm(pb(b, 128, 128 + NC), facts[b], ap("nI", 0, NC, NC), True, False)
                mm(pb(b, 128, 128 + NC), ap("Ib"), r, False, True)
                act(ap("yfs", NC * b, NC * b + NC), pb(b, 128, 128 + NC), AF.Abs)
                return
            mm(pb(b, 128, 256, NC), ap("nI", 0, NC, NC), facts[b], True, False)
            mm(pb(b, 128, 256, NC), r, ap("Ib"), False, True)
            facts[b] = ft("fw", NB * s + b) if s < 2 else ft("fo", NB * t + b)
            act(facts[b], pb(b, 128, 256, NC), AF.Abs)
            if s == 2:
                n = NB * t + b
                send(ring(1), ring(-1), ap("fin", 128 * n, 128 * n + 128), ap("fo", 128 * n, 128 * n + 128), "fa%d" % n)

        def book1():
            tt(w("o1"), k("k1"), k("p1"), A.not_equal)
            tt(w("PO2"), w("POS"), w("o1"), mul)
            tt(w("dm"), k("k1"), k("p1"), eq)
            tt(w("dm"), w("dm"), w("DUM"), mul)
            if t:
                count()
            for i in range(16):
                mm(pb(NB - 1, 448, 460), blk("Wz", i), ap("RS", (i, 192, 16)), i == 0, i == 15)
            ts(w("z1"), pb(NB - 1, 448, 460), 2.0 ** -16, mul, Zc, add)
            ts(ap("d1"), ap("run", (15, 192, 16)), 16, A.arith_shift_right)
            ts(ap("d1"), ap("d1"), Zc, add)
            if not last:
                gcp(seg(KN, SEG, "c1", "p1", None), ap("pkg%d" % (t + 1), 192, 216))
                cp(ap("CL0"), seg(KN, SEG, "c1", None, None))

        def book2():
            X1, X2, X3a, X3b = k("c1", "k1"), k("c2", "k2"), k("c3", "p1"), k("c3", "k1")
            ts(ap("d2"), ap("run", (207, 384, 16)), 16, A.arith_shift_right)
            tt(w("z2"), ap("d1"), ap("d2"), add)
            tt(w("ne"), k("k2"), k("k1"), A.not_equal)
            tt(w("T"), k("k2"), k("p1"), eq)
            gcp(w("Tb"), w("T"))
            tt(w("oa"), w("o1"), w("ne"), mul)
            tt(w("da", "db"), X3a, X1, sub)
            tt(ap("O2"), w("oa"), w("T"), A.is_gt)
            ts(w("y1", "y2"), w("z1", "z2"), 1, A.bitwise_and)
            gcp(w("y1b", "y2b"), w("y1", "y2"))
            tt(w("ea", "eb"), X2, X1, sub)
            tt(w("PO3"), w("POS"), ap("O2"), mul)
            for a, c in (("P1", "p1"), ("P2", "k1"), ("P3", "k2")):
                tt(w(a), k(c), w("PO3"), add)
            tt(w("fa", "fb"), X3b, X2, sub)
            tt(ab(0, 0, 2), w("y1", "y1b"), w("da", "db"), mul)
            tt(w("ga", "gb"), w("y1", "y1b"), w("ea", "eb"), mul)
            tt(w("ha", "hb"), w("y2", "y2b"), w("fa", "fb"), mul)
            ts(w("qa", "qb"), w("T", "Tb"), -16.0, mul, 16.0, add)
            tt(ab(0, 2, 3), w("da"), ab(0, 0, 1), sub)
            tt(w("oa"), w("db"), ab(0, 1, 2), sub)
            tt(w("ma", "mb"), w("ga", "gb"), w("T", "Tb"), mul)
            tt(ab(1, 0, 2), w("ha", "hb"), w("ea", "eb"), add)
            tt(ab(2, 4, 6), k("k1", "k2"), w("qa", "qb"), add)
            ts(ab(0, 4, 5), w("oa"), -16.0, add)
            tt(ab(2, 0, 2), X1, w("ma", "mb"), add)
            gcp(ab(1, 2, 3), w("da"))
            tt(ab(2, 2, 3), k("c1"), w("dm"), A.max)
            gcp(ab(2, 3, 4), k("c2"))

        def close(b):
            def sl(lo, hi):
                return ap("SL", 36 * b + NJ * lo, 36 * b + NJ * hi)
            e, h, o, u, q = 32 * b, 112 * b, 2 * NC * b, 6 * NJ, ap("Q", NC * b, NC * b + NC)
            tt(ap("E", e, e + NJ), k("L3", None, b), w("P1", None, b), eq)
            tt(ap("E", e + NJ, e + 2 * NJ), k("L3", None, b), w("P2", None, b), eq)
            tt(ap("H", h, h + 16 * RK), ind(ap("E", e, e + 2 * NJ), ap("rep", 0, RK)), nd("AB", (b, b + 1, 1), (0, 16 * RK, 1)), mul)
            if not last and b == NB - 1:
                tt(ap("E3"), k("L3"), w("P3"), eq)
            tt(ap("S", h, h + u), ap("H", h, h + u), nd("AB", (b, b + 1, 1), (2 * u, 3 * u, 1)), add)
            tt(sl(0, 6), ap("S", h, h + u), ap("H", h + u, h + 2 * u), add)
            act(ap("EQD", NC * b, NC * b + NC), ind(ap("tab"), sl(1, 2)), AF.Copy)
            act(ap("EQ", o, o + 2 * NC), ind(ap("tab"), sl(4, 6)), AF.Copy, M)
            tt(q, ind(ap("pf"), sl(0, 1)), ap("EQD", NC * b, NC * b + NC), mul)
            both = pb(b, 256, 256 + 2 * NC)
            mm(both, ap("Ib"), ap("nM", 0, 2 * NC), True, False)
            mm(pb(b, 256, 256 + NC), ap("BD32"), q, False, False)
            mm(pb(b, 256 + NC, 256 + 2 * NC), ap("BD32"), q, False, False)
            mm(both, ap("Ib"), ap("EQ", o, o + 2 * NC), False, True)
            tt(ap("Bv", o, o + 2 * NC), ind(ap("pf"), sl(2, 4)), ap("EQ", o, o + 2 * NC), sub)
            act(ap("PS", o, o + 2 * NC), both, AF.Copy)

        def change(b):
            o = 2 * NC * b
            scatter(ap("pf"), ap("SL", 36 * b + 2 * NJ, 36 * b + 4 * NJ), ap("Bv", o, o + 2 * NC), ap("PS", o, o + 2 * NC))

        def count():
            z = pb(NB - 1, 472, 484)
            mm(z, ap("onesb", 0, 128), ap("O2"), True, False)
            for b in range(NB):
                mm(pb(NB - 1, 472, 472 + 2 * NJ), ap("onesb", 0, 128), ap("E", 32 * b, 32 * b + 2 * NJ), False, False)
            mm(z, ap("onesb", 0, 128), ap("E3"), False, True)
            vector(Zn, [z], 1, lambda: g.vector.tensor_reduce(Zn[0], z[0], X, add))
            tt(Zc, Zc, Zn, add)

        if not last:
            send(ring(t + 1), ring(-t - 1), ap("pkg%d" % (t + 1)), ap("pkg0"), "pk%d" % (t + 1), PL, [len(ops) - 1] if t else [])
        for s in range(3):
            for b in range(NB):
                if s:
                    least(s - 1, b)
                if (s, b) == (1, NB - 1):
                    book1()
                if (s, b) == (2, NB - 1):
                    book2()
                keys(s, b)
        for b in range(NB):
            least(2, b)
            close(b)
            if b:
                change(b - 1)
        change(NB - 1)

    for t in range(VI):
        visit(t)
    dma("y", "dyf", T.yf[:], ap("yfs")[0], [ap("yfs")], [])

    for n in range(len(OUT) - 1):
        for lo in range(OUT[n], OUT[n + 1], 256):
            hi, o = lo + 256, 512 * turn[0]
            turn[0] = (turn[0] + 1) % RING
            if lo % 768 == 256:
                mm(ap("sub", o, o + 256), ap("I4k"), ap("pf", 2048 + lo, 2048 + hi), True, True)
            else:
                act(ap("sub", o, o + 256), ap("pf", 2048 + lo, 2048 + hi), AF.Copy, 4096.0)
            tt(ap("yps", lo, hi), ap("pf", lo, hi), ap("sub", o, o + hi - lo), add)
        piece = ap("yps", OUT[n], OUT[n + 1])
        dma("y", "dy%d" % n, T.yp[:, OUT[n]:OUT[n + 1]], piece[0], [piece], [])
    issue(g, T, ops)
